import numpy as np, ml_dtypes
CORES = [13,21,141,149]
N = 4
BF = ml_dtypes.bfloat16
S, CAP, WC, NB, RO, OC, SHO = 160, 64, 4096, 64, 3, 2, 6
MU = (47, 229, 101, 331)
FC, L = 16 * NB, N * CAP
KB = (np.arange(16)[:, None] >> np.arange(4)) & 1
def cells(x):
    p = [(x[..., e, :, None] >> 2) + KB[:, e] for e in range(4)]
    w = [np.where(KB[:, e] == 1, x[..., e, :, None] & 3, 4 - (x[..., e, :, None] & 3)) for e in range(4)]
    i = (((p[0] * (2 * p[1] + 1)) >> 2) + MU[0] * p[2] + MU[1] * p[3]) & (WC - 1)
    b = (((p[2] * (2 * p[3] + 1)) >> 2) + MU[2] * p[0] + MU[3] * p[1]) & (NB - 1)
    return i, b, w[0] * w[1] * w[2] * w[3]
def parts(rng):
    cf = rng.integers(0, 237, (N, 8, 1, WC)) + rng.integers(0, 4, (N, 8, 16, WC))
    ft = rng.integers(0, 256, (N, 8, 16, FC)); ft[:, ::2, :4] = 96 + (ft[:, ::2, :4] >> 2)
    tg = rng.integers(0, 256, (N, 8, 16, S)); x = rng.integers(0, 256, (N, 8, 4, S))
    fav = rng.integers(0, N, (N, 8, 1)); hit = rng.random((N, 8, S)) < rng.choice(np.array([0.0, 0.1, 0.3, 0.5]), (N, 8, 1))
    x[:, :, OC] = np.where(hit, (fav << SHO) + (x[:, :, OC] & ((1 << SHO) - 1)), x[:, :, OC])
    return cf, ft, tg, x
def pack(cf, ft, tg, x):
    b = lambda v, n: np.ascontiguousarray(v.reshape(N, 128, n)).astype(np.float32).astype(BF)
    return {"cf": b(cf, WC), "ft": b(ft, FC), "tg": b(tg, S), "x0": np.ascontiguousarray(x.reshape(N, 32, S)).astype(np.int32)}
def setup_inputs(rng):
    return pack(*parts(rng))
def setup_inputs_spread(rng):
    cf, ft, tg, x = parts(rng)
    cf = np.where(rng.random((N, 8, 1, WC)) < 0.5, rng.integers(0, 241, cf.shape), (241 * rng.random(cf.shape) ** 4).astype(np.int64))
    v = np.minimum(np.exp2(8 * rng.random(ft.shape)).astype(np.int64) - 1, 255); ft = np.where(rng.random((N, 8, 1, FC)) < 0.5, v, 255 - v)
    v = np.minimum(np.exp2(8 * rng.random(tg.shape)).astype(np.int64) - 1, 255); tg = np.where(rng.random((N, 8, 1, S)) < 0.5, v, 255 - v)
    v = np.minimum((256 * rng.random(x.shape) ** 2).astype(np.int64), 255); x = np.where(rng.random((N, 8, 4, 1)) < 0.5, v, 255 - v)
    return pack(cf, ft, tg, x)
def setup_inputs_ends(rng):
    e = lambda top, *shape: top * rng.integers(0, 2, shape)
    cf = e(240, N, 8, 16, WC); kind = rng.integers(0, 4, (N, 8, 1, NB, 1)); fv = e(255, N, 8, 16, NB, 16)
    fv = np.ascontiguousarray(np.where(kind == 0, 0, np.where(kind == 1, 255, fv)))
    rec = rng.integers(0, 3, (N, 8, 1, S)); tg = np.where(rec == 0, 0, np.where(rec == 1, 255, e(255, N, 8, 16, S)))
    x = e(255, N, 8, 4, S); x[:, :, OC] = np.where(rng.random((N, 8, S)) < 0.2, rng.integers(0, 256, (N, 8, S)), x[:, :, OC])
    z = np.zeros((4, 1), np.int64); z[OC] = 255; zi, zb, zw = cells(z); live = zw[0] > 0; zi = zi[0][live]; zb = zb[0][live]
    tb = cells(np.full((4, 1), 255))[1][0]; r = N - 1
    for g in range(8):
        for turn in ((0, 1) if g % 2 else (1, 0)):
            if turn == 0: cf[r, g][:, zi] = 0; cf[r, g][15, zi] = 240; fv[r, g][:, zb] = 255; fv[r, g][:, zb, 15] = 0
            else: fv[r, g][:, tb] = 255
    x[0, :, :, 0] = z[:, 0]; tg[0, :, :, 0] = 255; x[0, :, :, 1] = 255; tg[0, :, :, 1] = 0
    x[r, 7, OC, rng.permutation(S)[:CAP + 4]] = 255
    h = int(np.flatnonzero((x[r, 7, OC] >> SHO) == r)[CAP - 1]); x[r, 7, :, h] = 255; tg[r, 7, :, h] = 0
    return pack(cf, fv, tg, x)
def setup_inputs_corners(rng):
    cf, ft, tg, x = parts(rng)
    mode = rng.integers(0, 4, (N, 8, 1, S)); low = np.where(mode == 0, 0, np.where(mode == 1, 2, np.where(mode == 2, 3, x & 3)))
    hi = np.where(rng.random(x.shape) < 0.3, 252 * rng.integers(0, 2, x.shape), x - (x & 3)); x = hi + low
    own = np.zeros((N, 8, S), np.int64)
    for q in range(N):
        for g in range(8):
            o = int(rng.integers(0, N)); n = int(rng.choice(np.array([0, 1, CAP - 1, CAP, CAP + 1, S])))
            if q == 0: o = 1 + g % (N - 1); n = (CAP, CAP + 1, S, CAP - 1, 1, 0, CAP, CAP + 1)[g]
            own[q, g] = rng.permutation(np.concatenate([np.full(n, o), (o + rng.integers(1, N, S - n)) % N]))
    x[:, :, OC] = (own << SHO) + (hi[:, :, OC] & ((1 << SHO) - 1)) + low[:, :, OC]
    few = np.array([0, 1, 254, 255]); v = rng.choice(np.array([119, 120, 121, 127, 128, 129, 135, 136, 137]), (8, 16))
    v[5, 4:] = rng.choice(np.array([0, 1, 100, 254, 255]), 12)
    for g in (1, 3, 5, 7):
        ft[:, g, :4] = v[g, :4, None]; ft[:, g, 4:] = v[5, 4:, None] if g == 5 else rng.choice(few, (N, 12, FC))
        tg[:, g, :4] = v[g, :4, None] + rng.integers(-1, 2, (N, 4, S)); tg[:, g, 4:] = rng.choice(few, (N, 12, S))
    tg[:, 5] = np.where(rng.random((N, 1, S)) < 0.25, v[5][:, None], tg[:, 5])
    for o in range(N):
        two = np.flatnonzero(own[0, 5] == o)[:2]
        if len(two) == 2: x[0, 5, :, two[1]] = x[0, 5, :, two[0]]; tg[0, 5, :, two[0]] = v[5]; tg[0, 5, :, two[1]] = 255
    return pack(cf, ft, tg, x)
def setup_inputs_crowd(rng):
    cf, ft, tg, x = parts(rng); turn = int(rng.integers(0, N)); e = (OC + 1) % 4
    for g in range(8):
        o = (g + turn) % N
        for again in range(64):
            pt = 4 * rng.integers(0, 64, 4); pt[OC] = (o << SHO) + 4 * rng.integers(0, 1 << (SHO - 2))
            two = np.stack([pt, pt], axis=1); two[e, 1] = (two[e, 1] + 64) & 255; zi, zb, zw = cells(two)
            if zi[0, 0] != zi[1, 0] and zb[0, 0] != zb[1, 0]: break
        v = pt[None, :, None] + rng.integers(0, 3, (N, 4, S))
        if g == 1: v[N - 1, e, CAP - 1] = (v[N - 1, e, CAP - 1] + 64) & 255
        if g == 5: v[0, e, 0] = (v[0, e, 0] + 64) & 255
        if g % 4 == 2: v[:, e] = (v[:, e] + 64 * rng.integers(0, 3, (N, S))) & 255
        if g % 4 == 3: v[:, :, 1::2] = x[:, g, :, 1::2]
        x[:, g] = v
    return pack(cf, ft, tg, x)
def setup_inputs_calm(rng):
    cf, ft, tg, x = parts(rng)
    cf = 235 * rng.integers(0, 2, (N, 8, 1, WC)) + rng.integers(0, 6, (N, 8, 16, WC))
    step = 128 + (np.arange(8)[:, None] & 3) * (1 - 2 * rng.integers(0, 2, (8, 4)))
    ft[:, :, :4] = step[None, :, :, None]; tg[:, :, :4] = step[None, :, :, None]
    ft[:, 1::2, 4:] = rng.choice(np.array([0, 1, 2, 3, 252, 253, 254, 255]), (N, 4, 12, FC))
    tg[:, :, 4:] = 255 * rng.integers(0, 2, (N, 8, 12, S))
    for g in (0, 4):
        low = rng.integers(0, 2 if g == 0 else 1, (N, 16, WC)); low[:, 0] = 0
        cf[:, g] = np.where(rng.random((N, 1, WC)) < 0.5, low, cf[:, g]); tg[:, g, 4:] = np.where(rng.random((N, 1, S)) < 0.5, 0, tg[:, g, 4:])
        if g == 0: x[0, g, :, 0] = x[0, g, :, 0] - (x[0, g, :, 0] & 3)
        i, b, w = cells(x[0, g, :, :1]); tg[0, g, 4:, 0] = 0
        cf[int(x[0, g, OC, 0]) >> SHO, g, :, int(i[0, np.argmax(w[0])])] = 0 if g == 4 else (np.arange(16) >= int(rng.integers(1, 16))).astype(np.int64)
    for q, g in ((0, 3), (N - 1, 6)):
        o = (q + 1 + int(rng.integers(0, N - 1))) % N; r = (x[q, g, OC] - (o << SHO)) & 255
        r = np.where((r < (1 << SHO) + 12) | (r >= 244), (r + 128) & 255, r)
        s = rng.permutation(S)[:8]; r[s] = (1 << SHO) - 1 if step[g, OC] > 128 else 0
        x[q, g, OC] = ((o << SHO) + r) & 255; tg[q, g, 4:, s] = 255
    return pack(cf, ft, tg, x)
def check_inputs(d):
    bad = []
    for k, top in (("cf", 240), ("ft", 255), ("tg", 255), ("x0", 255)):
        v = np.asarray(d[k]).astype(np.float64)
        if not (np.min(v) >= 0 and np.max(v) <= top): bad.append("range of " + k)
        if np.any(v != np.floor(v)): bad.append("whole numbers of " + k)
    return bad
def firsts(lanes, key):
    return lanes[np.unique(key[lanes], return_index=True)[1]]
def reference(cf, ft, tg, x0):
    C = cf.astype(np.float32).astype(np.int64).reshape(N, 8, 16, WC); F = ft.astype(np.float32).astype(np.int64).reshape(N, 8, 16, FC)
    t = tg.astype(np.float32).astype(np.int64).reshape(N, 8, 16, S); x = x0.astype(np.int64).reshape(N, 8, 4, S); ys = np.zeros((N, 8, 16, S), np.int64)
    for rnd in range(RO):
        own = x[:, :, OC] >> SHO
        h = (own[:, :, None, :] == np.arange(N)[:, None]).astype(np.int64)
        place = np.take_along_axis(np.add.accumulate(h, axis=3) - h, own[:, :, None, :], 2)[:, :, 0]
        q, g, s = np.nonzero(place < CAP); o = own[q, g, s]; l = CAP * q + place[q, g, s]
        X = np.zeros((N, 8, 4, L), np.int64); T = np.zeros((N, 8, 16, L), np.int64); live = np.zeros((N, 8, L), bool)
        X[o, g, :, l] = x[q, g, :, s]; T[o, g, :, l] = t[q, g, :, s]; live[o, g, l] = True
        i, b, w = cells(X)
        m = np.argmax(np.take_along_axis(C, i.reshape(N, 8, 1, L * 16), 3), axis=2).reshape(N, 8, L, 16)
        v = np.take_along_axis(F, (16 * b + m).reshape(N, 8, 1, L * 16), 3).reshape(N, 8, 16, L, 16)
        y = np.sum(v * w[:, :, None], axis=4) >> 8
        sg = np.sign(T - y)
        k = np.argmax(w, axis=3)[..., None]
        ci, cb, cm = [np.take_along_axis(z, k, 3)[..., 0] for z in (i, b, m)]; fc = 16 * cb + cm
        u = np.take_along_axis(F, (16 * cb[..., None] + np.arange(16)).reshape(N, 8, 1, L * 16), 3).reshape(N, 8, 16, L, 16)
        up = np.sign(np.sum(sg[..., None] * u, axis=2))
        for r in range(N):
            for a in range(8):
                lanes = np.flatnonzero(live[r, a])
                win = firsts(lanes, ci[r, a]); C[r, a][:, ci[r, a, win]] += up[r, a, win].T
                win = firsts(lanes, fc[r, a]); at = fc[r, a, win]; F[r, a][:, at] = np.clip(F[r, a][:, at] + sg[r, a][:, win], 0, 255)
        back = y[o, g, :, l]
        ys[q, g, :, s] += back
        x[q, g, :, s] = (x[q, g, :, s] + np.clip(back[:, :4] - 128, -8, 8)) & 255
    yc = np.sum(C * (np.arange(16) + 1)[:, None], axis=2)
    return {"yc": yc.astype(np.float32), "yf": F.reshape(N, 128, FC).astype(np.float32).astype(BF), "ys": ys.reshape(N, 128, S).astype(np.float32), "yx": x.reshape(N, 32, S).astype(np.float32)}

@@ -1,0 +1,830 @@
+import math
+from concourse.bass import DstId, RemoteDMATransfer
+from concourse.mybir import AluOpType as Op, ActivationFunctionType as AF
+
+S, CAP, WC, FC, RO, NR = 160, 64, 4096, 1024, 3, 4
+SHIFTS = (0, 47, 229, 276)
+PAD = 288
+DC, DF = 4400, 1024
+WT = DC + 32
+MAGIC = 12582912.0
+LN4 = math.log(4.0)
+VL = 64
+PACK = True
+VM = False
+VJ = 2
+CY, WAKE, SLACK, HOP = 1.04e-3, 0.06, 0.02, 5.0
+PASSES, BLEND, SEED, SPAN, PRIO = 0, 60, 1, [0.0], {}
+
+sb = lambda shape, d: ("sbuf", shape, d)
+ps = lambda shape: ("psum", shape, "float32")
+B, F, I, U, H = "bfloat16", "float32", "int32", "uint16", "float16"
+SCRATCH = {
+    "mt": sb([128, PAD + WT], B), "ctab": sb([128, WT], B), "ftab": sb([128, FC + 32], B),
+    "ta": sb([128, NR * S], B), "xw": sb([128, RO * NR * S], B), "xl": sb([128, RO * 8, 32], B),
+    "yr": sb([128, RO * NR * S], B), "yb": sb([128, RO * 256], B), "rb": sb([128, S + 2 * RO * CAP], B),
+    "iot": sb([128, WT], F), "io_": sb([128, S], F), "pint": sb([128, 8], I), "g16": sb([128, 128], B),
+    "r4": sb([128, 128], B), "cc": sb([128, 32], F), "pa": sb([128, 16], F), "eye": sb([128, 10, 16], F),
+    "gm": sb([128, 8], F), "one": sb([128, S], B), "tri": sb([128, 16], F),
+    "ka": sb([128, 3, 16], B), "kg": sb([128, 10, 16], B), "ea": sb([128, 6, 160], B), "eg": sb([128, 10, 128], B),
+    "ed": sb([128, 20, 128], B), "et": sb([128, 16, 128], B), "zz": sb([128, 4, 144], B), "z16": sb([128, 144], H),
+    "i16": sb([128, 128], H), "i32": sb([128, 128], F),
+    "dmp": sb([128, 32], F), "jj": sb([128, 256], F), "lx": sb([128, 16], U), "ld": sb([128, 24], U),
+    "x0i": sb([128, S], I), "xp": sb([128, (RO + 1) * S], B), "xq": sb([128, S], B), "clp": sb([128, S], B),
+    "xa": sb([128, S], I), "xi": sb([128, S], I), "oh": sb([128, S], I), "hh": sb([128, S], H), "cum": sb([128, S], H),
+    "prd": sb([128, S], H), "wt": sb([128, S], B), "sl": sb([128, RO * 16], U), "acc": sb([128, RO * S], F),
+    "xf": sb([128, S], F),
+    "mx": sb([128, 512], F), "ki": sb([128, 256], I), "k2": sb([128, 512], I), "mq": sb([128, 512], B),
+    "va": sb([128, 768], F), "ra": sb([128, 256], F), "tsw": sb([128, 256], I), "tw": sb([128, 16, 16], I),
+    "ti": sb([128, 16, 5], I), "of1": sb([128, 64], U), "rbb": sb([128, 256], F), "tb": sb([128, 256], I),
+    "tb2": sb([128, 256], I), "b16": sb([128, 256], B), "wq": sb([128, 256], B), "wcd": sb([128, 4, 256], B),
+    "mg": sb([128, 1024], B), "ms": sb([128, 256], B), "of2": sb([128, 256], U),
+    "vv": sb([128, 4096], B), "pp": sb([128, 4096], H), "qq": sb([128, 1024], F),
+    "tmp": sb([128, 112], F), "kw": sb([128, RO * 32], F), "lk": sb([128, RO * 48], U), "bw": sb([128, 16], I),
+    "ofu": sb([128, 256], F), "ou": sb([128, 256], U), "sid": sb([128, 16], U), "tgl": sb([128, 256], B),
+    "kr": sb([128, 768], F), "eq": sb([128, 768], B), "lo": sb([128, RO * 32], U),
+    "v2": sb([128, 4096], B), "gv": sb([128, 4096], B), "gs": sb([128, 256], B), "uu": sb([128, RO * 256], B),
+    "f2": sb([128, 512], F), "v3": sb([128, 2048], F), "gw": sb([128, 2048], F), "bw8": sb([128, 16], I),
+    "hi": sb([128, 256], H), "zc": sb([128, 256], F), "z2": sb([128, 144], F), "d16": sb([128, 128], H),
+    "cg": sb([128, RO * 256], B), "fg": sb([128, 256], B), "fn": sb([128, 256], B), "ee": sb([128, 256], B),
+    "ohm": sb([128, 256], B), "mn": sb([128, 256], B), "yo": sb([128, 256], F),
+    "pA": ps([128, 16, 32]), "pB": ps([128, 16, 32]), "pC": ps([128, 512]), "pD": ps([128, 512]),
+    "pE": ps([128, 512]), "pF": ps([128, 512]), "pG": ps([128, 512]), "pH": ps([128, 512]),
+}
+MSGS = ["tg"] + [k + str(r) for r in range(RO) for k in "xy"]
+SEMAPHORES = (["cV", "cS", "cP", "cG", "sent"] + ["a" + m for m in MSGS] + ["h" + m for m in MSGS]
+              + ["d%d" % i for i in range(40)])
+
+
+def relays(T, topo):
+    out = {}
+    for q, src in enumerate(T.cores):
+        used = []
+        for o, dst in enumerate(T.cores):
+            if o != q and not topo.may_write(src, dst):
+                c = [k for k in topo.cores_of(src) if k not in T.cores and k not in used and topo.may_write(k, dst)]
+                c.sort(key=lambda k: topo.die(k) != topo.die(src))
+                out[(q, o)] = c[0]
+                used.append(c[0])
+    return out
+
+
+def bits(es):
+    return sum(1 << e for e in es)
+
+
+def landing(T, m, q):
+    if m == "tg":
+        return T.ta[:, S * q:S * q + S]
+    r = int(m[1])
+    if m[0] == "x":
+        return T.xl[:, 8 * r + 2 * q:8 * r + 2 * q + 2, :]
+    return T.yr[:, NR * S * r + S * q:NR * S * r + S * q + CAP]
+
+
+def slot(T, m):
+    i = MSGS.index(m)
+    return T.rb[:, 0:S] if i == 0 else T.rb[:, S + CAP * (i - 1):S + CAP * i]
+
+
+def relay_program(g, core, T, topo, q, o):
+    src, dst = T.cores[q], T.cores[o]
+    n = len(topo.engines(core, dst))
+    rid, pid = topo.addr(dst, core)
+    for m in MSGS:
+        g.wait_ge(T.sem["h" + m], n)
+        g.remote_dma(landing(T, m, q), slot(T, m), T.sem["a" + m], T.sem.sent, pid, rid, topo.mask(core, dst))
+    g.wait_ge(T.sem.sent, n * len(MSGS))
+
+
+def rank_program(g, core, T, topo):
+    rel = relays(T, topo)
+    rank = T.rank_of(core)
+    if rank is None:
+        for (q, o), c in rel.items():
+            if c == core:
+                relay_program(g, core, T, topo, q, o)
+        return
+    ops = []
+    build(g, core, rank, T, topo, rel, ops)
+    emit(g, T, ops)
+
+
+def emit(g, T, ops):
+    Q = {"V": g.vector, "S": g.scalar, "P": g.tensor, "G": g, "Y": g.sync}
+    hist, group, index = {}, {}, {}
+    for n, o in enumerate(ops):
+        index[o["key"]] = n
+        if o["sem"] is not None:
+            group.setdefault(o["sem"], []).append(n)
+    for n, o in enumerate(ops):
+        e, dep, order = o["e"], set(), set(index[k] for k in o["after"])
+        for regs, wr in ((o["r"], False), (o["w"], True)):
+            for (nm, lo, hi, tag) in regs:
+                psum = SCRATCH[nm][0] == "psum"
+                for (l2, h2, t2, k, w2) in hist.get(nm, []):
+                    p = ops[k]
+                    hit = l2 < hi and lo < h2 and (tag is None or t2 is None or tag == t2) and (wr or w2)
+                    if p["e"] == e and p["sem"] is None and o["sem"] is None:
+                        if e == "P":
+                            if psum:
+                                order.add(k)
+                        elif hit:
+                            dep.add(k)
+                    elif p["sem"] is not None and p["sem"] == o["sem"]:
+                        pass
+                    elif psum or hit:
+                        dep.update([k] if p["sem"] is None else group[p["sem"]])
+        o["dep"], o["ord"] = (set() if e == "X" else dep), order
+        if o["sem"] == "sent":
+            continue
+        for regs, wr in ((o["r"], False), (o["w"], True)):
+            for (nm, lo, hi, tag) in regs:
+                psum, seen = SCRATCH[nm][0] == "psum", o["dep"] | o["ord"]
+                keep = [z for z in hist.get(nm, []) if not (z[3] in seen and ops[z[3]]["sem"] is None and o["sem"] is None and (
+                    (wr and tag is None and lo <= z[0] and z[1] <= hi and not psum) or (psum and e == "P" and ops[z[3]]["e"] == "P")))]
+                if psum and keep and ops[keep[-1][3]]["e"] != e:
+                    keep = [z for z in keep if ops[z[3]]["e"] == ops[keep[-1][3]]["e"]]
+                hist[nm] = keep + [(lo, hi, tag, n, wr)]
+    succ = [[] for o in ops]
+    for n, o in enumerate(ops):
+        for k in o["dep"] | o["ord"]:
+            succ[k].append(n)
+    left = [len(o["dep"] | o["ord"]) for o in ops]
+    topo_order, stack, cnt0 = [], [n for n in range(len(ops)) if left[n] == 0], list(left)
+    while stack:
+        n = stack.pop()
+        topo_order.append(n)
+        for k in succ[n]:
+            cnt0[k] -= 1
+            if cnt0[k] == 0:
+                stack.append(k)
+    tail = [0.0] * len(ops)
+    for n in reversed(topo_order):
+        tail[n] = ops[n]["t"] + ops[n]["lat"] + ops[n]["mb"] * 5.0 + WAKE + max([tail[k] for k in succ[n]] + [0.0])
+    pred = [list(o["dep"] | o["ord"]) for o in ops]
+
+    def plan(prio, back):
+        nxt, prv = (pred, succ) if back else (succ, pred)
+        todo = [len(p) for p in prv]
+        at = [(ops[n]["lat"] + ops[n]["mb"] * 5.0 if back else 0.0) for n in range(len(ops))]
+        rdy = {}
+        for n in range(len(ops)):
+            if todo[n] == 0:
+                rdy.setdefault(ops[n]["e"], {})[n] = at[n]
+        free, seq, ends, pipe, span = {}, [], [0.0] * len(ops), 0.0, 0.0
+        while any(rdy.values()):
+            t0, e = min((max(min(d.values()), free.get(q, 0.0)), q) for q, d in rdy.items() if d)
+            n = max((k for k, t in rdy[e].items() if t <= t0 + SLACK), key=lambda k: (prio[k], -k))
+            o = ops[n]
+            end = max(rdy[e].pop(n), t0) + o["t"]
+            if e != "X":
+                free[e] = end
+            fin = end + o["lat"]
+            if o["mb"] and not back:
+                pipe = max(pipe, fin) + o["mb"] * 5.0
+                fin = pipe
+            seq.append(n)
+            ends[n] = end
+            span = max(span, end if back else fin)
+            for k in nxt[n]:
+                if back:
+                    t = end + (ops[k]["lat"] + ops[k]["mb"] * 5.0 + WAKE if k in o["dep"] else 0.0)
+                else:
+                    t = fin + WAKE if n in ops[k]["dep"] else end
+                at[k] = max(at[k], t)
+                todo[k] -= 1
+                if todo[k] == 0:
+                    rdy.setdefault(ops[k]["e"], {})[k] = at[k]
+        return span, seq, ends
+
+    if len(ops) not in PRIO:
+        name = [((o["w"] or o["r"] or [("",)])[0][0], n // 60) for n, o in enumerate(ops)]
+        kinds = sorted(set(name))
+        prio, seed, best = tail, SEED, (1e9, tail)
+        for it in range(BLEND):
+            s, sq, en = plan(prio, False)
+            if s < best[0]:
+                best = (s, prio)
+            b = plan(en, True)[2]
+            prio = [0.7 * x + 0.3 * y for x, y in zip(prio, b)]
+        span, prio = best
+        for it in range(PASSES):
+            bump = {}
+            for k in kinds:
+                seed = (seed * 1103515245 + 12345) % 2147483648
+                if (seed >> 8) % 1000 < 25:
+                    bump[k] = ((seed >> 18) % 1000 - 500) / 100.0
+            cand = [p + bump.get(k, 0.0) for p, k in zip(prio, name)]
+            s = plan(cand, False)[0]
+            if s <= span + 0.4 * (1.0 - it / PASSES):
+                prio, span = cand, s
+                if s < best[0]:
+                    best = (s, cand)
+        PRIO[len(ops)] = best[1]
+    SPAN[0], seq, ends = plan(PRIO[len(ops)], False)
+    SPAN[1:] = [ops, seq, ends, tail]
+    pos = {n: i for i, n in enumerate(seq)}
+    known = {e: {} for e in Q}
+    for n in seq:
+        o, need = ops[n], {}
+        for k in o["dep"]:
+            key = ops[k]["sem"] or ops[k]["e"]
+            need[key] = max(need.get(key, -1), pos[k])
+        o["wait"], o["kn"] = [], {}
+        if o["e"] != "X":
+            kn = known[o["e"]]
+            for key, k in sorted(need.items(), key=lambda z: -z[1]):
+                if kn.get(key, -1) < k:
+                    p = ops[seq[k]]
+                    o["wait"].append(k)
+                    p["sig"] = True
+                    kn[key] = k
+                    for a, b in p["kn"].items():
+                        kn[a] = max(kn.get(a, -1), b)
+            o["kn"] = dict(kn)
+    ops = [ops[n] for n in seq]
+    cnt = {}
+    for o in ops:
+        key = o["sem"] or "c" + o["e"]
+        if o["sem"] is not None:
+            cnt[key] = cnt.get(key, 0) + o["inc"]
+        elif o.get("sig"):
+            cnt[key] = cnt.get(key, 0) + 1
+        o["cnt"] = (key, cnt.get(key, 0))
+    done = {}
+    for o in ops:
+        if o["e"] == "X":
+            continue
+        for k in o["wait"]:
+            key, c = ops[k]["cnt"]
+            Q[o["e"]].wait_ge(T.sem[key], c)
+            done[key] = max(done.get(key, 0), c)
+        ins = o["fn"]()
+        if o["sem"] is not None and o["sem"] != "sent":
+            ins.then_inc(T.sem[o["sem"]], 16)
+        elif o["sem"] is None and o.get("sig"):
+            ins.then_inc(T.sem["c" + o["e"]], 1)
+    for key, c in cnt.items():
+        if done.get(key, 0) < c:
+            g.wait_ge(T.sem[key], c)
+
+
+def build(g, core, rank, T, topo, rel, ops):
+    V, SC, PE = g.vector, g.scalar, g.tensor
+
+    def a(nm, *ix, part=slice(None), tag=None):
+        shape = SCRATCH[nm][1][1:]
+        ix = list(ix) + [slice(None)] * (len(shape) - len(ix))
+        lo, hi, n = 0, 0, 1
+        for d, k in zip(shape, ix):
+            rg = range(d)[k] if isinstance(k, slice) else range(k, k + 1)
+            lo, hi, n = lo * d + rg[0], hi * d + rg[-1], n * len(rg)
+        return {"ap": T[nm][tuple([part] + ix)], "reg": [(nm, lo, hi + 1, tag)], "n": n, "d": SCRATCH[nm][2],
+                "ps": SCRATCH[nm][0] == "psum", "ind": False}
+
+    def c2(nm, lo, hi, st=1):
+        return a(nm, slice(lo, hi, st))
+
+    def ind(win, off):
+        return dict(win, ap=win["ap"].indirect(off["ap"]), off=off["reg"], n=16 * off["n"], ind=True)
+
+    def add(e, fn, outs, ins, t, sem=None, inc=16, lat=0.0, mb=0.0, after=()):
+        r, w = [], []
+        for x in ins:
+            if isinstance(x, dict):
+                r += x["reg"] + x.get("off", [])
+        for x in outs:
+            w += x["reg"]
+            r += x.get("off", [])
+        ops.append({"e": e, "fn": fn, "r": r, "w": w, "sem": sem, "inc": inc, "t": t, "lat": lat, "mb": mb,
+                    "after": list(after), "key": len(ops)})
+        return len(ops) - 1
+
+    ap = lambda x: x["ap"] if isinstance(x, dict) else x
+
+    def cost(out, in0, f):
+        if out["ind"]:
+            return 0.05 + out["n"] * 3.8 * CY
+        if in0["ind"]:
+            return 0.05 + in0["n"] * 1.56 * CY
+        if f == 0:
+            f = 0.5 if out["d"] in (B, U, H) and in0["d"] in (B, U, H) else 1
+        return max(64, in0["n"] * f) * CY
+
+    def ts(out, in0, s1, op0, s2=None, op1=None):
+        if op1 is None:
+            add("V", lambda: V.tensor_scalar(out["ap"], in0["ap"], ap(s1), None, op0), [out], [in0, s1], cost(out, in0, 0))
+        else:
+            add("V", lambda: V.tensor_scalar(out["ap"], in0["ap"], ap(s1), ap(s2), op0, op1), [out], [in0, s1, s2],
+                cost(out, in0, 0))
+
+    def tt(out, in0, in1, op):
+        add("V", lambda: V.tensor_tensor(out["ap"], in0["ap"], in1["ap"], op), [out], [in0, in1],
+            cost(out, in0, 1 if in0["ps"] or in1["ps"] else 2))
+
+    def cp(out, in_):
+        add("V", lambda: V.tensor_copy(out["ap"], in_["ap"]), [out], [in_], cost(out, in_, 0))
+
+    def mset(out, v):
+        add("V", lambda: V.memset(out["ap"], v), [out], [], cost(out, out, 0))
+
+    def act(out, in_, func=AF.Identity, scale=1.0, bias=0.0):
+        add("S", lambda: SC.activation(out["ap"], in_["ap"], func, bias=ap(bias), scale=ap(scale)), [out],
+            [in_, scale, bias], cost(out, in_, 1))
+
+    def mm(out, terms):
+        for i, (l, r) in enumerate(terms):
+            mm1(out, l, r, i == 0, i == len(terms) - 1)
+
+    def mm1(out, l, r, st, sp):
+        add("P", lambda: PE.matmul(out["ap"], l["ap"], r["ap"], st, sp), [out], [l, r],
+            max(64, r["n"]) * CY * (2 if r["d"] == F else 0.5))
+
+    def iota(out, pat, base, cm, after=()):
+        t = 0.13 + 2 * out["n"] * CY
+        if out["d"] == I:
+            add("G", lambda: g.iota(out["ap"], pat, base, cm), [out], [], t, after=after)
+        else:
+            add("G", lambda: g.iota(out["ap"], pat, base, cm, allow_small_or_imprecise_dtypes=True), [out], [], t, after=after)
+
+    nd = [0]
+
+    def dma(e, out, in_, new=True, mb=0.02, after=()):
+        if new:
+            nd[0] += 1
+        q = {"Y": g.sync, "S": g.scalar}[e]
+        return add(e, lambda: q.dma_start(ap(out), ap(in_)), [out] if isinstance(out, dict) else [], [in_], 0.06,
+                   sem="d%d" % (nd[0] - 1), lat=2.3, mb=mb, after=after)
+
+    def send(m, piece, land, ready=()):
+        via = [o for o in range(NR) if (rank, o) in rel]
+        tr, n = [], 0
+        es = topo.engines(core, rel[(rank, via[0])])[::-1]
+        for i, o in enumerate(via):
+            k = rel[(rank, o)]
+            w = len(topo.engines(k, T.cores[o]))
+            rid, pid = topo.addr(k, core)
+            tr.append(RemoteDMATransfer(dst_ids=[DstId(rid=rid, pnc=pid)], dma_engine_mask=bits(es[n:n + w]),
+                                        remote_sem=T.sem["h" + m], src=piece(o)["ap"], dst=slot(T, m)))
+            n += w
+        calls = [add("G", lambda: g.remote_dma_fused(tr, local_sem=T.sem.sent), [], [piece(o) for o in via] + list(ready),
+                     2.5 if m == "tg" else 0.5, sem="sent", inc=n)]
+        for o in range(NR):
+            if o != rank and o not in via:
+                d = T.cores[o]
+                rid, pid = topo.addr(d, core)
+                calls.append(add("G", lambda o=o, d=d, rid=rid, pid=pid: g.remote_dma(
+                    landing(T, m, rank), piece(o)["ap"], T.sem["a" + m], T.sem.sent, pid, rid, topo.mask(core, d)),
+                    [], [piece(o)], 0.5, sem="sent", inc=len(topo.engines(core, d)), after=calls[:1]))
+        tot = sum(len(topo.engines(rel.get((q, rank), T.cores[q]), core)) for q in range(NR) if q != rank)
+        add("X", None, [land(q) for q in range(NR) if q != rank], [], HOP, sem="a" + m, inc=tot, after=calls)
+        return calls
+
+    def send_one(m, o, piece, land):
+        via = [k for k in range(NR) if (rank, k) in rel]
+        d = rel.get((rank, o), T.cores[o])
+        rid, pid = topo.addr(d, core)
+        if o in via:
+            w = len(topo.engines(d, T.cores[o]))
+            es = topo.engines(core, d)[::-1][w * via.index(o):w * via.index(o) + w]
+            dst, sem = slot(T, m), T.sem["h" + m]
+        else:
+            es, dst, sem = topo.engines(core, d), landing(T, m, rank), T.sem["a" + m]
+        k = add("G", lambda: g.remote_dma(dst, piece["ap"], sem, T.sem.sent, pid, rid, bits(es)), [], [piece], 0.5,
+                sem="sent", inc=len(es))
+        add("X", None, [land], [], HOP + 0.5 if o in via else HOP / 2, sem="a" + m,
+            inc=len(topo.engines(rel.get((o, rank), T.cores[o]), core)), after=[k])
+
+    cols = {}
+
+    def col(nm):
+        if nm not in cols:
+            cols[nm] = len(cols)
+        return c2("cc", cols[nm], cols[nm] + 1)
+
+    eye = lambda k, i: a("eye", k, slice(i, i + 1))
+    ED = {k: i for i, k in enumerate(["RXO", "RX", "RW", "I", "NI", "BDH", "NS4", "VB", "CY", "GW", "I4", "BD"] + ["REP%d" % q for q in range(8)])}
+    KG = {k: i for i, k in enumerate(["UB", "LB", "UW", "VW", "S0", "S1", "S2", "S3", "JW", "S4"])}
+    ed = lambda k: a("ed", ED[k])
+    eg = lambda k: a("eg", KG[k])
+    zv = lambda k, r: a("zz", k, slice(15 - r, 143 - r))
+    mwin = c2("mt", PAD, PAD + WT)
+    mrow = lambda s, lo, hi: a("mt", slice(lo, hi), part=slice(s, 128, 16), tag=s)
+
+    mset(a("x0i"), 0)
+    first = [dma("S", c2("ta", S * rank, S * rank + S), T.tg[:])]
+    for e in range(4):
+        first.append(dma("YS"[e % 2], a("x0i", part=slice(8 + e, 128, 16), tag=e), T.x0[e::4, :], new=e == 0))
+    for m in range(16):
+        first.append(dma("YS"[m % 2], c2("mt", PAD + 256 * m, PAD + 256 * m + 256), T.cf[m::16, :], mb=0.065, after=first[:5]))
+    dma("Y", c2("ftab", 0, FC), T.ft[:], mb=0.26, after=first)
+    iota(c2("pint", 0, 1), [[1, 1]], 0, 1)
+    iota(a("r4"), [[16, 8], [0, 4], [1, 4]], 8, 0)
+    iota(a("io_"), [[1, S]], 0, 0)
+    iota(a("g16"), [[16, 8], [0, 16]], 0, 0)
+    send("tg", lambda o: c2("ta", S * rank, S * rank + S), lambda q: c2("ta", S * q, S * q + S))
+
+    pi = lambda i: c2("pint", i, i + 1)
+    mset(a("one"), 1.0)
+    mset(c2("yr", 0, NR * S), 0.0)
+    cp(col("p"), pi(0))
+    ts(pi(1), pi(0), 15, Op.bitwise_and)
+    ts(pi(2), pi(0), 2, Op.logical_shift_right, 3, Op.bitwise_and)
+    ts(pi(3), pi(0), 3, Op.bitwise_and)
+    ts(ed("RXO"), a("r4"), col("p"), Op.is_equal)
+    cp(col("p16"), pi(1))
+    ts(col("q1"), pi(2), 1.0, Op.add)
+    ts(col("ini"), pi(2), float(S), Op.mult, -1.0, Op.add)
+    ts(col("thr"), pi(2), float(S), Op.mult, float(CAP), Op.add)
+    ts(a("ed", ED["RXO"], slice(15, 128, 16)), c2("io_", 15, 128, 16), col("p"), Op.is_equal)
+    ts(col("oc"), pi(3), 2.0, Op.is_equal, col("q1"), Op.mult)
+    ts(a("eye", 0), c2("io_", 0, 16), col("p16"), Op.is_equal)
+    ts(col("g16"), col("p"), col("p16"), Op.subtract)
+    ts(col("off"), col("p16"), 8.0, Op.is_lt, 192.0, Op.mult)
+    ts(col("t1"), col("p16"), 8.0, Op.is_ge, 0.75, Op.mult)
+    ts(col("t2"), pi(2), 1.0, Op.is_equal, 0.25, Op.mult)
+    ts(col("tm"), eye(0, 12), eye(0, 13), Op.add)
+    ts(a("z16"), c2("io_", 0, 144), -15.0, Op.add, col("g16"), Op.is_equal)
+    ts(col("t3"), col("off"), -0.375 / 192, Op.mult, col("t2"), Op.add)
+    ts(col("sc"), col("t1"), 0.25, Op.add, col("tm"), Op.subtract)
+    ts(col("bi"), col("t3"), eye(0, 12), Op.add, col("off"), Op.add)
+    for o in range(NR):
+        act(c2("xw", S * o, S * o + CAP), c2("one", 0, CAP), scale=col("tm"))
+    cp(c2("xp", 0, S), a("x0i"))
+
+    def source(r):
+        px, pslot = c2("pH", 0, S), c2("pH", 256, 266)
+        old = c2("xp", S * r, S * r + S)
+        if r == 0:
+            ts(a("clp"), a("io_"), eye(0, 15), Op.mult)
+            mm(px, [(ed("RXO"), a("clp")), (ed("RXO"), old)])
+            cp(a("xa"), px)
+        else:
+            back = ind(c2("yr", NR * S * (r - 1), NR * S * r), c2("sl", 16 * (r - 1), 16 * (r - 1) + 10))
+            mm1(px, ed("RXO"), old, True, False)
+            mm1(px, ed("RW"), a("wt"), False, False)
+            ts(a("clp"), back, 120.0, Op.max, 136.0, Op.min)
+            mm1(px, ed("RX"), a("clp"), False, True)
+            sums = c2("acc", S * (r - 1), S * r)
+            if r == 1:
+                act(sums, back)
+            else:
+                tt(sums, back, c2("acc", S * (r - 2), S * (r - 1)), Op.add)
+            if r == RO:
+                dma("Y", T.ys[:], sums)
+            ts(a("xa"), px, col("cadd"), Op.add)
+        if r == RO:
+            ts(a("xi"), a("xa"), 255, Op.bitwise_and)
+            cp(a("xf"), a("xi"))
+            for e in range(4):
+                dma("YS"[e % 2], T.yx[e::4, :], a("xf", part=slice(e, 128, 16)), new=e == 0)
+            return
+        ts(a("oh"), a("xa"), 6, Op.logical_shift_right, 3, Op.bitwise_and)
+        ts(a("xi"), a("xa"), 255, Op.bitwise_and)
+        ts(a("hh"), a("oh"), 1.0, Op.add, col("oc"), Op.is_equal)
+        ts(a("xq"), a("xi"), col("sc"), Op.mult, col("bi"), Op.add)
+        add("V", lambda: V.tensor_tensor_scan(T.cum[:], T.one[:], T.hh[:], col("ini")["ap"], Op.mult, Op.add),
+            [a("cum")], [a("one"), a("hh"), col("ini")], S * CY / 2)
+        new = c2("xp", S * (r + 1), S * (r + 2))
+        tt(a("prd"), a("hh"), a("cum"), Op.mult)
+        mm(pslot, [(c2("z16", 15 - k, 143 - k), c2("prd", k, S, 16)) for k in range(16)])
+        ts(new, a("xq"), col("off"), Op.subtract)
+        ts(a("wt"), a("prd"), col("thr"), Op.is_ge)
+        sl = c2("sl", 16 * r, 16 * r + 10)
+        cp(sl, pslot)
+        base = NR * S * r
+        cp(ind(c2("xw", base, base + NR * S), sl), new)
+        piece = lambda o: c2("xw", base + S * o, base + S * o + CAP)
+        land = lambda q: a("xl", slice(8 * r + 2 * q, 8 * r + 2 * q + 2))
+        act(land(rank), piece(rank))
+        return send("x%d" % r, piece, land, [c2("yr", base, base + NR * S)])
+
+    sent0 = source(0)
+    iota(c2("jj", 0, 256), [[1, 16], [0, 16]], 0, 0, after=sent0)
+    iota(c2("dmp", 0, 16), [[0, 8], [16, 2]], DC, 0, after=sent0)
+    for lo in range(0, WT, WT // 8):
+        iota(c2("iot", lo, lo + WT // 8), [[1, WT // 8]], lo, 0, after=sent0)
+
+    def keys(m):
+        bank = c2("pC" if m % 2 else "pD", 0, 256)
+        acc = c2("mx", 0, 256)
+        if m == 0:
+            act(acc, c2("mt", PAD, PAD + 256), scale=16.0, bias=15.0)
+            return
+        act(bank, c2("mt", PAD + 256 * m, PAD + 256 * m + 256), scale=16.0, bias=float(15 - m))
+        tt(a("ki") if m == 15 else acc, bank, acc, Op.max)
+
+    one = lambda n: c2("one", 0, n)
+    ts(pi(4), pi(0), 1, Op.logical_shift_right, 1, Op.bitwise_and)
+    ts(pi(5), pi(0), 3, Op.logical_shift_right, 1, Op.bitwise_and)
+    ts(a("pa"), c2("io_", 0, 16), -1.0, Op.mult, col("p"), Op.add)
+    ts(a("gm"), c2("g16", 0, 128, 16), col("g16"), Op.is_equal)
+    mset(a("ka"), 0.0)
+    mset(a("kg"), 0.0)
+    mset(a("ea"), 0.0)
+    for k, v in enumerate((4.0, -1.0, -4.0, 188.0, 916.0, 592.0, 176.0, 768.0, 60.0)):
+        act(a("eye", k + 1), a("eye", 0), scale=v)
+    E1, E4, EN, EN4, E188, E916, E592, E176, E768, E60 = range(10)
+    HI, HS, XR, ONE, DEAD, SID = 0, 4, 8, 12, 13, 15
+
+    def kset(nm, m, lo, hi, st, t1, t2=None):
+        out = a(nm, m, slice(lo, hi, st))
+        act(out, one(len(range(lo, hi, st))), scale=eye(*t1), bias=eye(*t2) if t2 else 0.0)
+
+    def kadd(nm, m, lo, hi, st, t):
+        out = a(nm, m, slice(lo, hi, st))
+        act(out, out, bias=eye(*t))
+
+    kset("ka", 0, 0, 4, 2, (E1, HI)); kset("ka", 0, 1, 4, 2, (E1, HI), (E1, ONE))
+    kset("ka", 0, 4, 5, 1, (E1, HS)); kset("ka", 0, 5, 6, 1, (E4, HS + 2))
+    kset("ka", 1, 0, 4, 1, (E1, HI + 1)); kset("ka", 1, 4, 5, 1, (E1, HS + 1)); kset("ka", 1, 5, 6, 1, (E1, HS + 3))
+    kset("ka", 2, 0, 4, 1, (E188, HI + 2), (E916, HI + 3)); kset("ka", 2, 4, 5, 1, (E188, HS + 2), (E916, HS + 3))
+    kset("ka", 2, 5, 6, 1, (E592, HS), (E176, HS + 1)); kset("ka", 2, 6, 7, 1, (E1, SID))
+    act(a("ka", 2, slice(7, 8)), eye(E1, DEAD), scale=8192.0)
+    for m in range(4):
+        keys(m)
+    kset("kg", KG["UB"], 0, 16, 1, (E4, HI + 2))
+    kadd("kg", KG["UB"], 4, 8, 1, (E4, ONE)); kadd("kg", KG["UB"], 12, 16, 1, (E4, ONE))
+    kset("kg", KG["LB"], 0, 16, 1, (E592, HI), (E176, HI + 1))
+    for kk, e in ((1, E592), (2, E176), (3, E768)):
+        kadd("kg", KG["LB"], kk, 16, 4, (e, ONE))
+    for m in range(4, 8):
+        keys(m)
+    for b, e in ((0, 0), (4, 2)):
+        kset("kg", KG["UW"], b, b + 4, 2, (E4, HI + e), (EN, XR + e)); kadd("kg", KG["UW"], b, b + 4, 2, (E4, ONE))
+        kset("kg", KG["UW"], b + 1, b + 4, 2, (EN4, HI + e), (E1, XR + e))
+        kset("kg", KG["VW"], b, b + 4, 1, (EN4, HI + e + 1), (E1, XR + e + 1))
+    for kk in range(4):
+        cp(a("kg", KG["S%d" % kk], slice(kk, 16, 4)), a("eye", 0, slice(0, 4)))
+    ts(a("kg", KG["JW"], slice(0, 1)), col("p16"), 0.5, Op.mult)
+    cp(a("kg", KG["S4"], slice(4, 5)), eye(E1, 4))
+    ts(col("bva"), pi(4), 2.0, Op.mult, 1.0, Op.add)
+    ts(col("bvb"), pi(5), 2.0, Op.mult, 1.0, Op.add)
+    ts(col("sw"), pi(4), 2.0, Op.mult, -1.0, Op.add)
+    ts(col("bw"), pi(4), -4.0, Op.mult, 4.0, Op.add)
+    for m in range(8, 16):
+        keys(m)
+    ts(c2("k2", 0, 256), a("ki"), 15, Op.bitwise_and)
+    ts(c2("k2", 256, 512), a("ki"), 4, Op.logical_shift_right)
+    ts(c2("mq", 0, 256), c2("k2", 0, 256), -1.0, Op.mult, 15.0, Op.add)
+    cp(c2("mq", 256, 512), c2("k2", 256, 512))
+    mset(c2("mt", PAD + WC, PAD + WT), 0.0)
+    for s, sh in enumerate(SHIFTS):
+        dma("Y", mrow(s, PAD - sh, PAD - sh + WC), c2("mq", 0, 256), new=s == 0)
+        for q in range(2):
+            n = min(sh - 256 * q, 256)
+            if n > 0:
+                lo = PAD - sh + WC + 256 * q
+                dma("Y", mrow(s, lo, lo + n), a("mq", slice(0, n), part=slice(q, 128, 16)), new=False)
+    k = dma("Y", mrow(4, PAD, PAD + WC), c2("mq", 256, 512), new=False)
+    dma("Y", c2("ctab", 0, WC), T.cf[:], mb=1.0, after=range(k - 8, k + 1))
+    for gq in range(8):
+        gm = c2("gm", gq, gq + 1)
+        act(a("ea", slice(gq % 2, 6, 2), slice(16 + 16 * gq, 32 + 16 * gq)), a("ka"), scale=gm)
+        ts(a("eg", slice(None), slice(16 * gq, 16 * gq + 16)), a("kg"), gm, Op.mult)
+    pac = lambda i: c2("pa", i, i + 1)
+    ts(ed("BD"), a("g16"), col("g16"), Op.is_equal)
+    act(ed("VB"), ed("BD"), scale=eye(E1, HI + 3))
+    ts(ed("I"), c2("io_", 0, 128), col("p"), Op.is_equal)
+    for q in range(8):
+        act(ed("REP%d" % q), ed("BD"), scale=eye(E1, q))
+    ts(a("zz", 0), a("z16"), 1.0, Op.mult)
+    ts(ed("CY"), a("g16"), pac(ONE), Op.is_equal, -255.0 / 512, Op.mult)
+    cp(a("i16"), ed("I"))
+    act(a("i32"), ed("I"), scale=1.0 / 256)
+    act(ed("NI"), ed("I"), scale=-1.0)
+    act(a("zz", 1), a("zz", 0), scale=8192.0)
+    act(a("zz", 2), a("zz", 0), scale=eye(E1, 0))
+    ts(c2("dmp", 0, 16), c2("dmp", 0, 16), col("p16"), Op.add)
+    ts(a("lx"), one(16), col("p16"), Op.mult)
+    cp(c2("ld", 0, 16), c2("io_", 0, 16))
+    cp(c2("ld", 16, 24), c2("io_", 0, 16, 2))
+    mset(c2("ctab", WC, WT), 0.0)
+    mset(c2("ftab", FC, FC + 32), 0.0)
+    ts(c2("dmp", 16, 32), c2("dmp", 0, 16), float(DF - DC), Op.add)
+
+    def late():
+        ts(a("tri"), c2("io_", 0, 16), col("p16"), Op.is_gt)
+        ts(col("jp1"), col("p16"), 1.0, Op.add)
+        ts(col("eb"), col("p16"), -LN4, Op.mult)
+        ts(col("cadd"), col("p16"), 15.0, Op.is_lt, 128.0, Op.mult)
+        ts(ed("RX"), a("r4"), -8.0, Op.add, col("p"), Op.is_equal)
+        act(ed("RW"), ed("BD"), scale=8.0)
+        act(ed("GW"), ed("BD"), scale=-0.5)
+        tt(ed("BDH"), ed("GW"), ed("I"), Op.add)
+        if PACK:
+            ts(pi(6), pi(0), 1, Op.bitwise_and)
+            ts(col("ev"), pi(6), -256.0, Op.mult, 256.0, Op.add)
+            ts(col("pm"), pi(6), 2.0, Op.mult, -1.0, Op.add)
+            act(ed("I4"), ed("I"), scale=4096.0)
+            ts(a("d16"), ed("I"), col("pm"), Op.mult)
+            ts(a("ed", ED["GW"], slice(0, 128, 2)), c2("g16", 0, 128, 2), col("g16"), Op.is_equal, 127.5 / 4096, Op.mult)
+            ts(a("ed", ED["GW"], slice(1, 128, 2)), c2("g16", 1, 128, 2), col("g16"), Op.is_equal, 128.0, Op.mult)
+            mset(a("z2"), 0.0)
+            tt(c2("z2", 0, 143), a("zz", 0, slice(0, 143)), a("zz", 0, slice(1, 144)), Op.add)
+            act(a("z2"), a("z2"), scale=1.0 / 4096)
+        act(ed("NS4"), ed("BD"), scale=eye(EN, 4))
+        for k in range(16):
+            if k % 2:
+                ts(a("et", k), zv(1, k), c2("tri", k, k + 1), Op.mult)
+            else:
+                act(a("et", k), zv(1, k), scale=c2("tri", k, k + 1))
+        act(a("zz", 3), a("zz", 0), scale=col("jp1"))
+        mset(a("ed", slice(ED["RX"], ED["RW"] + 1), slice(15, 128, 16)), 0.0)
+        for r in range(1, RO):
+            for o in range(NR):
+                lo = NR * S * r + S * o
+                act(c2("xw", lo, lo + CAP), c2("one", 0, CAP), scale=col("tm"))
+
+    mset(c2("yr", NR * S, RO * NR * S), 0.0)
+    late()
+
+    half = lambda nm, h: a(nm, slice(8 * h, 8 * h + 8))
+    ftw = c2("ftab", 0, FC + 32)
+    kw = lambda r, lo, hi, st=1: c2("kw", 32 * r + lo, 32 * r + hi, st)
+    lk = lambda r, lo, hi: c2("lk", 48 * r + lo, 48 * r + hi)
+    tmp = lambda i: c2("tmp", 16 * i, 16 * i + 16)
+
+    def index(r):
+        X = a("xl", slice(8 * r, 8 * r + 8))
+
+        def swapped(nm, h0, m):
+            for g2 in range(2):
+                out = a(nm, slice(8 * h0, 8 * h0 + 8), slice(16 * g2, 16 * g2 + 16))
+                mm(out, [(a("ea", 2 * m + g2, slice(16 - 16 * (h - g2), 144 - 16 * (h - g2))),
+                          a("xl", slice(8 * r, 8 * r + 8), slice(16 * h, 16 * h + 16))) for h in range(2)])
+        swapped("pB", 0, 1)
+        swapped("pA", 0, 0)
+        swapped("pA", 1, 2)
+        act(c2("va", 0, 256), half("pB", 0), scale=2.0, bias=col("bva"))
+        mm(half("pB", 1), [(ed("VB"), X)])
+        mm(c2("pD", 256, 512), [(eg("VW"), X)])
+        mm(c2("pD", 0, 256), [(eg("UW"), X)])
+        mm(c2("pC", 0, 256), [(eg("UB"), X)])
+        mm(c2("pC", 256, 512), [(eg("LB"), X)])
+        act(c2("va", 256, 512), half("pB", 1), scale=2.0, bias=col("bvb"))
+        act(c2("va", 512, 768), c2("pD", 256, 512), scale=col("sw"), bias=col("bw"))
+        tt(a("ra"), half("pA", 0), c2("va", 0, 256), Op.mult)
+        tt(a("tsw"), half("pA", 1), a("ra"), Op.add)
+        add("V", lambda: V.transpose(T.tw[:], T.tsw[:]), [a("tw")], [a("tsw")], 256 * CY)
+        al = slice(None)
+        ts(a("ti"), a("tw", al, slice(0, 5)), 2, Op.logical_shift_right, WC - 1, Op.bitwise_and)
+        tt(a("wq"), c2("pD", 0, 256), c2("va", 512, 768), Op.mult)
+        for kk in range(4):
+            cp(c2("of1", 16 * kk, 16 * kk + 16), a("ti", al, kk))
+        for h in range(2):
+            (act, cp if VM else act)[h](c2("mg", 512 * h, 512 * h + 512), ind(mwin, c2("of1", 32 * h, 32 * h + 32)))
+        for s in range(4):
+            mm(c2("pG" if s < 2 else "pH", 256 * (s % 2), 256 * (s % 2) + 256), [(ed("REP%d" % (4 + s)), a("wq"))])
+        for h, nm in enumerate(("pE", "pF")):
+            for kk in range(4):
+                mm(c2(nm, 128 * kk, 128 * kk + 128), [(ed("REP%d" % kk), c2("wq", 128 * h, 128 * h + 128))])
+        tt(a("rbb"), c2("pC", 0, 256), c2("va", 256, 512), Op.mult)
+        tt(tmp(0), a("ti", al, 4), a("tw", al, 7), Op.add)
+        tt(a("tb"), c2("pC", 256, 512), a("rbb"), Op.add)
+        tt(kw(r, 0, 16), tmp(0), c2("dmp", 0, 16), Op.min)
+        ts(a("tb2"), a("tb"), 1008, Op.bitwise_and)
+        cp(lk(r, 0, 16), kw(r, 0, 16))
+        cp(a("b16"), a("tb2"))
+        po = half("pB", 1)
+        mm(po, [(eg("S%d" % kk), c2("mg", 256 * kk, 256 * kk + 256)) for kk in range(4)] + [(ed("I"), a("b16"))])
+        act(a("wcd", slice(0, 2)), a("pG"))
+        act(a("wcd", slice(2, 4)), a("pH"))
+        cp(lk(r, 16, 24), kw(r, 1, 16, 2))
+        ts(a("bw"), a("tw", al, 5), 1008, Op.bitwise_and)
+        cp(a("sid"), a("tw", al, 6))
+        cp(a("of2"), po)
+
+    def value(r):
+        al = slice(None)
+        yb = lambda lo, hi: c2("yb", 256 * r + lo, 256 * r + hi)
+        base = NR * S * r
+        land = lambda q: c2("yr", base + S * q, base + S * q + CAP)
+        turn = sorted(range(NR), key=lambda q: (q == rank, (rank, q) not in rel))
+        for i, c in enumerate(turn):
+            lo, hi = 64 * c, 64 * c + 64
+            if i == 0 and VL:
+                ts(c2("vv", 16 * lo, 16 * (lo + VL)), ind(ftw, c2("of2", lo, lo + VL)), -128.0, Op.add)
+                lo += VL
+            if hi > lo:
+                act(c2("vv", 16 * lo, 16 * hi), ind(ftw, c2("of2", lo, hi)), bias=-128.0)
+        for i, c in enumerate(turn):
+            lo, sums, py = 64 * c, ("pC", "pD")[i % 2], c2(("pG", "pH")[i % 2], 0, 64)
+            pp = lambda k: c2("pp", 16 * lo + 64 * k, 16 * lo + 64 * k + 64)
+            for s in range(4):
+                for kk in range(4):
+                    o = 128 * kk + lo % 128
+                    tt(pp(4 * s + kk), c2("vv", 16 * lo + 4 * s + kk, 16 * lo + 1024, 16), c2(("pE", "pF")[c // 2], o, o + 64), Op.mult)
+                mm(c2(sums, 64 * s, 64 * s + 64), [(a("i16"), pp(4 * s + kk)) for kk in range(4)])
+            tt(c2("qq", 4 * lo, 4 * lo + 256), c2(sums, 0, 256), a("wcd", al, slice(lo, lo + 64)), Op.mult)
+            mm(py, [(ed("CY"), a("xl", slice(8 * r + 2 * c, 8 * r + 2 * c + 2)))]
+               + [(a("i32"), c2("qq", 4 * lo + 64 * s, 4 * lo + 64 * s + 64)) for s in range(4)])
+            ts(yb(lo, lo + 64), py, MAGIC + 128.0, Op.add, MAGIC, Op.subtract)
+            if c == rank:
+                cp(land(c), yb(lo, lo + 64))
+            else:
+                send_one("y%d" % r, c, yb(lo, lo + 64), land(c))
+
+    def dedupe(r, t):
+        key = kw(r, 16 * t, 16 * t + 16)
+        act(c2("kr", 384 * t, 384 * t + 384), ind(a("iot"), lk(r, 24 * t, 24 * t + 24)))
+        eq = lambda lo, hi, st=1: c2("eq", 384 * t + lo, 384 * t + hi, st)
+        tt(eq(0, 384), ind(key, a("ld")), c2("kr", 384 * t, 384 * t + 384), Op.is_equal)
+        bank = lambda lo, st: c2("pG", lo, 16, st) if t else a("pB", 1, slice(lo, 16, st))
+        for k in range(16):
+            mm1(bank(0, 1), a("et", k), eq(k, 256, 16), k == 0, False)
+        for k in range(16):
+            mm1(bank(1, 2), zv(1, k), eq(256 + k, 384, 16), False, k == 15)
+        t1, t2 = tmp(3 + 2 * t), tmp(4 + 2 * t)
+        tt(t1, bank(0, 1), key, Op.add)
+        tt(t2, t1, c2("dmp", 16 * t, 16 * t + 16), Op.min)
+        cp(c2("lo", 32 * r + 16 * t, 32 * r + 16 * t + 16), t2)
+
+    def early(r):
+        al = slice(None)
+        act(a("ms"), ind(mwin, lk(r, 0, 16)))
+        mm(a("pB", 0, slice(0, 16)), [(zv(2, k), c2("ms", k, 256, 16)) for k in range(16)])
+        tt(tmp(1), a("bw"), a("tw", al, 7), Op.add)
+        tt(tmp(2), a("pB", 0, slice(0, 16)), tmp(1), Op.add)
+        tt(kw(r, 16, 32), tmp(2), c2("dmp", 16, 32), Op.min)
+        cp(lk(r, 24, 40), kw(r, 16, 32))
+        cp(lk(r, 40, 48), kw(r, 17, 32, 2))
+        dedupe(r, 0)
+        for q in range(NR):
+            act(c2("tgl", CAP * q, CAP * q + CAP), ind(c2("ta", S * q, S * q + S), c2("sid", 4 * q, 4 * q + 4)))
+        act(a("fg"), ind(ftw, lk(r, 24, 40)))
+        act(c2("cg", 256 * r, 256 * r + 256), ind(a("ctab"), lk(r, 0, 16)))
+        if PACK:
+            mm(a("pA"), [(ed("I"), c2("ftab", 0, FC, 2)), (ed("I4"), c2("ftab", 1, FC, 2))])
+            act(a("f2"), a("pA"), bias=-127.5 - 128.0 * 4096)
+            ts(a("bw8"), a("tw", al, 5), 1, Op.logical_shift_right, 504, Op.bitwise_and)
+            tt(c2("ofu", 0, 128), ind(a("bw8"), c2("lx", 0, 8)), c2("jj", 0, 128), Op.add)
+            cp(c2("ou", 0, 128), c2("ofu", 0, 128))
+            for i in range(4):
+                act(c2("v3", 512 * i, 512 * i + 512), ind(a("f2"), c2("ou", 32 * i, 32 * i + 32)))
+        else:
+            tt(a("ofu"), ind(a("bw"), a("lx")), a("jj"), Op.add)
+            cp(a("ou"), a("ofu"))
+            for i in range((16 - VJ) // 2):
+                act(c2("v2", 512 * i, 512 * i + 512), ind(ftw, c2("ou", 32 * i, 32 * i + 32)))
+
+    def train(r):
+        last = r == RO - 1
+        pg, pu = c2("pE", 0, 256), c2("pF", 0, 256)
+        cg, uu = c2("cg", 256 * r, 256 * r + 256), c2("uu", 256 * r, 256 * r + 256)
+        mm(half("pA", 0), [(ed("I"), a("tgl")), (ed("NI"), c2("yb", 256 * r, 256 * r + 256))])
+        act(pg, half("pA", 0), AF.Sign)
+        act(a("gs"), half("pA", 0), AF.Sign)
+        dedupe(r, 1)
+        mm(c2("pG", 256, 512), [(ed("I"), a("fg")), (ed("I"), a("gs"))])
+        ts(a("fn"), c2("pG", 256, 512), 0.0, Op.max, 255.0, Op.min)
+        if PACK:
+            for j in range(8):
+                gv = c2("gw", 256 * j, 256 * j + 256)
+                tt(gv, c2("v3", 256 * j, 256 * j + 256), pg, Op.mult)
+                mm1(pu, c2("z2", 14 - 2 * j, 142 - 2 * j), gv, j == 0, j == 7)
+            ts(a("hi"), pu, MAGIC, Op.add, MAGIC, Op.subtract)
+            act(a("zc"), pu, scale=col("ev"))
+            pu = c2("pE", 256, 512)
+            mm(pu, [(ed("GW"), a("gs")), (a("d16"), a("hi")), (a("i32"), a("zc"))])
+        else:
+            for n, j in enumerate(list(range(16 - VJ)) + list(range(16 - VJ, 16))):
+                gv = c2("gv", 256 * j, 256 * j + 256)
+                if j < 16 - VJ:
+                    tt(gv, c2("v2", 256 * j, 256 * j + 256), pg, Op.mult)
+                else:
+                    tt(gv, ind(ftw, c2("ou", 16 * j, 16 * j + 16)), a("gs"), Op.mult)
+                mm1(pu, zv(0, j), gv, n == 0, n == 15)
+        act(uu, pu, AF.Sign)
+
+        def scat(win, t, fn):
+            for k in range(7, -1, -1):
+                o = 32 * r + 16 * t + 2 * k
+                fn(ind(win, c2("lo", o, o + 2)), 32 * k, 32 * k + 32)
+        scat(ftw, 1, lambda w, lo, hi: cp(w, c2("fn", lo, hi)))
+        scat(a("ctab"), 0, lambda w, lo, hi: tt(w, c2("cg", 256 * r + lo, 256 * r + hi), c2("uu", 256 * r + lo, 256 * r + hi), Op.add))
+        source(r + 1)
+        if last:
+            dma("S", T.yf[:], c2("ftab", 0, FC), mb=0.26)
+            mm(c2("pC", 0, 256), [(zv(3, q), c2("ctab", 256 * q, 256 * q + 256)) for q in range(16)])
+            act(a("yo"), c2("pC", 0, 256))
+            dma("Y", T.yc[:], a("yo"), mb=0.13)
+            return
+        mm(c2("pF", 256, 512), [(ed("I"), cg), (ed("NS4"), a("ms")), (ed("I"), uu)])
+        act(a("ee"), c2("pF", 256, 512), AF.Exp, scale=16 * LN4, bias=col("eb"))
+        mm(pg, [(ed("BDH"), a("ee"))])
+        act(a("ohm"), pg, AF.Sign)
+        mm(c2("pF", 0, 256), [(eg("S4"), a("ms")), (eg("JW"), a("ohm"))])
+        act(a("mn"), c2("pF", 0, 256), bias=eye(E60, 0))
+        scat(mwin, 0, lambda w, lo, hi: cp(w, c2("mn", lo, hi)))
+        for s in range(1, 4):
+            sh = SHIFTS[s]
+            dma("YSY"[s - 1], mrow(s, PAD, PAD + WC - sh), mrow(0, PAD + sh, PAD + WC), new=s == 1, mb=0.065)
+            dma("SYS"[s - 1], mrow(s, PAD + WC - sh, PAD + WC), mrow(0, PAD, PAD + sh), new=False, mb=0.0)
+
+    for r in range(RO):
+        index(r)
+        early(r)
+        value(r)
+        train(r)

@@ -11,10 +11,14 @@ MAGIC = 12582912.0
 LN4 = math.log(4.0)
 VL = 64
 PACK = True
-VM = False
+VM = 1
 VJ = 2
-CY, WAKE, SLACK, HOP = 1.04e-3, 0.06, 0.02, 5.0
-PASSES, BLEND, SEED, SPAN, PRIO = 0, 60, 1, [0.0], {}
+CY, WAKE, SLACK, HOP = 0.9e-3, 0.2, 0.02, 5.5
+ALPHA, SWEEPS, LOOK, GAP = (0.3, 0.15), 1, 0.8, 1.5
+ADD, ADDP, PEF = 0.03, 0.0, 1.3
+LB = 8
+PC = ((0, 128), (128, 64), (192, 64))
+PASSES, BLEND, SEED, SPAN, PRIO = 0, 30, 1, [0.0], {}
 
 sb = lambda shape, d: ("sbuf", shape, d)
 ps = lambda shape: ("psum", shape, "float32")
@@ -37,12 +41,12 @@ SCRATCH = {
     "mx": sb([128, 512], F), "ki": sb([128, 256], I), "k2": sb([128, 512], I), "mq": sb([128, 512], B),
     "va": sb([128, 768], F), "ra": sb([128, 256], F), "tsw": sb([128, 256], I), "tw": sb([128, 16, 16], I),
     "ti": sb([128, 16, 5], I), "of1": sb([128, 64], U), "rbb": sb([128, 256], F), "tb": sb([128, 256], I),
-    "tb2": sb([128, 256], I), "b16": sb([128, 256], B), "wq": sb([128, 256], B), "wcd": sb([128, 4, 256], B),
+    "tb2": sb([128, 256], I), "b16": sb([128, 256], B), "wq": sb([128, 256], B), "wcd": sb([128, 2, 4, 128], B),
     "mg": sb([128, 1024], B), "ms": sb([128, 256], B), "of2": sb([128, 256], U),
     "vv": sb([128, 4096], B), "pp": sb([128, 4096], H), "qq": sb([128, 1024], F),
     "tmp": sb([128, 112], F), "kw": sb([128, RO * 32], F), "lk": sb([128, RO * 48], U), "bw": sb([128, 16], I),
     "ofu": sb([128, 256], F), "ou": sb([128, 256], U), "sid": sb([128, 16], U), "tgl": sb([128, 256], B),
-    "kr": sb([128, 768], F), "eq": sb([128, 768], B), "lo": sb([128, RO * 32], U),
+    "kr": sb([128, 768], F), "eq": sb([128, 2, 384], B), "lo": sb([128, RO * 32], U),
     "v2": sb([128, 4096], B), "gv": sb([128, 4096], B), "gs": sb([128, 256], B), "uu": sb([128, RO * 256], B),
     "f2": sb([128, 512], F), "v3": sb([128, 2048], F), "gw": sb([128, 2048], F), "bw8": sb([128, 16], I),
     "hi": sb([128, 256], H), "zc": sb([128, 256], F), "z2": sb([128, 144], F), "d16": sb([128, 128], H),
@@ -53,7 +57,7 @@ SCRATCH = {
 }
 MSGS = ["tg"] + [k + str(r) for r in range(RO) for k in "xy"]
 SEMAPHORES = (["cV", "cS", "cP", "cG", "sent"] + ["a" + m for m in MSGS] + ["h" + m for m in MSGS]
-              + ["d%d" % i for i in range(40)])
+              + ["b" + m for m in MSGS if m[0] != "y"] + ["d%d" % i for i in range(40)])
 
 
 def relays(T, topo):
@@ -73,12 +77,17 @@ def bits(es):
     return sum(1 << e for e in es)
 
 
-def landing(T, m, q):
+def places(o, rel):
+    return sorted(range(NR), key=lambda q: (q == o, (o, q) not in rel))
+
+
+def landing(T, m, q, o, rel):
     if m == "tg":
         return T.ta[:, S * q:S * q + S]
     r = int(m[1])
     if m[0] == "x":
-        return T.xl[:, 8 * r + 2 * q:8 * r + 2 * q + 2, :]
+        i = places(o, rel).index(q)
+        return T.xl[:, 8 * r + 2 * i:8 * r + 2 * i + 2, :]
     return T.yr[:, NR * S * r + S * q:NR * S * r + S * q + CAP]
 
 
@@ -93,7 +102,7 @@ def relay_program(g, core, T, topo, q, o):
     rid, pid = topo.addr(dst, core)
     for m in MSGS:
         g.wait_ge(T.sem["h" + m], n)
-        g.remote_dma(landing(T, m, q), slot(T, m), T.sem["a" + m], T.sem.sent, pid, rid, topo.mask(core, dst))
+        g.remote_dma(landing(T, m, q, o, relays(T, topo)), slot(T, m), T.sem["a" + m], T.sem.sent, pid, rid, topo.mask(core, dst))
     g.wait_ge(T.sem.sent, n * len(MSGS))
 
 
@@ -176,6 +185,10 @@ def emit(g, T, ops):
         while any(rdy.values()):
             t0, e = min((max(min(d.values()), free.get(q, 0.0)), q) for q, d in rdy.items() if d)
             n = max((k for k, t in rdy[e].items() if t <= t0 + SLACK), key=lambda k: (prio[k], -k))
+            if not back and ops[n]["t"] > 0.15:
+                soon = [k for k, t in rdy[e].items() if t <= t0 + LOOK * ops[n]["t"] and prio[k] > prio[n] + GAP]
+                if soon:
+                    n = max(soon, key=lambda k: (prio[k], -k))
             o = ops[n]
             end = max(rdy[e].pop(n), t0) + o["t"]
             if e != "X":
@@ -202,12 +215,24 @@ def emit(g, T, ops):
         name = [((o["w"] or o["r"] or [("",)])[0][0], n // 60) for n, o in enumerate(ops)]
         kinds = sorted(set(name))
         prio, seed, best = tail, SEED, (1e9, tail)
-        for it in range(BLEND):
-            s, sq, en = plan(prio, False)
-            if s < best[0]:
-                best = (s, prio)
-            b = plan(en, True)[2]
-            prio = [0.7 * x + 0.3 * y for x, y in zip(prio, b)]
+        for w in ALPHA:
+            prio = best[1]
+            for it in range(BLEND):
+                s, sq, en = plan(prio, False)
+                if s < best[0]:
+                    best = (s, prio)
+                b = plan(en, True)[2]
+                prio = [(1 - w) * x + w * y for x, y in zip(prio, b)]
+        for names in ([o["tag"] for o in ops], name, [o["tag"] for o in ops]):
+            for sweep in range(SWEEPS):
+                for k in sorted(set(names)):
+                    for d in (-4.0, -1.2, 1.2, 4.0):
+                        cand = [p + (d if x == k else 0.0) for p, x in zip(best[1], names)]
+                        s = plan(cand, False)[0]
+                        if s < best[0] - 0.01:
+                            best = (s, cand)
+                if names is name:
+                    break
         span, prio = best
         for it in range(PASSES):
             bump = {}
@@ -272,6 +297,8 @@ def emit(g, T, ops):
 
 def build(g, core, rank, T, topo, rel, ops):
     V, SC, PE = g.vector, g.scalar, g.tensor
+    tag = ["a"]
+    turn = places(rank, rel)
 
     def a(nm, *ix, part=slice(None), tag=None):
         shape = SCRATCH[nm][1][1:]
@@ -297,8 +324,9 @@ def build(g, core, rank, T, topo, rel, ops):
         for x in outs:
             w += x["reg"]
             r += x.get("off", [])
+        t = t * PEF + ADDP if e == "P" else t + (ADD if e in "VS" else 0.0)
         ops.append({"e": e, "fn": fn, "r": r, "w": w, "sem": sem, "inc": inc, "t": t, "lat": lat, "mb": mb,
-                    "after": list(after), "key": len(ops)})
+                    "after": list(after), "key": len(ops), "tag": tag[0] + e})
         return len(ops) - 1
 
     ap = lambda x: x["ap"] if isinstance(x, dict) else x
@@ -375,10 +403,11 @@ def build(g, core, rank, T, topo, rel, ops):
                 d = T.cores[o]
                 rid, pid = topo.addr(d, core)
                 calls.append(add("G", lambda o=o, d=d, rid=rid, pid=pid: g.remote_dma(
-                    landing(T, m, rank), piece(o)["ap"], T.sem["a" + m], T.sem.sent, pid, rid, topo.mask(core, d)),
+                    landing(T, m, rank, o, rel), piece(o)["ap"], T.sem["b" + m], T.sem.sent, pid, rid, topo.mask(core, d)),
                     [], [piece(o)], 0.5, sem="sent", inc=len(topo.engines(core, d)), after=calls[:1]))
-        tot = sum(len(topo.engines(rel.get((q, rank), T.cores[q]), core)) for q in range(NR) if q != rank)
-        add("X", None, [land(q) for q in range(NR) if q != rank], [], HOP, sem="a" + m, inc=tot, after=calls)
+                add("X", None, [land(o)], [], HOP / 2, sem="b" + m, inc=len(topo.engines(d, core)), after=calls)
+        tot = sum(len(topo.engines(rel[(q, rank)], core)) for q in via)
+        add("X", None, [land(q) for q in via], [], HOP + 0.5, sem="a" + m, inc=tot, after=calls[:1])
         return calls
 
     def send_one(m, o, piece, land):
@@ -390,7 +419,7 @@ def build(g, core, rank, T, topo, rel, ops):
             es = topo.engines(core, d)[::-1][w * via.index(o):w * via.index(o) + w]
             dst, sem = slot(T, m), T.sem["h" + m]
         else:
-            es, dst, sem = topo.engines(core, d), landing(T, m, rank), T.sem["a" + m]
+            es, dst, sem = topo.engines(core, d), landing(T, m, rank, o, rel), T.sem["a" + m]
         k = add("G", lambda: g.remote_dma(dst, piece["ap"], sem, T.sem.sent, pid, rid, bits(es)), [], [piece], 0.5,
                 sem="sent", inc=len(es))
         add("X", None, [land], [], HOP + 0.5 if o in via else HOP / 2, sem="a" + m,
@@ -454,6 +483,7 @@ def build(g, core, rank, T, topo, rel, ops):
     cp(c2("xp", 0, S), a("x0i"))
 
     def source(r):
+        tag[0] = "s%d" % r
         px, pslot = c2("pH", 0, S), c2("pH", 256, 266)
         old = c2("xp", S * r, S * r + S)
         if r == 0:
@@ -496,12 +526,14 @@ def build(g, core, rank, T, topo, rel, ops):
         base = NR * S * r
         cp(ind(c2("xw", base, base + NR * S), sl), new)
         piece = lambda o: c2("xw", base + S * o, base + S * o + CAP)
-        land = lambda q: a("xl", slice(8 * r + 2 * q, 8 * r + 2 * q + 2))
+        land = lambda q: a("xl", slice(8 * r + 2 * turn.index(q), 8 * r + 2 * turn.index(q) + 2))
         act(land(rank), piece(rank))
         return send("x%d" % r, piece, land, [c2("yr", base, base + NR * S)])
 
     sent0 = source(0)
-    iota(c2("jj", 0, 256), [[1, 16], [0, 16]], 0, 0, after=sent0)
+    tag[0] = "b"
+    iota(c2("jj", 0, 128), [[0, 16 // LB], [1, 8], [0, LB]], 0, 0, after=sent0)
+    iota(c2("jj", 128, 136), [[LB, 16 // LB], [0, LB // 2]], 0, 0, after=sent0)
     iota(c2("dmp", 0, 16), [[0, 8], [16, 2]], DC, 0, after=sent0)
     for lo in range(0, WT, WT // 8):
         iota(c2("iot", lo, lo + WT // 8), [[1, WT // 8]], lo, 0, after=sent0)
@@ -597,7 +629,9 @@ def build(g, core, rank, T, topo, rel, ops):
     act(a("zz", 1), a("zz", 0), scale=8192.0)
     act(a("zz", 2), a("zz", 0), scale=eye(E1, 0))
     ts(c2("dmp", 0, 16), c2("dmp", 0, 16), col("p16"), Op.add)
-    ts(a("lx"), one(16), col("p16"), Op.mult)
+    ts(pi(7), pi(0), LB - 1, Op.bitwise_and)
+    cp(col("p4"), pi(7))
+    ts(c2("lx", 0, 8), c2("jj", 128, 136), col("p4"), Op.add)
     cp(c2("ld", 0, 16), c2("io_", 0, 16))
     cp(c2("ld", 16, 24), c2("io_", 0, 16, 2))
     mset(c2("ctab", WC, WT), 0.0)
@@ -605,6 +639,7 @@ def build(g, core, rank, T, topo, rel, ops):
     ts(c2("dmp", 16, 32), c2("dmp", 0, 16), float(DF - DC), Op.add)
 
     def late():
+        tag[0] = "l"
         ts(a("tri"), c2("io_", 0, 16), col("p16"), Op.is_gt)
         ts(col("jp1"), col("p16"), 1.0, Op.add)
         ts(col("eb"), col("p16"), -LN4, Op.mult)
@@ -637,7 +672,8 @@ def build(g, core, rank, T, topo, rel, ops):
                 lo = NR * S * r + S * o
                 act(c2("xw", lo, lo + CAP), c2("one", 0, CAP), scale=col("tm"))
 
-    mset(c2("yr", NR * S, RO * NR * S), 0.0)
+    for lo in range(NR * S, RO * NR * S, 2 * S):
+        mset(c2("yr", lo, lo + 2 * S), 0.0)
     late()
 
     half = lambda nm, h: a(nm, slice(8 * h, 8 * h + 8))
@@ -647,113 +683,123 @@ def build(g, core, rank, T, topo, rel, ops):
     tmp = lambda i: c2("tmp", 16 * i, 16 * i + 16)
 
     def index(r):
-        X = a("xl", slice(8 * r, 8 * r + 8))
-
-        def swapped(nm, h0, m):
-            for g2 in range(2):
-                out = a(nm, slice(8 * h0, 8 * h0 + 8), slice(16 * g2, 16 * g2 + 16))
-                mm(out, [(a("ea", 2 * m + g2, slice(16 - 16 * (h - g2), 144 - 16 * (h - g2))),
-                          a("xl", slice(8 * r, 8 * r + 8), slice(16 * h, 16 * h + 16))) for h in range(2)])
-        swapped("pB", 0, 1)
-        swapped("pA", 0, 0)
-        swapped("pA", 1, 2)
-        act(c2("va", 0, 256), half("pB", 0), scale=2.0, bias=col("bva"))
-        mm(half("pB", 1), [(ed("VB"), X)])
-        mm(c2("pD", 256, 512), [(eg("VW"), X)])
-        mm(c2("pD", 0, 256), [(eg("UW"), X)])
-        mm(c2("pC", 0, 256), [(eg("UB"), X)])
-        mm(c2("pC", 256, 512), [(eg("LB"), X)])
-        act(c2("va", 256, 512), half("pB", 1), scale=2.0, bias=col("bvb"))
-        act(c2("va", 512, 768), c2("pD", 256, 512), scale=col("sw"), bias=col("bw"))
-        tt(a("ra"), half("pA", 0), c2("va", 0, 256), Op.mult)
-        tt(a("tsw"), half("pA", 1), a("ra"), Op.add)
-        add("V", lambda: V.transpose(T.tw[:], T.tsw[:]), [a("tw")], [a("tsw")], 256 * CY)
         al = slice(None)
-        ts(a("ti"), a("tw", al, slice(0, 5)), 2, Op.logical_shift_right, WC - 1, Op.bitwise_and)
-        tt(a("wq"), c2("pD", 0, 256), c2("va", 512, 768), Op.mult)
-        for kk in range(4):
-            cp(c2("of1", 16 * kk, 16 * kk + 16), a("ti", al, kk))
-        for h in range(2):
-            (act, cp if VM else act)[h](c2("mg", 512 * h, 512 * h + 512), ind(mwin, c2("of1", 32 * h, 32 * h + 32)))
-        for s in range(4):
-            mm(c2("pG" if s < 2 else "pH", 256 * (s % 2), 256 * (s % 2) + 256), [(ed("REP%d" % (4 + s)), a("wq"))])
-        for h, nm in enumerate(("pE", "pF")):
+
+        def front(u):
+            tag[0] = "i%d%d" % (r, u)
+            X = a("xl", slice(8 * r + 4 * u, 8 * r + 4 * u + 4))
+            p3 = lambda nm, h0: a(nm, slice(8 * h0 + 4 * u, 8 * h0 + 4 * u + 4))
+            h2 = lambda nm, k=0: c2(nm, 256 * k + 128 * u, 256 * k + 128 * u + 128)
+
+            def swapped(nm, h0, m):
+                for g2 in range(2):
+                    out = a(nm, slice(8 * h0 + 4 * u, 8 * h0 + 4 * u + 4), slice(16 * g2, 16 * g2 + 16))
+                    mm(out, [(a("ea", 2 * m + g2, slice(16 - 16 * (h - g2), 144 - 16 * (h - g2))),
+                              a("xl", slice(8 * r + 4 * u, 8 * r + 4 * u + 4), slice(16 * h, 16 * h + 16))) for h in range(2)])
+            swapped("pB", 0, 1)
+            swapped("pA", 0, 0)
+            swapped("pA", 1, 2)
+            act(h2("va"), p3("pB", 0), scale=2.0, bias=col("bva"))
+            mm(h2("pD", 1), [(eg("VW"), X)])
+            mm(h2("pD"), [(eg("UW"), X)])
+            mm(h2("pC"), [(eg("UB"), X)])
+            mm(h2("pC", 1), [(eg("LB"), X)])
+            mm(p3("pB", 1), [(ed("VB"), X)])
+            act(h2("va", 2), h2("pD", 1), scale=col("sw"), bias=col("bw"))
+            act(h2("va", 1), p3("pB", 1), scale=2.0, bias=col("bvb"))
+            tt(h2("ra"), p3("pA", 0), h2("va"), Op.mult)
+            tt(h2("tsw"), p3("pA", 1), h2("ra"), Op.add)
+            lb = slice(8 * u, 8 * u + 8)
+            o, i = a("tw", lb), h2("tsw")
+            add("V", lambda: V.transpose(o["ap"], i["ap"]), [o], [i], 128 * CY)
+            ts(a("ti", lb), a("tw", lb, slice(0, 5)), 2, Op.logical_shift_right, WC - 1, Op.bitwise_and)
             for kk in range(4):
-                mm(c2(nm, 128 * kk, 128 * kk + 128), [(ed("REP%d" % kk), c2("wq", 128 * h, 128 * h + 128))])
-        tt(a("rbb"), c2("pC", 0, 256), c2("va", 256, 512), Op.mult)
+                cp(c2("of1", 32 * u + 8 * kk, 32 * u + 8 * kk + 8), a("ti", lb, kk))
+            tt(h2("wq"), h2("pD"), h2("va", 2), Op.mult)
+            tt(h2("rbb"), h2("pC"), h2("va", 1), Op.mult)
+            tt(h2("tb"), h2("pC", 1), h2("rbb"), Op.add)
+            ts(h2("tb2"), h2("tb"), 1008, Op.bitwise_and)
+            cp(h2("b16"), h2("tb2"))
+
+        def rest(u):
+            tag[0] = "j%d%d" % (r, u)
+            h2 = lambda nm: c2(nm, 128 * u, 128 * u + 128)
+            for s in range(4):
+                mm(c2(("pG", "pH")[u], 128 * s, 128 * s + 128), [(ed("REP%d" % (4 + s)), h2("wq"))])
+                mm(c2(("pE", "pF")[u], 128 * s, 128 * s + 128), [(ed("REP%d" % s), h2("wq"))])
+            act(a("wcd", u), a(("pG", "pH")[u]))
+            for h in range(2):
+                o = 512 * u + 256 * h
+                (act, cp if VM > u else act)[h](c2("mg", o, o + 256), ind(mwin, c2("of1", o // 16, o // 16 + 16)))
+            po = a("pB", slice(8 + 4 * u, 12 + 4 * u))
+            mm(po, [(ed("I"), h2("b16"))]
+               + [(eg("S%d" % kk), c2("mg", 512 * u + 128 * kk, 512 * u + 128 * kk + 128)) for kk in range(4)])
+            cp(h2("of2"), po)
+
+        front(1)
+        front(0)
+        rest(0)
+        rest(1)
+        tag[0] = "k%d" % r
         tt(tmp(0), a("ti", al, 4), a("tw", al, 7), Op.add)
-        tt(a("tb"), c2("pC", 256, 512), a("rbb"), Op.add)
         tt(kw(r, 0, 16), tmp(0), c2("dmp", 0, 16), Op.min)
-        ts(a("tb2"), a("tb"), 1008, Op.bitwise_and)
         cp(lk(r, 0, 16), kw(r, 0, 16))
-        cp(a("b16"), a("tb2"))
-        po = half("pB", 1)
-        mm(po, [(eg("S%d" % kk), c2("mg", 256 * kk, 256 * kk + 256)) for kk in range(4)] + [(ed("I"), a("b16"))])
-        act(a("wcd", slice(0, 2)), a("pG"))
-        act(a("wcd", slice(2, 4)), a("pH"))
         cp(lk(r, 16, 24), kw(r, 1, 16, 2))
         ts(a("bw"), a("tw", al, 5), 1008, Op.bitwise_and)
         cp(a("sid"), a("tw", al, 6))
-        cp(a("of2"), po)
 
     def value(r):
         al = slice(None)
         yb = lambda lo, hi: c2("yb", 256 * r + lo, 256 * r + hi)
         base = NR * S * r
         land = lambda q: c2("yr", base + S * q, base + S * q + CAP)
-        turn = sorted(range(NR), key=lambda q: (q == rank, (rank, q) not in rel))
-        for i, c in enumerate(turn):
-            lo, hi = 64 * c, 64 * c + 64
+        for i in range(NR):
+            lo, hi = 64 * i, 64 * i + 64
             if i == 0 and VL:
                 ts(c2("vv", 16 * lo, 16 * (lo + VL)), ind(ftw, c2("of2", lo, lo + VL)), -128.0, Op.add)
                 lo += VL
             if hi > lo:
                 act(c2("vv", 16 * lo, 16 * hi), ind(ftw, c2("of2", lo, hi)), bias=-128.0)
-        for i, c in enumerate(turn):
-            lo, sums, py = 64 * c, ("pC", "pD")[i % 2], c2(("pG", "pH")[i % 2], 0, 64)
-            pp = lambda k: c2("pp", 16 * lo + 64 * k, 16 * lo + 64 * k + 64)
+        for i, (lo, n) in enumerate(PC):
+            u, sums, py = lo // 128, ("pC", "pD")[i % 2], c2(("pG", "pH")[i % 2], 0, n)
+            pp = lambda k: c2("pp", 16 * lo + n * k, 16 * lo + n * k + n)
             for s in range(4):
                 for kk in range(4):
                     o = 128 * kk + lo % 128
-                    tt(pp(4 * s + kk), c2("vv", 16 * lo + 4 * s + kk, 16 * lo + 1024, 16), c2(("pE", "pF")[c // 2], o, o + 64), Op.mult)
-                mm(c2(sums, 64 * s, 64 * s + 64), [(a("i16"), pp(4 * s + kk)) for kk in range(4)])
-            tt(c2("qq", 4 * lo, 4 * lo + 256), c2(sums, 0, 256), a("wcd", al, slice(lo, lo + 64)), Op.mult)
-            mm(py, [(ed("CY"), a("xl", slice(8 * r + 2 * c, 8 * r + 2 * c + 2)))]
-               + [(a("i32"), c2("qq", 4 * lo + 64 * s, 4 * lo + 64 * s + 64)) for s in range(4)])
-            ts(yb(lo, lo + 64), py, MAGIC + 128.0, Op.add, MAGIC, Op.subtract)
-            if c == rank:
-                cp(land(c), yb(lo, lo + 64))
-            else:
-                send_one("y%d" % r, c, yb(lo, lo + 64), land(c))
+                    tt(pp(4 * s + kk), c2("vv", 16 * lo + 4 * s + kk, 16 * (lo + n), 16), c2(("pE", "pF")[u], o, o + n), Op.mult)
+                mm(c2(sums, n * s, n * s + n), [(a("i16"), pp(4 * s + kk)) for kk in range(4)])
+            tt(c2("qq", 4 * lo, 4 * lo + 4 * n), c2(sums, 0, 4 * n), a("wcd", u, al, slice(lo % 128, lo % 128 + n)), Op.mult)
+            mm(py, [(ed("CY"), a("xl", slice(8 * r + lo // 32, 8 * r + (lo + n) // 32)))]
+               + [(a("i32"), c2("qq", 4 * lo + n * s, 4 * lo + n * s + n)) for s in range(4)])
+            ts(yb(lo, lo + n), py, MAGIC + 128.0, Op.add, MAGIC, Op.subtract)
+            for c in range(lo // 64, (lo + n) // 64):
+                if turn[c] == rank:
+                    cp(land(rank), yb(64 * c, 64 * c + 64))
+                else:
+                    send_one("y%d" % r, turn[c], yb(64 * c, 64 * c + 64), land(turn[c]))
 
     def dedupe(r, t):
         key = kw(r, 16 * t, 16 * t + 16)
         act(c2("kr", 384 * t, 384 * t + 384), ind(a("iot"), lk(r, 24 * t, 24 * t + 24)))
-        eq = lambda lo, hi, st=1: c2("eq", 384 * t + lo, 384 * t + hi, st)
-        tt(eq(0, 384), ind(key, a("ld")), c2("kr", 384 * t, 384 * t + 384), Op.is_equal)
-        bank = lambda lo, st: c2("pG", lo, 16, st) if t else a("pB", 1, slice(lo, 16, st))
+        tt(a("eq", t), ind(key, a("ld")), c2("kr", 384 * t, 384 * t + 384), Op.is_equal)
+        if t == 0:
+            return
+        al = slice(None)
         for k in range(16):
-            mm1(bank(0, 1), a("et", k), eq(k, 256, 16), k == 0, False)
+            mm1(c2("pG", 0, 32), a("et", k), a("eq", al, slice(k, 256, 16)), k == 0, False)
         for k in range(16):
-            mm1(bank(1, 2), zv(1, k), eq(256 + k, 384, 16), False, k == 15)
-        t1, t2 = tmp(3 + 2 * t), tmp(4 + 2 * t)
-        tt(t1, bank(0, 1), key, Op.add)
-        tt(t2, t1, c2("dmp", 16 * t, 16 * t + 16), Op.min)
-        cp(c2("lo", 32 * r + 16 * t, 32 * r + 16 * t + 16), t2)
+            mm1(c2("pG", 1, 32, 2), zv(1, k), a("eq", al, slice(256 + k, 384, 16)), False, k == 15)
+        t1, t2 = c2("tmp", 48, 80), c2("tmp", 80, 112)
+        tt(t1, c2("pG", 0, 32), kw(r, 0, 32), Op.add)
+        tt(t2, t1, a("dmp"), Op.min)
+        cp(c2("lo", 32 * r, 32 * r + 32), t2)
 
     def early(r):
         al = slice(None)
         act(a("ms"), ind(mwin, lk(r, 0, 16)))
-        mm(a("pB", 0, slice(0, 16)), [(zv(2, k), c2("ms", k, 256, 16)) for k in range(16)])
         tt(tmp(1), a("bw"), a("tw", al, 7), Op.add)
-        tt(tmp(2), a("pB", 0, slice(0, 16)), tmp(1), Op.add)
-        tt(kw(r, 16, 32), tmp(2), c2("dmp", 16, 32), Op.min)
-        cp(lk(r, 24, 40), kw(r, 16, 32))
-        cp(lk(r, 40, 48), kw(r, 17, 32, 2))
-        dedupe(r, 0)
-        for q in range(NR):
-            act(c2("tgl", CAP * q, CAP * q + CAP), ind(c2("ta", S * q, S * q + S), c2("sid", 4 * q, 4 * q + 4)))
-        act(a("fg"), ind(ftw, lk(r, 24, 40)))
+        for i, q in enumerate(turn):
+            act(c2("tgl", CAP * i, CAP * i + CAP), ind(c2("ta", S * q, S * q + S), c2("sid", 4 * i, 4 * i + 4)))
         act(c2("cg", 256 * r, 256 * r + 256), ind(a("ctab"), lk(r, 0, 16)))
         if PACK:
             mm(a("pA"), [(ed("I"), c2("ftab", 0, FC, 2)), (ed("I4"), c2("ftab", 1, FC, 2))])
@@ -761,50 +807,51 @@ def build(g, core, rank, T, topo, rel, ops):
             ts(a("bw8"), a("tw", al, 5), 1, Op.logical_shift_right, 504, Op.bitwise_and)
             tt(c2("ofu", 0, 128), ind(a("bw8"), c2("lx", 0, 8)), c2("jj", 0, 128), Op.add)
             cp(c2("ou", 0, 128), c2("ofu", 0, 128))
-            for i in range(4):
+            for i in range(NR):
                 act(c2("v3", 512 * i, 512 * i + 512), ind(a("f2"), c2("ou", 32 * i, 32 * i + 32)))
-        else:
-            tt(a("ofu"), ind(a("bw"), a("lx")), a("jj"), Op.add)
-            cp(a("ou"), a("ofu"))
-            for i in range((16 - VJ) // 2):
-                act(c2("v2", 512 * i, 512 * i + 512), ind(ftw, c2("ou", 32 * i, 32 * i + 32)))
 
     def train(r):
         last = r == RO - 1
-        pg, pu = c2("pE", 0, 256), c2("pF", 0, 256)
+        pg, pu = c2("pE", 256, 512), half("pB", 0)
         cg, uu = c2("cg", 256 * r, 256 * r + 256), c2("uu", 256 * r, 256 * r + 256)
-        mm(half("pA", 0), [(ed("I"), a("tgl")), (ed("NI"), c2("yb", 256 * r, 256 * r + 256))])
-        act(pg, half("pA", 0), AF.Sign)
+        n, w = 16 * LB, LB // 2
+        for c in range(16 // LB):
+            lo, d, sg = n * c, a("pA", slice(w * c, w * c + w)), a("pA", slice(8 + w * c, 8 + w * c + w))
+            mm(d, [(ed("I"), c2("tgl", lo, lo + n)), (ed("NI"), c2("yb", 256 * r + lo, 256 * r + lo + n))])
+            act(sg, d, AF.Sign)
+            for j in range(8):
+                o = 8 * lo + n * j
+                tt(c2("gw", o, o + n), c2("v3", o, o + n), sg, Op.mult)
+                mm1(a("pB", slice(w * c, w * c + w)), c2("z2", 14 - 2 * j, 142 - 2 * j), c2("gw", o, o + n), j == 0, j == 7)
         act(a("gs"), half("pA", 0), AF.Sign)
+        al = slice(None)
+        tag[0] = "d%d" % r
+        mm(c2("pE", 0, 16), [(zv(2, k), c2("ms", k, 256, 16)) for k in range(16)])
+        tt(tmp(2), c2("pE", 0, 16), tmp(1), Op.add)
+        tt(kw(r, 16, 32), tmp(2), c2("dmp", 16, 32), Op.min)
+        cp(lk(r, 24, 40), kw(r, 16, 32))
+        cp(lk(r, 40, 48), kw(r, 17, 32, 2))
+        act(a("fg"), ind(ftw, lk(r, 24, 40)))
+        dedupe(r, 0)
         dedupe(r, 1)
         mm(c2("pG", 256, 512), [(ed("I"), a("fg")), (ed("I"), a("gs"))])
         ts(a("fn"), c2("pG", 256, 512), 0.0, Op.max, 255.0, Op.min)
-        if PACK:
-            for j in range(8):
-                gv = c2("gw", 256 * j, 256 * j + 256)
-                tt(gv, c2("v3", 256 * j, 256 * j + 256), pg, Op.mult)
-                mm1(pu, c2("z2", 14 - 2 * j, 142 - 2 * j), gv, j == 0, j == 7)
-            ts(a("hi"), pu, MAGIC, Op.add, MAGIC, Op.subtract)
-            act(a("zc"), pu, scale=col("ev"))
-            pu = c2("pE", 256, 512)
-            mm(pu, [(ed("GW"), a("gs")), (a("d16"), a("hi")), (a("i32"), a("zc"))])
-        else:
-            for n, j in enumerate(list(range(16 - VJ)) + list(range(16 - VJ, 16))):
-                gv = c2("gv", 256 * j, 256 * j + 256)
-                if j < 16 - VJ:
-                    tt(gv, c2("v2", 256 * j, 256 * j + 256), pg, Op.mult)
-                else:
-                    tt(gv, ind(ftw, c2("ou", 16 * j, 16 * j + 16)), a("gs"), Op.mult)
-                mm1(pu, zv(0, j), gv, n == 0, n == 15)
+        tag[0] = "u%d" % r
+        act(a("zc"), pu, scale=col("ev"))
+        ts(a("hi"), pu, MAGIC, Op.add, MAGIC, Op.subtract)
+        pu = c2("pF", 0, 256)
+        mm(pu, [(ed("GW"), a("gs")), (a("i32"), a("zc")), (a("d16"), a("hi"))])
         act(uu, pu, AF.Sign)
 
         def scat(win, t, fn):
-            for k in range(7, -1, -1):
+            tag[0] = "w%d%s" % (r, win["reg"][0][0])
+            for k in [2 * turn.index(q) + z for q in range(NR - 1, -1, -1) for z in (1, 0)]:
                 o = 32 * r + 16 * t + 2 * k
                 fn(ind(win, c2("lo", o, o + 2)), 32 * k, 32 * k + 32)
         scat(ftw, 1, lambda w, lo, hi: cp(w, c2("fn", lo, hi)))
         scat(a("ctab"), 0, lambda w, lo, hi: tt(w, c2("cg", 256 * r + lo, 256 * r + hi), c2("uu", 256 * r + lo, 256 * r + hi), Op.add))
         source(r + 1)
+        tag[0] = "m%d" % r
         if last:
             dma("S", T.yf[:], c2("ftab", 0, FC), mb=0.26)
             mm(c2("pC", 0, 256), [(zv(3, q), c2("ctab", 256 * q, 256 * q + 256)) for q in range(16)])
@@ -824,7 +871,6 @@ def build(g, core, rank, T, topo, rel, ops):
             dma("SYS"[s - 1], mrow(s, PAD + WC - sh, PAD + WC), mrow(0, PAD, PAD + sh), new=False, mb=0.0)
 
     for r in range(RO):
-        index(r)
-        early(r)
-        value(r)
-        train(r)
+        for k, f in enumerate((index, early, value, train)):
+            tag[0] = "p%d%d" % (k, r)
+            f(r)

@@ -5,59 +5,60 @@ from concourse.mybir import AluOpType as Op, ActivationFunctionType as AF
 S, CAP, WC, FC, RO, NR = 160, 64, 4096, 1024, 3, 4
 SHIFTS = (0, 47, 229, 276)
 PAD = 288
-DC, DF = 4400, 1024
+FX = 768
+DC, DF = WC, FC + FX
 WT = DC + 32
 MAGIC = 12582912.0
 LN4 = math.log(4.0)
-VL = 64
-PACK = True
-VM = 1
-VJ = 2
-CY, WAKE, SLACK, HOP = 0.9e-3, 0.2, 0.02, 5.5
-ALPHA, SWEEPS, LOOK, GAP = (0.3, 0.15), 1, 0.8, 1.5
-ADD, ADDP, PEF = 0.03, 0.0, 1.3
-LB = 8
-PC = ((0, 128), (128, 64), (192, 64))
-PASSES, BLEND, SEED, SPAN, PRIO = 0, 30, 1, [0.0], {}
+VL = ((((64, 0),), ((64, 16),), ((64, 16),), ((64, 0),)),) * 2
+VM = (0, 1, 0, 0)
+TQ = "S"
+VJ = (0, 0)
+CY, WAKE, GAT, SCA, HOP = 0.85e-3, 0.25, 1.45, 3.6, 4.8
+MARK, EF = (), {}
+SEED, HEAT, MU, LOG, FB, STEP, BACK = 1, 0.15, 1.0, [], 2, 6.0, 50
+ADD, ADDP, PEF = 0.0, 0.0, 0.75
+BLEND, SPAN, PRIO, WAW, CH, MS, MZ = 4000, [0.0], {}, True, 32, 2, 4
 
 sb = lambda shape, d: ("sbuf", shape, d)
 ps = lambda shape: ("psum", shape, "float32")
 B, F, I, U, H = "bfloat16", "float32", "int32", "uint16", "float16"
 SCRATCH = {
-    "mt": sb([128, PAD + WT], B), "ctab": sb([128, WT], B), "ftab": sb([128, FC + 32], B),
-    "ta": sb([128, NR * S], B), "xw": sb([128, RO * NR * S], B), "xl": sb([128, RO * 8, 32], B),
+    "mt": sb([128, PAD + WT], B), "ct": sb([128, WC], B), "ctab": sb([128, WC], B), "ftab": sb([128, DF + 32], B),
+    "ycw": sb([128, WT], F),
+    "ta": sb([128, NR * S], B), "xw": sb([128, RO * NR * S], B), "xl": sb([128, RO * 256], B),
     "yr": sb([128, RO * NR * S], B), "yb": sb([128, RO * 256], B), "rb": sb([128, S + 2 * RO * CAP], B),
-    "iot": sb([128, WT], F), "io_": sb([128, S], F), "pint": sb([128, 8], I), "g16": sb([128, 128], B),
-    "r4": sb([128, 128], B), "cc": sb([128, 32], F), "pa": sb([128, 16], F), "eye": sb([128, 10, 16], F),
-    "gm": sb([128, 8], F), "one": sb([128, S], B), "tri": sb([128, 16], F),
-    "ka": sb([128, 3, 16], B), "kg": sb([128, 10, 16], B), "ea": sb([128, 6, 160], B), "eg": sb([128, 10, 128], B),
-    "ed": sb([128, 20, 128], B), "et": sb([128, 16, 128], B), "zz": sb([128, 4, 144], B), "z16": sb([128, 144], H),
-    "i16": sb([128, 128], H), "i32": sb([128, 128], F),
-    "dmp": sb([128, 32], F), "jj": sb([128, 256], F), "lx": sb([128, 16], U), "ld": sb([128, 24], U),
+    "io_": sb([128, S], F), "pint": sb([128, 16], I), "g16": sb([128, 128], B),
+    "r4": sb([128, 128], B), "cc": sb([128, 64], F), "pa": sb([128, 16], F), "eye": sb([128, 4, 16], F),
+    "gm": sb([128, 8], F), "one": sb([128, 256], B), "tri": sb([128, 16], F), "kc": sb([128, 2, 256], B),
+    "kz": sb([128, 9, 4], B), "zk": sb([128, 9, 140], B), "kw": sb([128, 5, 4], B), "zw": sb([128, 5, 140], B),
+    "kg": sb([128, 18, 16], B), "eg": sb([128, 18, 128], B), "pk": sb([128, 16, 16], B), "rk": sb([128, 16, 128], B), "rp": sb([128, 16, 128], B),
+    "ed": sb([128, 21, 128], B), "et": sb([128, 16, 128], B), "zz": sb([128, 5, 144], B), "z16": sb([128, 144], B),
+    "i32": sb([128, 128], F), "q4": sb([128, 64], I),
+    "dmp": sb([128, 32], F), "cst": sb([128, 96], B),
     "x0i": sb([128, S], I), "xp": sb([128, (RO + 1) * S], B), "xq": sb([128, S], B), "clp": sb([128, S], B),
-    "xa": sb([128, S], I), "xi": sb([128, S], I), "oh": sb([128, S], I), "hh": sb([128, S], H), "cum": sb([128, S], H),
+    "th": sb([128, S], B), "cum": sb([128, S], H),
     "prd": sb([128, S], H), "wt": sb([128, S], B), "sl": sb([128, RO * 16], U), "acc": sb([128, RO * S], F),
     "xf": sb([128, S], F),
     "mx": sb([128, 512], F), "ki": sb([128, 256], I), "k2": sb([128, 512], I), "mq": sb([128, 512], B),
-    "va": sb([128, 768], F), "ra": sb([128, 256], F), "tsw": sb([128, 256], I), "tw": sb([128, 16, 16], I),
-    "ti": sb([128, 16, 5], I), "of1": sb([128, 64], U), "rbb": sb([128, 256], F), "tb": sb([128, 256], I),
-    "tb2": sb([128, 256], I), "b16": sb([128, 256], B), "wq": sb([128, 256], B), "wcd": sb([128, 2, 4, 128], B),
+    "va": sb([128, 448], F), "ra": sb([128, 192], F), "tsw": sb([128, 192], I), "ti": sb([128, 256], I),
+    "of1": sb([128, 64], U), "b0": sb([128, 64], B), "st": sb([128, 128], H),
+    "wq": sb([128, 256], B), "wcd": sb([128, 1024], B),
     "mg": sb([128, 1024], B), "ms": sb([128, 256], B), "of2": sb([128, 256], U),
-    "vv": sb([128, 4096], B), "pp": sb([128, 4096], H), "qq": sb([128, 1024], F),
-    "tmp": sb([128, 112], F), "kw": sb([128, RO * 32], F), "lk": sb([128, RO * 48], U), "bw": sb([128, 16], I),
-    "ofu": sb([128, 256], F), "ou": sb([128, 256], U), "sid": sb([128, 16], U), "tgl": sb([128, 256], B),
-    "kr": sb([128, 768], F), "eq": sb([128, 2, 384], B), "lo": sb([128, RO * 32], U),
-    "v2": sb([128, 4096], B), "gv": sb([128, 4096], B), "gs": sb([128, 256], B), "uu": sb([128, RO * 256], B),
-    "f2": sb([128, 512], F), "v3": sb([128, 2048], F), "gw": sb([128, 2048], F), "bw8": sb([128, 16], I),
-    "hi": sb([128, 256], H), "zc": sb([128, 256], F), "z2": sb([128, 144], F), "d16": sb([128, 128], H),
-    "cg": sb([128, RO * 256], B), "fg": sb([128, 256], B), "fn": sb([128, 256], B), "ee": sb([128, 256], B),
-    "ohm": sb([128, 256], B), "mn": sb([128, 256], B), "yo": sb([128, 256], F),
-    "pA": ps([128, 16, 32]), "pB": ps([128, 16, 32]), "pC": ps([128, 512]), "pD": ps([128, 512]),
+    "vv": sb([128, 4096], B), "pp": sb([128, 256, 16], H), "qq": sb([128, 1024], F),
+    "tmp": sb([128, 32], F), "lk": sb([128, RO * 80], U), "kh": sb([128, 3, 16], H),
+    "tgl": sb([128, 256], B), "eq": sb([128, 768], B), "lo": sb([128, RO * 64], U),
+    "gs": sb([128, 256], B), "uu": sb([128, 256], B), "su": sb([128, 256], B),
+    "f2": sb([128, 512], F), "v3": sb([128, 2048], F), "gw": sb([128, 2048], F),
+    "zc": sb([128, 256], F), "gq": sb([128, 8], F),
+    "cg": sb([128, 256], B), "fg": sb([128, 256], B), "fn": sb([128, 256], B), "ee": sb([128, 256], B),
+    "ohm": sb([128, 256], B), "mn": sb([128, 256], B), "yo": sb([128, 512], F), "yg": sb([128, 512], F),
+    "pA": ps([128, 512]), "pB": ps([128, 512]), "pC": ps([128, 512]), "pD": ps([128, 512]),
     "pE": ps([128, 512]), "pF": ps([128, 512]), "pG": ps([128, 512]), "pH": ps([128, 512]),
 }
 MSGS = ["tg"] + [k + str(r) for r in range(RO) for k in "xy"]
 SEMAPHORES = (["cV", "cS", "cP", "cG", "sent"] + ["a" + m for m in MSGS] + ["h" + m for m in MSGS]
-              + ["b" + m for m in MSGS if m[0] != "y"] + ["d%d" % i for i in range(40)])
+              + ["b" + m for m in MSGS if m[0] != "y"] + ["d%d" % i for i in range(44)])
 
 
 def relays(T, topo):
@@ -86,8 +87,8 @@ def landing(T, m, q, o, rel):
         return T.ta[:, S * q:S * q + S]
     r = int(m[1])
     if m[0] == "x":
-        i = places(o, rel).index(q)
-        return T.xl[:, 8 * r + 2 * i:8 * r + 2 * i + 2, :]
+        i = 256 * r + CAP * places(o, rel).index(q)
+        return T.xl[:, i:i + CAP]
     return T.yr[:, NR * S * r + S * q:NR * S * r + S * q + CAP]
 
 
@@ -116,10 +117,10 @@ def rank_program(g, core, T, topo):
         return
     ops = []
     build(g, core, rank, T, topo, rel, ops)
-    emit(g, T, ops)
+    emit(g, T, ops, rank)
 
 
-def emit(g, T, ops):
+def emit(g, T, ops, rank):
     Q = {"V": g.vector, "S": g.scalar, "P": g.tensor, "G": g, "Y": g.sync}
     hist, group, index = {}, {}, {}
     for n, o in enumerate(ops):
@@ -130,30 +131,23 @@ def emit(g, T, ops):
         e, dep, order = o["e"], set(), set(index[k] for k in o["after"])
         for regs, wr in ((o["r"], False), (o["w"], True)):
             for (nm, lo, hi, tag) in regs:
-                psum = SCRATCH[nm][0] == "psum"
                 for (l2, h2, t2, k, w2) in hist.get(nm, []):
                     p = ops[k]
-                    hit = l2 < hi and lo < h2 and (tag is None or t2 is None or tag == t2) and (wr or w2)
+                    if not (l2 < hi and lo < h2 and (tag is None or t2 is None or tag == t2) and (wr or w2)):
+                        continue
                     if p["e"] == e and p["sem"] is None and o["sem"] is None:
-                        if e == "P":
-                            if psum:
-                                order.add(k)
-                        elif hit:
-                            dep.add(k)
-                    elif p["sem"] is not None and p["sem"] == o["sem"]:
-                        pass
-                    elif psum or hit:
+                        (order if e == "P" or (wr and not WAW) else dep).add(k)
+                    elif p["sem"] is None or p["sem"] != o["sem"]:
                         dep.update([k] if p["sem"] is None else group[p["sem"]])
-        o["dep"], o["ord"] = (set() if e == "X" else dep), order
+        o["dep"], o["ord"] = (set() if e == "X" else dep), order - dep
+        o["banks"] = set(z[0] for z in o["r"] + o["w"] if SCRATCH[z[0]][0] == "psum")
         if o["sem"] == "sent":
             continue
         for regs, wr in ((o["r"], False), (o["w"], True)):
             for (nm, lo, hi, tag) in regs:
-                psum, seen = SCRATCH[nm][0] == "psum", o["dep"] | o["ord"]
-                keep = [z for z in hist.get(nm, []) if not (z[3] in seen and ops[z[3]]["sem"] is None and o["sem"] is None and (
-                    (wr and tag is None and lo <= z[0] and z[1] <= hi and not psum) or (psum and e == "P" and ops[z[3]]["e"] == "P")))]
-                if psum and keep and ops[keep[-1][3]]["e"] != e:
-                    keep = [z for z in keep if ops[z[3]]["e"] == ops[keep[-1][3]]["e"]]
+                seen = o["dep"] | o["ord"]
+                keep = [z for z in hist.get(nm, []) if not (z[3] in seen and ops[z[3]]["sem"] is None and o["sem"] is None
+                                                            and wr and tag is None and lo <= z[0] and z[1] <= hi)]
                 hist[nm] = keep + [(lo, hi, tag, n, wr)]
     succ = [[] for o in ops]
     for n, o in enumerate(ops):
@@ -170,89 +164,138 @@ def emit(g, T, ops):
                 stack.append(k)
     tail = [0.0] * len(ops)
     for n in reversed(topo_order):
-        tail[n] = ops[n]["t"] + ops[n]["lat"] + ops[n]["mb"] * 5.0 + WAKE + max([tail[k] for k in succ[n]] + [0.0])
+        far = ops[n]["lat"] + ops[n]["mb"] * 5.0
+        tail[n] = ops[n]["t"] + max([tail[k] + (far + WAKE if n in ops[k]["dep"] else 0.0) for k in succ[n]] + [far])
     pred = [list(o["dep"] | o["ord"]) for o in ops]
 
     def plan(prio, back):
-        nxt, prv = (pred, succ) if back else (succ, pred)
-        todo = [len(p) for p in prv]
-        at = [(ops[n]["lat"] + ops[n]["mb"] * 5.0 if back else 0.0) for n in range(len(ops))]
-        rdy = {}
-        for n in range(len(ops)):
-            if todo[n] == 0:
-                rdy.setdefault(ops[n]["e"], {})[n] = at[n]
-        free, seq, ends, pipe, span = {}, [], [0.0] * len(ops), 0.0, 0.0
-        while any(rdy.values()):
-            t0, e = min((max(min(d.values()), free.get(q, 0.0)), q) for q, d in rdy.items() if d)
-            n = max((k for k, t in rdy[e].items() if t <= t0 + SLACK), key=lambda k: (prio[k], -k))
-            if not back and ops[n]["t"] > 0.15:
-                soon = [k for k, t in rdy[e].items() if t <= t0 + LOOK * ops[n]["t"] and prio[k] > prio[n] + GAP]
-                if soon:
-                    n = max(soon, key=lambda k: (prio[k], -k))
-            o = ops[n]
-            end = max(rdy[e].pop(n), t0) + o["t"]
-            if e != "X":
-                free[e] = end
-            fin = end + o["lat"]
-            if o["mb"] and not back:
-                pipe = max(pipe, fin) + o["mb"] * 5.0
-                fin = pipe
-            seq.append(n)
-            ends[n] = end
-            span = max(span, end if back else fin)
-            for k in nxt[n]:
-                if back:
-                    t = end + (ops[k]["lat"] + ops[k]["mb"] * 5.0 + WAKE if k in o["dep"] else 0.0)
-                else:
-                    t = fin + WAKE if n in ops[k]["dep"] else end
-                at[k] = max(at[k], t)
-                todo[k] -= 1
-                if todo[k] == 0:
-                    rdy.setdefault(ops[k]["e"], {})[k] = at[k]
-        return span, seq, ends
+        if not back:
+            prio = list(prio)
+            for n in rev:
+                p, d = prio[n], dur[n]
+                for k in succ[n]:
+                    if p < prio[k] + d:
+                        p = prio[k] + d
+                prio[n] = p
+        at = list(far) if back else [0.0] * len(ops)
+        line = {k: ([], []) for k in keys}
+        ends, span = [0.0] * len(ops), 0.0
 
-    if len(ops) not in PRIO:
-        name = [((o["w"] or o["r"] or [("",)])[0][0], n // 60) for n, o in enumerate(ops)]
-        kinds = sorted(set(name))
-        prio, seed, best = tail, SEED, (1e9, tail)
-        for w in ALPHA:
-            prio = best[1]
-            for it in range(BLEND):
-                s, sq, en = plan(prio, False)
-                if s < best[0]:
-                    best = (s, prio)
-                b = plan(en, True)[2]
-                prio = [(1 - w) * x + w * y for x, y in zip(prio, b)]
-        for names in ([o["tag"] for o in ops], name, [o["tag"] for o in ops]):
-            for sweep in range(SWEEPS):
-                for k in sorted(set(names)):
-                    for d in (-4.0, -1.2, 1.2, 4.0):
-                        cand = [p + (d if x == k else 0.0) for p, x in zip(best[1], names)]
-                        s = plan(cand, False)[0]
-                        if s < best[0] - 0.01:
-                            best = (s, cand)
-                if names is name:
-                    break
-        span, prio = best
-        for it in range(PASSES):
-            bump = {}
-            for k in kinds:
-                seed = (seed * 1103515245 + 12345) % 2147483648
-                if (seed >> 8) % 1000 < 25:
-                    bump[k] = ((seed >> 18) % 1000 - 500) / 100.0
-            cand = [p + bump.get(k, 0.0) for p, k in zip(prio, name)]
-            s = plan(cand, False)[0]
-            if s <= span + 0.4 * (1.0 - it / PASSES):
-                prio, span = cand, s
-                if s < best[0]:
-                    best = (s, cand)
+        def gap(key, t, d, pad):
+            st, en = line[key]
+            hi = n = len(en)
+            if not n or en[-1] + pad <= t + 1e-9:
+                return t, n
+            lo = 0
+            while lo < hi:
+                mid = (lo + hi) // 2
+                if en[mid] + pad <= t + 1e-9:
+                    lo = mid + 1
+                else:
+                    hi = mid
+            while lo < n and st[lo] - pad < t + d - 1e-9:
+                t = en[lo] + pad
+                lo += 1
+            return t, lo
+
+        def put(key, t, d):
+            i = gap(key, t, d, 0.0)[1]
+            line[key][0].insert(i, t)
+            line[key][1].insert(i, t + d)
+
+        for n in sorted(range(len(ops)), key=lambda k: -prio[k]):
+            t, d = at[n], dur[n]
+            look = looks[n]
+            i = ok = 0
+            while ok < len(look):
+                t1 = gap(look[i][0], t, d, look[i][1])[0]
+                if t1 > t + 1e-9:
+                    t, ok = t1, 0
+                ok += 1
+                i = (i + 1) % len(look)
+            for key in puts[n]:
+                put(key, t, d)
+            end = ends[n] = t + d
+            if back:
+                if end > span:
+                    span = end
+                for k, lag in lags[n]:
+                    if at[k] < end + lag:
+                        at[k] = end + lag
+                continue
+            fin = end + ops[n]["lat"]
+            if bulk[n]:
+                fin = gap("pipe", fin, bulk[n], 0.0)[0]
+                put("pipe", fin, bulk[n])
+                fin += bulk[n]
+            if fin > span:
+                span = fin
+            for k in hard[n]:
+                if at[k] < fin + WAKE:
+                    at[k] = fin + WAKE
+            for k in soft[n]:
+                if at[k] < end:
+                    at[k] = end
+        return span + MU * sum(ends[n] for n in marks) / len(marks), ends, prio
+
+    rev, dur, bulk = topo_order[::-1], [o["t"] for o in ops], [o["mb"] * 5.0 for o in ops]
+    far = [o["lat"] + o["mb"] * 5.0 for o in ops]
+    hard = [[k for k in succ[n] if n in ops[k]["dep"]] for n in range(len(ops))]
+    soft = [[k for k in succ[n] if n not in ops[k]["dep"]] for n in range(len(ops))]
+    lags = [[(k, far[k] + WAKE if k in o["dep"] else 0.0) for k in pred[n]] for n, o in enumerate(ops)]
+    looks = [[] if o["e"] == "X" else [(o["e"], 0.0)] + [(b + q, WAKE) for b in o["banks"] for q in "VSP" if q != o["e"]] for o in ops]
+    puts = [[] if o["e"] == "X" else [o["e"]] + [b + o["e"] for b in o["banks"]] for o in ops]
+    keys = set(k for l in looks for k, pad in l) | {"pipe"}
+
+    marks = [n for n, o in enumerate(ops) if o["e"] != "X" and o["tag"][0] not in "abcly"
+             and (o["sem"] is not None or o["w"][0][0] in MARK)]
+    if True:
+        start = PRIO.get(len(ops), tail)
+        turns = BLEND // 4 if len(ops) in PRIO else BLEND
+        best = (plan(start, False)[0], start)
+        for it in range(FB):
+            back = plan(plan(best[1], False)[1], True)[1]
+            best = min(best, (plan(back, False)[0], back))
+        wide, fine = [o["tag"][:-1] for o in ops], [o["tag"] + (o["w"] or o["r"])[0][0] for o in ops]
+        levels = []
+        for names in (wide, fine, [x[0] + x[2:] for x in wide], [x[0] + x[2:] for x in fine]):
+            kinds = {}
+            for n, x in enumerate(names):
+                kinds.setdefault(x, []).append(n)
+            levels.append([kinds[x] for x in sorted(kinds)])
+        state, now = [SEED], best
+
+        def rnd(n):
+            state[0] = (state[0] * 1103515245 + 12345) % 2147483648
+            return (state[0] >> 8) % n
+
+        for it in range(turns):
+            prio = list(now[1])
+            for z in range(1 + rnd(2)):
+                kinds = levels[rnd(4)]
+                d = (rnd(2001) - 1000) / 1000.0
+                for n in kinds[rnd(len(kinds))]:
+                    prio[n] += STEP * d * abs(d)
+            s, en, prio = plan(prio, False)
+            if it % BACK == BACK - 1:
+                back = [0.7 * x + 0.3 * y for x, y in zip(prio, plan(en, True)[1])]
+                s, prio = min((s, prio), (plan(back, False)[0], back))
+            if s < now[0] + HEAT * (turns - it) / BLEND:
+                now = (s, prio)
+            best = min(best, now)
+            if it % 200 == 0:
+                LOG.append(round(now[0], 1))
         PRIO[len(ops)] = best[1]
-    SPAN[0], seq, ends = plan(PRIO[len(ops)], False)
+    SPAN[0], ends = plan(PRIO[len(ops)], False)[:2]
+    seq = sorted(range(len(ops)), key=lambda n: ends[n] - ops[n]["t"])
     SPAN[1:] = [ops, seq, ends, tail]
     pos = {n: i for i, n in enumerate(seq)}
-    known = {e: {} for e in Q}
+    known, users = {e: {} for e in Q}, {}
     for n in seq:
         o, need = ops[n], {}
+        for b in o["banks"]:
+            o["dep"].update(k for q, k in users.setdefault(b, {}).items() if q != o["e"])
+            users[b][o["e"]] = n
         for k in o["dep"]:
             key = ops[k]["sem"] or ops[k]["e"]
             need[key] = max(need.get(key, -1), pos[k])
@@ -299,6 +342,7 @@ def build(g, core, rank, T, topo, rel, ops):
     V, SC, PE = g.vector, g.scalar, g.tensor
     tag = ["a"]
     turn = places(rank, rel)
+    al = slice(None)
 
     def a(nm, *ix, part=slice(None), tag=None):
         shape = SCRATCH[nm][1][1:]
@@ -313,6 +357,9 @@ def build(g, core, rank, T, topo, rel, ops):
     def c2(nm, lo, hi, st=1):
         return a(nm, slice(lo, hi, st))
 
+    def cn(nm, lo, n):
+        return a(nm, slice(lo, lo + n))
+
     def ind(win, off):
         return dict(win, ap=win["ap"].indirect(off["ap"]), off=off["reg"], n=16 * off["n"], ind=True)
 
@@ -324,7 +371,7 @@ def build(g, core, rank, T, topo, rel, ops):
         for x in outs:
             w += x["reg"]
             r += x.get("off", [])
-        t = t * PEF + ADDP if e == "P" else t + (ADD if e in "VS" else 0.0)
+        t = t * PEF + ADDP if e == "P" else t * EF.get(e, 1.0) + (ADD if e in "VS" else 0.0)
         ops.append({"e": e, "fn": fn, "r": r, "w": w, "sem": sem, "inc": inc, "t": t, "lat": lat, "mb": mb,
                     "after": list(after), "key": len(ops), "tag": tag[0] + e})
         return len(ops) - 1
@@ -333,9 +380,9 @@ def build(g, core, rank, T, topo, rel, ops):
 
     def cost(out, in0, f):
         if out["ind"]:
-            return 0.05 + out["n"] * 3.8 * CY
+            return 0.05 + out["n"] * SCA * CY
         if in0["ind"]:
-            return 0.05 + in0["n"] * 1.56 * CY
+            return 0.06 + in0["n"] * GAT * CY
         if f == 0:
             f = 0.5 if out["d"] in (B, U, H) and in0["d"] in (B, U, H) else 1
         return max(64, in0["n"] * f) * CY
@@ -361,13 +408,27 @@ def build(g, core, rank, T, topo, rel, ops):
         add("S", lambda: SC.activation(out["ap"], in_["ap"], func, bias=ap(bias), scale=ap(scale)), [out],
             [in_, scale, bias], cost(out, in_, 1))
 
-    def mm(out, terms):
-        for i, (l, r) in enumerate(terms):
-            mm1(out, l, r, i == 0, i == len(terms) - 1)
+    def lin(e, out, in_, scale, bias):
+        if e == "S":
+            act(out, in_, scale=scale, bias=bias)
+        else:
+            ts(out, in_, scale, Op.mult, bias, Op.add)
 
-    def mm1(out, l, r, st, sp):
-        add("P", lambda: PE.matmul(out["ap"], l["ap"], r["ap"], st, sp), [out], [l, r],
-            max(64, r["n"]) * CY * (2 if r["d"] == F else 0.5))
+    def mm(out, terms):
+        mmg([[(out, l, r) for l, r in terms]])
+
+    def mms(parts):
+        mmg([parts])
+
+    def mmg(groups, start=True, stop=True):
+        def fn():
+            for parts in groups:
+                for i, (o, l, r) in enumerate(parts):
+                    ins = PE.matmul(o["ap"], l["ap"], r["ap"], start and i == 0, stop and i == len(parts) - 1)
+            return ins
+        flat = [p for parts in groups for p in parts]
+        add("P", fn, [p[0] for p in flat], [x for p in flat for x in p[1:]],
+            sum(max(min(64, l["n"]), r["n"]) * CY * (2 if r["d"] == F else 0.5) for o, l, r in flat))
 
     def iota(out, pat, base, cm, after=()):
         t = 0.13 + 2 * out["n"] * CY
@@ -376,13 +437,20 @@ def build(g, core, rank, T, topo, rel, ops):
         else:
             add("G", lambda: g.iota(out["ap"], pat, base, cm, allow_small_or_imprecise_dtypes=True), [out], [], t, after=after)
 
+    def select(out, in_, pat, op, v, cm):
+        add("G", lambda: g.affine_select(out["ap"], in_["ap"], pat, op, v, 0, cm), [out], [in_], 0.17 + 2 * out["n"] * CY,
+            after=sent0)
+
+    def fill(out, v, src=None):
+        act(out, src or c2("one", 0, out["n"]), scale=0.0, bias=v)
+
     nd = [0]
 
-    def dma(e, out, in_, new=True, mb=0.02, after=()):
+    def dma(e, out, in_, new=True, mb=0.02, after=(), behind=None):
         if new:
             nd[0] += 1
         q = {"Y": g.sync, "S": g.scalar}[e]
-        return add(e, lambda: q.dma_start(ap(out), ap(in_)), [out] if isinstance(out, dict) else [], [in_], 0.06,
+        return add(e, lambda: q.dma_start(ap(out), ap(in_)), [out] if isinstance(out, dict) else [], [in_, behind], 0.06,
                    sem="d%d" % (nd[0] - 1), lat=2.3, mb=mb, after=after)
 
     def send(m, piece, land, ready=()):
@@ -433,444 +501,518 @@ def build(g, core, rank, T, topo, rel, ops):
         return c2("cc", cols[nm], cols[nm] + 1)
 
     eye = lambda k, i: a("eye", k, slice(i, i + 1))
-    ED = {k: i for i, k in enumerate(["RXO", "RX", "RW", "I", "NI", "BDH", "NS4", "VB", "CY", "GW", "I4", "BD"] + ["REP%d" % q for q in range(8)])}
-    KG = {k: i for i, k in enumerate(["UB", "LB", "UW", "VW", "S0", "S1", "S2", "S3", "JW", "S4"])}
+    ED = {k: i for i, k in enumerate(["RXO", "MH", "RX", "RW", "MZ", "I", "NI", "BDH", "NS4", "CY", "GW", "I4", "BD"]
+                                     + ["REP%d" % q for q in range(8)])}
+    KG = {k: i for i, k in enumerate(["UW", "VW", "S0", "S1", "S2", "S3", "EB0", "EB1", "EB2", "EB3", "CB",
+                                      "JW", "S4", "S4D", "NSU", "US", "PV", "PKU"])}
+    ZK = {k: i for i, k in enumerate(["Vc", "Vb", "Uc", "Ub", "Lc", "Lb", "Vs", "Us", "Ls"])}
+    ZW = {k: i for i, k in enumerate(["i", "s", "b", "b16", "d"])}
     ed = lambda k: a("ed", ED[k])
     eg = lambda k: a("eg", KG[k])
     zv = lambda k, r: a("zz", k, slice(15 - r, 143 - r))
+    zk = lambda k, l: a("zk", ZK[k], slice(12 - 4 * l, 140 - 4 * l))
+    zw = lambda k, l: a("zw", ZW[k], slice(12 - 4 * l, 140 - 4 * l))
     mwin = c2("mt", PAD, PAD + WT)
     mrow = lambda s, lo, hi: a("mt", slice(lo, hi), part=slice(s, 128, 16), tag=s)
+    one = lambda n: c2("one", 0, n)
+    pi = lambda i: c2("pint", i, i + 1)
+    E1, E4, EN, EN4 = range(4)
+    HI, HS, XR, ONE, DEAD, SID = 0, 4, 8, 12, 13, 15
+    e1 = lambda i: eye(E1, i)
 
     mset(a("x0i"), 0)
     first = [dma("S", c2("ta", S * rank, S * rank + S), T.tg[:])]
     for e in range(4):
         first.append(dma("YS"[e % 2], a("x0i", part=slice(8 + e, 128, 16), tag=e), T.x0[e::4, :], new=e == 0))
     for m in range(16):
-        first.append(dma("YS"[m % 2], c2("mt", PAD + 256 * m, PAD + 256 * m + 256), T.cf[m::16, :], mb=0.065, after=first[:5]))
-    dma("Y", c2("ftab", 0, FC), T.ft[:], mb=0.26, after=first)
+        first.append(dma("YS"[m % 2], cn("ct", 256 * m, 256), T.cf[m::16, :], mb=0.065, after=first[:5]))
     iota(c2("pint", 0, 1), [[1, 1]], 0, 1)
     iota(a("r4"), [[16, 8], [0, 4], [1, 4]], 8, 0)
     iota(a("io_"), [[1, S]], 0, 0)
     iota(a("g16"), [[16, 8], [0, 16]], 0, 0)
     send("tg", lambda o: c2("ta", S * rank, S * rank + S), lambda q: c2("ta", S * q, S * q + S))
 
-    pi = lambda i: c2("pint", i, i + 1)
     mset(a("one"), 1.0)
     mset(c2("yr", 0, NR * S), 0.0)
+    mset(ed("MH"), 0.0)
     cp(col("p"), pi(0))
     ts(pi(1), pi(0), 15, Op.bitwise_and)
     ts(pi(2), pi(0), 2, Op.logical_shift_right, 3, Op.bitwise_and)
-    ts(pi(3), pi(0), 3, Op.bitwise_and)
     ts(ed("RXO"), a("r4"), col("p"), Op.is_equal)
     cp(col("p16"), pi(1))
-    ts(col("q1"), pi(2), 1.0, Op.add)
     ts(col("ini"), pi(2), float(S), Op.mult, -1.0, Op.add)
     ts(col("thr"), pi(2), float(S), Op.mult, float(CAP), Op.add)
     ts(a("ed", ED["RXO"], slice(15, 128, 16)), c2("io_", 15, 128, 16), col("p"), Op.is_equal)
-    ts(col("oc"), pi(3), 2.0, Op.is_equal, col("q1"), Op.mult)
     ts(a("eye", 0), c2("io_", 0, 16), col("p16"), Op.is_equal)
     ts(col("g16"), col("p"), col("p16"), Op.subtract)
-    ts(col("off"), col("p16"), 8.0, Op.is_lt, 192.0, Op.mult)
+    ts(col("off"), col("p16"), 8.0, Op.is_lt, -192.0, Op.mult)
     ts(col("t1"), col("p16"), 8.0, Op.is_ge, 0.75, Op.mult)
     ts(col("t2"), pi(2), 1.0, Op.is_equal, 0.25, Op.mult)
-    ts(col("tm"), eye(0, 12), eye(0, 13), Op.add)
+    ts(col("tm"), e1(12), e1(13), Op.add)
     ts(a("z16"), c2("io_", 0, 144), -15.0, Op.add, col("g16"), Op.is_equal)
-    ts(col("t3"), col("off"), -0.375 / 192, Op.mult, col("t2"), Op.add)
+    ts(a("gm"), c2("g16", 0, 128, 16), col("g16"), Op.is_equal)
+    ts(col("t3"), col("off"), 0.375 / 192, Op.mult, col("t2"), Op.add)
     ts(col("sc"), col("t1"), 0.25, Op.add, col("tm"), Op.subtract)
-    ts(col("bi"), col("t3"), eye(0, 12), Op.add, col("off"), Op.add)
+    ts(col("bi0"), col("t3"), e1(12), Op.add, col("off"), Op.subtract)
+    act(col("tsc"), e1(12), scale=-1.0 / 256, bias=1.0 / 256)
+    ts(col("t4"), pi(2), -0.25, Op.mult, 192.0 - 127.5 / 256, Op.add)
+    ts(col("tb0"), col("t4"), col("tsc"), Op.mult, 256.0, Op.mult)
+    act(col("tb0"), col("tb0"), bias=e1(12))
     for o in range(NR):
-        act(c2("xw", S * o, S * o + CAP), c2("one", 0, CAP), scale=col("tm"))
+        if o < 3:
+            act(col("h%d" % o), e1(4 * o + 6), scale=-1.0, bias=e1(4 * o + 2))
+        else:
+            ts(col("h3"), e1(14), e1(2), Op.subtract, e1(12), Op.add)
+        act(a("ed", ED["MH"], slice(4 * o, 128, 16)), a("gm"), scale=col("h%d" % o))
+        act(c2("xw", S * o, S * o + CAP), one(CAP), scale=col("tm"))
     cp(c2("xp", 0, S), a("x0i"))
 
     def source(r):
         tag[0] = "s%d" % r
-        px, pslot = c2("pH", 0, S), c2("pH", 256, 266)
+        px, pm, ph, pslot = c2("pC", 0, S), cn("pC", 256, S), c2("pD", 0, S), c2("pD", 256, 266)
         old = c2("xp", S * r, S * r + S)
         if r == 0:
-            ts(a("clp"), a("io_"), eye(0, 15), Op.mult)
+            ts(a("clp"), a("io_"), e1(15), Op.mult)
             mm(px, [(ed("RXO"), a("clp")), (ed("RXO"), old)])
-            cp(a("xa"), px)
+            pm = px
         else:
             back = ind(c2("yr", NR * S * (r - 1), NR * S * r), c2("sl", 16 * (r - 1), 16 * (r - 1) + 10))
-            mm1(px, ed("RXO"), old, True, False)
-            mm1(px, ed("RW"), a("wt"), False, False)
             ts(a("clp"), back, 120.0, Op.max, 136.0, Op.min)
-            mm1(px, ed("RX"), a("clp"), False, True)
+            terms = [(ed("RXO"), old), (ed("RW"), a("wt")), (ed("RX"), a("clp"))]
+            mm(px, terms)
+        lin(TQ, a("th"), px, col("tsc"), col("tb%d" % min(r, 1)))
+        if r < RO:
+            mm(ph, [(ed("MH"), a("th"))])
+        if r > 0:
+            mm(pm, terms + [(ed("MZ"), a("th"))])
             sums = c2("acc", S * (r - 1), S * r)
             if r == 1:
                 act(sums, back)
             else:
                 tt(sums, back, c2("acc", S * (r - 2), S * (r - 1)), Op.add)
-            if r == RO:
-                dma("Y", T.ys[:], sums)
-            ts(a("xa"), px, col("cadd"), Op.add)
         if r == RO:
-            ts(a("xi"), a("xa"), 255, Op.bitwise_and)
-            cp(a("xf"), a("xi"))
+            dma("Y", T.ys[:], sums)
+            act(a("xf"), pm, bias=256.0 * 192 - 128)
             for e in range(4):
                 dma("YS"[e % 2], T.yx[e::4, :], a("xf", part=slice(e, 128, 16)), new=e == 0)
             return
-        ts(a("oh"), a("xa"), 6, Op.logical_shift_right, 3, Op.bitwise_and)
-        ts(a("xi"), a("xa"), 255, Op.bitwise_and)
-        ts(a("hh"), a("oh"), 1.0, Op.add, col("oc"), Op.is_equal)
-        ts(a("xq"), a("xi"), col("sc"), Op.mult, col("bi"), Op.add)
-        add("V", lambda: V.tensor_tensor_scan(T.cum[:], T.one[:], T.hh[:], col("ini")["ap"], Op.mult, Op.add),
-            [a("cum")], [a("one"), a("hh"), col("ini")], S * CY / 2)
+        add("V", lambda: V.tensor_tensor_scan(T.cum[:], T.one[:, 0:S], ph["ap"], col("ini")["ap"], Op.mult, Op.add),
+            [a("cum")], [one(S), ph, col("ini")], S * CY)
         new = c2("xp", S * (r + 1), S * (r + 2))
-        tt(a("prd"), a("hh"), a("cum"), Op.mult)
+        tt(a("prd"), ph, a("cum"), Op.mult)
         mm(pslot, [(c2("z16", 15 - k, 143 - k), c2("prd", k, S, 16)) for k in range(16)])
-        ts(new, a("xq"), col("off"), Op.subtract)
-        ts(a("wt"), a("prd"), col("thr"), Op.is_ge)
+        act(a("xq"), pm, scale=col("sc"), bias=col("bi%d" % min(r, 1)))
+        act(new, a("xq"), bias=col("off"))
         sl = c2("sl", 16 * r, 16 * r + 10)
         cp(sl, pslot)
         base = NR * S * r
         cp(ind(c2("xw", base, base + NR * S), sl), new)
+        ts(a("wt"), a("prd"), col("thr"), Op.is_ge)
         piece = lambda o: c2("xw", base + S * o, base + S * o + CAP)
-        land = lambda q: a("xl", slice(8 * r + 2 * turn.index(q), 8 * r + 2 * turn.index(q) + 2))
+        land = lambda q: cn("xl", 256 * r + CAP * turn.index(q), CAP)
         act(land(rank), piece(rank))
         return send("x%d" % r, piece, land, [c2("yr", base, base + NR * S)])
 
     sent0 = source(0)
     tag[0] = "b"
-    iota(c2("jj", 0, 128), [[0, 16 // LB], [1, 8], [0, LB]], 0, 0, after=sent0)
-    iota(c2("jj", 128, 136), [[LB, 16 // LB], [0, LB // 2]], 0, 0, after=sent0)
-    iota(c2("dmp", 0, 16), [[0, 8], [16, 2]], DC, 0, after=sent0)
-    for lo in range(0, WT, WT // 8):
-        iota(c2("iot", lo, lo + WT // 8), [[1, WT // 8]], lo, 0, after=sent0)
+    dma("Y", c2("ftab", 0, FC), T.ft[:], mb=0.26, behind=c2("xl", 192, 256))
+    dma("Y", c2("ftab", FC, DF), T.ft[:, 0:FX], mb=0.2, new=False, behind=c2("xl", 192, 256))
+    iota(a("q4"), [[4, 4], [0, 4], [1, 4]], 0, 0)
+    for lo in range(0, WT, WT // 16):
+        iota(c2("ycw", lo, lo + WT // 16), [[1, WT // 16]], lo, 0, after=sent0)
 
-    def keys(m):
-        bank = c2("pC" if m % 2 else "pD", 0, 256)
-        acc = c2("mx", 0, 256)
-        if m == 0:
-            act(acc, c2("mt", PAD, PAD + 256), scale=16.0, bias=15.0)
-            return
-        act(bank, c2("mt", PAD + 256 * m, PAD + 256 * m + 256), scale=16.0, bias=float(15 - m))
-        tt(a("ki") if m == 15 else acc, bank, acc, Op.max)
-
-    one = lambda n: c2("one", 0, n)
-    ts(pi(4), pi(0), 1, Op.logical_shift_right, 1, Op.bitwise_and)
-    ts(pi(5), pi(0), 3, Op.logical_shift_right, 1, Op.bitwise_and)
-    ts(a("pa"), c2("io_", 0, 16), -1.0, Op.mult, col("p"), Op.add)
-    ts(a("gm"), c2("g16", 0, 128, 16), col("g16"), Op.is_equal)
-    mset(a("ka"), 0.0)
-    mset(a("kg"), 0.0)
-    mset(a("ea"), 0.0)
-    for k, v in enumerate((4.0, -1.0, -4.0, 188.0, 916.0, 592.0, 176.0, 768.0, 60.0)):
-        act(a("eye", k + 1), a("eye", 0), scale=v)
-    E1, E4, EN, EN4, E188, E916, E592, E176, E768, E60 = range(10)
-    HI, HS, XR, ONE, DEAD, SID = 0, 4, 8, 12, 13, 15
-
-    def kset(nm, m, lo, hi, st, t1, t2=None):
-        out = a(nm, m, slice(lo, hi, st))
-        act(out, one(len(range(lo, hi, st))), scale=eye(*t1), bias=eye(*t2) if t2 else 0.0)
-
-    def kadd(nm, m, lo, hi, st, t):
-        out = a(nm, m, slice(lo, hi, st))
-        act(out, out, bias=eye(*t))
-
-    kset("ka", 0, 0, 4, 2, (E1, HI)); kset("ka", 0, 1, 4, 2, (E1, HI), (E1, ONE))
-    kset("ka", 0, 4, 5, 1, (E1, HS)); kset("ka", 0, 5, 6, 1, (E4, HS + 2))
-    kset("ka", 1, 0, 4, 1, (E1, HI + 1)); kset("ka", 1, 4, 5, 1, (E1, HS + 1)); kset("ka", 1, 5, 6, 1, (E1, HS + 3))
-    kset("ka", 2, 0, 4, 1, (E188, HI + 2), (E916, HI + 3)); kset("ka", 2, 4, 5, 1, (E188, HS + 2), (E916, HS + 3))
-    kset("ka", 2, 5, 6, 1, (E592, HS), (E176, HS + 1)); kset("ka", 2, 6, 7, 1, (E1, SID))
-    act(a("ka", 2, slice(7, 8)), eye(E1, DEAD), scale=8192.0)
-    for m in range(4):
-        keys(m)
-    kset("kg", KG["UB"], 0, 16, 1, (E4, HI + 2))
-    kadd("kg", KG["UB"], 4, 8, 1, (E4, ONE)); kadd("kg", KG["UB"], 12, 16, 1, (E4, ONE))
-    kset("kg", KG["LB"], 0, 16, 1, (E592, HI), (E176, HI + 1))
-    for kk, e in ((1, E592), (2, E176), (3, E768)):
-        kadd("kg", KG["LB"], kk, 16, 4, (e, ONE))
-    for m in range(4, 8):
-        keys(m)
-    for b, e in ((0, 0), (4, 2)):
-        kset("kg", KG["UW"], b, b + 4, 2, (E4, HI + e), (EN, XR + e)); kadd("kg", KG["UW"], b, b + 4, 2, (E4, ONE))
-        kset("kg", KG["UW"], b + 1, b + 4, 2, (EN4, HI + e), (E1, XR + e))
-        kset("kg", KG["VW"], b, b + 4, 1, (EN4, HI + e + 1), (E1, XR + e + 1))
-    for kk in range(4):
-        cp(a("kg", KG["S%d" % kk], slice(kk, 16, 4)), a("eye", 0, slice(0, 4)))
-    ts(a("kg", KG["JW"], slice(0, 1)), col("p16"), 0.5, Op.mult)
-    cp(a("kg", KG["S4"], slice(4, 5)), eye(E1, 4))
-    ts(col("bva"), pi(4), 2.0, Op.mult, 1.0, Op.add)
-    ts(col("bvb"), pi(5), 2.0, Op.mult, 1.0, Op.add)
-    ts(col("sw"), pi(4), 2.0, Op.mult, -1.0, Op.add)
-    ts(col("bw"), pi(4), -4.0, Op.mult, 4.0, Op.add)
-    for m in range(8, 16):
-        keys(m)
+    ts(ed("BD"), a("g16"), col("g16"), Op.is_equal)
+    ts(ed("I"), c2("io_", 0, 128), col("p"), Op.is_equal)
+    act(ed("I4"), ed("I"), scale=16.0)
+    for q in range(8):
+        act(a("rp", q), ed("BD"), scale=e1(q))
+    act(col("k0"), col("p16"), scale=-1.0, bias=15.0)
+    act(a("kc", 0), one(256), scale=col("k0"))
+    act(a("kc", 1), one(256), scale=col("k0"), bias=-8.0)
+    for i, lo in enumerate(range(PAD, PAD + WT, WT // 8)):
+        if i < MZ:
+            mset(cn("mt", lo, WT // 8), 0.0)
+        else:
+            fill(cn("mt", lo, WT // 8), 0.0, cn("ct", 0, WT // 8))
+    tag[0] = "c"
+    for m in range(16):
+        bank = cn(("pE", "pF", "pG", "pH")[m % 4], 0, 256)
+        mm(bank, [(a("rp", m % 8), a("kc", m // 8)), (ed("I4"), cn("ct", 256 * m, 256))])
+        acc = cn("mx", 256 * (m % 2), 256)
+        if m < 2:
+            act(acc, bank)
+        else:
+            tt(cn("pE", 256, 256) if m == 14 else acc, bank, acc, Op.max)
+    tt(a("ki"), cn("pE", 256, 256), acc, Op.max)
     ts(c2("k2", 0, 256), a("ki"), 15, Op.bitwise_and)
-    ts(c2("k2", 256, 512), a("ki"), 4, Op.logical_shift_right)
     ts(c2("mq", 0, 256), c2("k2", 0, 256), -1.0, Op.mult, 15.0, Op.add)
-    cp(c2("mq", 256, 512), c2("k2", 256, 512))
-    mset(c2("mt", PAD + WC, PAD + WT), 0.0)
     for s, sh in enumerate(SHIFTS):
-        dma("Y", mrow(s, PAD - sh, PAD - sh + WC), c2("mq", 0, 256), new=s == 0)
+        dma("YS"[s % 2], mrow(s, PAD - sh, PAD - sh + WC), c2("mq", 0, 256), new=s == 0, mb=0.065)
         for q in range(2):
             n = min(sh - 256 * q, 256)
             if n > 0:
                 lo = PAD - sh + WC + 256 * q
-                dma("Y", mrow(s, lo, lo + n), a("mq", slice(0, n), part=slice(q, 128, 16)), new=False)
-    k = dma("Y", mrow(4, PAD, PAD + WC), c2("mq", 256, 512), new=False)
-    dma("Y", c2("ctab", 0, WC), T.cf[:], mb=1.0, after=range(k - 8, k + 1))
+                dma("SY"[s % 2], mrow(s, lo, lo + n), a("mq", slice(0, n), part=slice(q, 128, 16)), new=False)
+    ts(c2("k2", 256, 512), a("ki"), 4, Op.logical_shift_right)
+    cp(c2("mq", 256, 512), c2("k2", 256, 512))
+    dma("Y", mrow(4, PAD, PAD + WC), c2("mq", 256, 512), mb=0.065)
+    dma("Y", a("ctab"), T.cf[:], mb=1.0, behind=mwin)
+
+    tag[0] = "b"
+    ts(pi(4), pi(0), 1, Op.logical_shift_right, 1, Op.bitwise_and)
+    ts(a("pa"), c2("io_", 0, 16), -1.0, Op.mult, col("p"), Op.add)
+    mset(a("kz"), 0.0)
+    mset(a("kg"), 0.0)
+    mset(a("zk"), 0.0)
+    for k, v in enumerate((4.0, -1.0, -4.0)):
+        act(a("eye", k + 1), a("eye", 0), scale=v)
+
+    def kset(nm, m, lo, hi, st, t1, t2=0.0):
+        out = a(nm, m, slice(lo, hi, st))
+        act(out, one(out["n"]), scale=t1, bias=t2)
+
+    def mix(nm, c1, r1, c2_, r2):
+        act(col(nm), e1(r1), scale=c1)
+        ts(col(nm), e1(r2), c2_, Op.mult, col(nm), Op.add)
+        return col(nm)
+
+    kset("kz", ZK["Vc"], 0, 4, 1, e1(HI + 1)); kset("kz", ZK["Vb"], 0, 4, 1, e1(HI + 3))
+    for nm, r0 in (("Uc", HI), ("Ub", HI + 2)):
+        kset("kz", ZK[nm], 0, 4, 2, e1(r0)); kset("kz", ZK[nm], 1, 4, 2, e1(r0), e1(ONE))
+    kset("kz", ZK["Lc"], 0, 4, 1, mix("lc", 188.0, HI + 2, 916.0, HI + 3))
+    kset("kz", ZK["Lb"], 0, 4, 1, mix("lb", 148.0, HI, 44.0, HI + 1))
+    cp(a("kz", ZK["Vs"], slice(0, 2)), a("eye", E1, slice(HS + 1, HS + 4, 2)))
+    cp(a("kz", ZK["Us"], slice(0, 2)), a("eye", E1, slice(HS, HS + 4, 2)))
+    kset("kz", ZK["Ls"], 0, 1, 1, mix("ls", 188.0, HS + 2, 916.0, HS + 3))
+    kset("kz", ZK["Ls"], 1, 2, 1, mix("lt", 148.0, HS, 44.0, HS + 1))
+    kset("kz", ZK["Ls"], 2, 3, 1, eye(E4, SID)); kset("kz", ZK["Ls"], 3, 4, 1, eye(E4, DEAD))
+    for b, e in ((0, 0), (4, 2)):
+        kset("kg", KG["UW"], b, b + 4, 2, eye(E4, HI + e), eye(EN, XR + e))
+        out = a("kg", KG["UW"], slice(b, b + 4, 2))
+        act(out, out, bias=eye(E4, ONE))
+        kset("kg", KG["UW"], b + 1, b + 4, 2, eye(EN4, HI + e), e1(XR + e))
+        kset("kg", KG["VW"], b, b + 4, 1, eye(EN4, HI + e + 1), e1(XR + e + 1))
+    for kk in range(4):
+        cp(a("kg", KG["S%d" % kk], slice(4 * kk, 4 * kk + 4)), a("eye", 0, slice(0, 4)))
+    ts(a("kg", slice(KG["EB0"], KG["EB0"] + 4)), a("q4"), col("p16"), Op.is_equal, 16.0, Op.mult)
+    for kk, v in ((1, 592.0), (2, 176.0), (3, 768.0)):
+        ts(a("kg", KG["CB"], slice(4 * kk, 4 * kk + 4)), one(4), e1(ONE), Op.mult, v, Op.mult)
+    ts(col("bva"), pi(4), 2.0, Op.mult, 1.0, Op.add)
+    ts(col("sw"), pi(4), 2.0, Op.mult, -1.0, Op.add)
+    ts(col("bw"), pi(4), -4.0, Op.mult, 4.0, Op.add)
+    NE = KG["JW"]
     for gq in range(8):
         gm = c2("gm", gq, gq + 1)
-        act(a("ea", slice(gq % 2, 6, 2), slice(16 + 16 * gq, 32 + 16 * gq)), a("ka"), scale=gm)
-        ts(a("eg", slice(None), slice(16 * gq, 16 * gq + 16)), a("kg"), gm, Op.mult)
-    pac = lambda i: c2("pa", i, i + 1)
-    ts(ed("BD"), a("g16"), col("g16"), Op.is_equal)
-    act(ed("VB"), ed("BD"), scale=eye(E1, HI + 3))
-    ts(ed("I"), c2("io_", 0, 128), col("p"), Op.is_equal)
-    for q in range(8):
-        act(ed("REP%d" % q), ed("BD"), scale=eye(E1, q))
-    ts(a("zz", 0), a("z16"), 1.0, Op.mult)
-    ts(ed("CY"), a("g16"), pac(ONE), Op.is_equal, -255.0 / 512, Op.mult)
-    cp(a("i16"), ed("I"))
+        act(a("zk", al, slice(12 + 16 * gq, 16 + 16 * gq)), a("kz"), scale=gm)
+        ts(a("eg", slice(0, NE), slice(16 * gq, 16 * gq + 16)), a("kg", slice(0, NE)), gm, Op.mult)
+    ts(ed("CY"), a("g16"), c2("pa", ONE, ONE + 1), Op.is_equal, -255.0 / 512, Op.mult)
     act(a("i32"), ed("I"), scale=1.0 / 256)
+
+    tag[0] = "l"
     act(ed("NI"), ed("I"), scale=-1.0)
-    act(a("zz", 1), a("zz", 0), scale=8192.0)
-    act(a("zz", 2), a("zz", 0), scale=eye(E1, 0))
-    ts(c2("dmp", 0, 16), c2("dmp", 0, 16), col("p16"), Op.add)
-    ts(pi(7), pi(0), LB - 1, Op.bitwise_and)
-    cp(col("p4"), pi(7))
-    ts(c2("lx", 0, 8), c2("jj", 128, 136), col("p4"), Op.add)
-    cp(c2("ld", 0, 16), c2("io_", 0, 16))
-    cp(c2("ld", 16, 24), c2("io_", 0, 16, 2))
-    mset(c2("ctab", WC, WT), 0.0)
-    mset(c2("ftab", FC, FC + 32), 0.0)
-    ts(c2("dmp", 16, 32), c2("dmp", 0, 16), float(DF - DC), Op.add)
+    act(a("zz", 1), a("z16"), scale=8192.0)
+    act(a("zz", 2), a("z16"), scale=e1(0))
+    act(col("dm0"), col("p16"), bias=float(DC))
+    act(col("dm1"), col("p16"), bias=float(DF))
+    if CH == 32:
+        for t in range(2):
+            for z in range(2):
+                act(c2("dmp", 16 * t + z, 16 * t + 16, 2), one(8), scale=col("dm%d" % t), bias=16.0 * z)
+    fill(c2("ftab", DF, DF + 32), 0.0)
+    for k in range(5):
+        fill(a("zw", k), 0.0)
+    for nm, t, v in (("i", 0, 1.0), ("s", 2, 1.0), ("b", 1, 1.0), ("b16", 1, 16.0), ("d", 3, 8192.0)):
+        act(a("kw", ZW[nm]), a("eye", E1, slice(t, 16, 4)), scale=v)
+    fill(a("cst"), 0.0)
+    for lo, n, v in ((0, 8, 2048.0), (32, 8, 2048.0), (64, 16, 4096.0), (80, 16, 2048.0)):
+        fill(cn("cst", lo, n), v)
+    for i, q in enumerate(turn):
+        fill(cn("cst", 32 * (i // 2) + 16 + 4 * (i % 2), 4), float(S * q))
+    ts(pi(3), pi(0), 3, Op.bitwise_and)
+    ts(col("cen"), pi(3), 0.0, Op.is_equal, 2048.0, Op.mult)
+    for k in range(8, 16):
+        act(a("rp", k), ed("BD"), scale=e1(k))
+    for k in range(0, 16, 2):
+        select(a("rk", slice(k, k + 2)), a("rp", slice(k, k + 2)), [[0, 2], [-1, 128]], Op.not_equal, -1.0, 1)
+    for k in range(16):
+        select(a("et", k), zv(1, k), [[1, 128]], Op.is_gt, 0.0, -1)
+    ts(pi(6), pi(0), 1, Op.bitwise_and)
+    ts(col("sb"), pi(6), 4.0, Op.mult, -2.0, Op.add)
+    ts(col("w4"), pi(6), 3.0, Op.mult, 1.0, Op.add)
+    ts(pi(7), pi(1), 1, Op.logical_shift_right)
+    cp(col("ph"), pi(7))
+    act(a("kg", KG["JW"], slice(0, 1)), col("p16"), scale=0.5)
+    act(a("kg", KG["S4"], slice(4, 5)), e1(4))
+    act(a("kg", KG["S4D"], slice(4, 5)), e1(4))
+    act(a("kg", KG["S4D"], slice(13, 14)), e1(13))
+    for z in range(2):
+        act(a("kg", KG["PV"], slice(z, 16, 2)), a("eye", E1, slice(5, 13)))
+        ts(a("kg", KG["US"], slice(z, 16, 2)), c2("io_", 0, 8), col("ph"), Op.is_equal, (-2.0, 0.5)[z], Op.mult)
+    act(a("kg", KG["NSU"], slice(0, 16, 2)), a("eye", E1, slice(5, 13)), bias=eye(EN, 4))
+    act(a("kg", KG["NSU"], slice(1, 16, 2)), one(8), scale=eye(EN, 4))
+    ts(a("kg", KG["PKU"], slice(5, 13)), c2("io_", 0, 8), col("ph"), Op.is_equal, col("w4"), Op.mult)
+    for gq in range(8):
+        gm = c2("gm", gq, gq + 1)
+        act(a("zw", al, slice(12 + 16 * gq, 16 + 16 * gq)), a("kw"), scale=gm)
+        ts(a("eg", slice(NE, 18), slice(16 * gq, 16 * gq + 16)), a("kg", slice(NE, 18)), gm, Op.mult)
+    act(col("jp1"), col("p16"), bias=1.0)
+    act(col("eb"), col("p16"), scale=-LN4)
+    act(col("e60"), e1(0), scale=60.0)
+    ts(col("t5"), col("p16"), 12.0, Op.is_lt, col("sc"), Op.mult)
+    act(col("bi1"), col("t5"), scale=256.0 * 192 - 128, bias=col("bi0"))
+    act(col("tb1"), col("tsc"), scale=-128.0, bias=col("tb0"))
+    ts(ed("RX"), a("r4"), -8.0, Op.add, col("p"), Op.is_equal)
+    act(ed("RW"), ed("BD"), scale=8.0)
+    mset(a("ed", slice(ED["RX"], ED["RW"] + 1), slice(15, 128, 16)), 0.0)
+    act(ed("MZ"), ed("RX"), scale=-256.0)
+    act(ed("GW"), ed("BD"), scale=-0.5)
+    tt(ed("BDH"), ed("GW"), ed("I"), Op.add)
+    act(ed("I4"), ed("I"), scale=4096.0)
+    ts(a("ed", ED["GW"], slice(0, 128, 2)), c2("g16", 0, 128, 2), col("g16"), Op.is_equal, 127.5 / 4096 / 256, Op.mult)
+    ts(a("ed", ED["GW"], slice(1, 128, 2)), c2("g16", 1, 128, 2), col("g16"), Op.is_equal, 0.5, Op.mult)
+    act(a("gq"), a("gm"), scale=1.0 / 4096)
+    act(ed("NS4"), ed("BD"), scale=eye(EN, 4))
+    act(a("zz", 3), a("z16"), scale=col("jp1"))
+    for r in range(1, RO):
+        for o in range(NR):
+            lo = NR * S * r + S * o
+            act(c2("xw", lo, lo + CAP), one(CAP), scale=col("tm"))
+    for lo in range(NR * S, RO * NR * S, S):
+        fill(c2("yr", lo, lo + S), 0.0)
 
-    def late():
-        tag[0] = "l"
-        ts(a("tri"), c2("io_", 0, 16), col("p16"), Op.is_gt)
-        ts(col("jp1"), col("p16"), 1.0, Op.add)
-        ts(col("eb"), col("p16"), -LN4, Op.mult)
-        ts(col("cadd"), col("p16"), 15.0, Op.is_lt, 128.0, Op.mult)
-        ts(ed("RX"), a("r4"), -8.0, Op.add, col("p"), Op.is_equal)
-        act(ed("RW"), ed("BD"), scale=8.0)
-        act(ed("GW"), ed("BD"), scale=-0.5)
-        tt(ed("BDH"), ed("GW"), ed("I"), Op.add)
-        if PACK:
-            ts(pi(6), pi(0), 1, Op.bitwise_and)
-            ts(col("ev"), pi(6), -256.0, Op.mult, 256.0, Op.add)
-            ts(col("pm"), pi(6), 2.0, Op.mult, -1.0, Op.add)
-            act(ed("I4"), ed("I"), scale=4096.0)
-            ts(a("d16"), ed("I"), col("pm"), Op.mult)
-            ts(a("ed", ED["GW"], slice(0, 128, 2)), c2("g16", 0, 128, 2), col("g16"), Op.is_equal, 127.5 / 4096, Op.mult)
-            ts(a("ed", ED["GW"], slice(1, 128, 2)), c2("g16", 1, 128, 2), col("g16"), Op.is_equal, 128.0, Op.mult)
-            mset(a("z2"), 0.0)
-            tt(c2("z2", 0, 143), a("zz", 0, slice(0, 143)), a("zz", 0, slice(1, 144)), Op.add)
-            act(a("z2"), a("z2"), scale=1.0 / 4096)
-        act(ed("NS4"), ed("BD"), scale=eye(EN, 4))
-        for k in range(16):
-            if k % 2:
-                ts(a("et", k), zv(1, k), c2("tri", k, k + 1), Op.mult)
-            else:
-                act(a("et", k), zv(1, k), scale=c2("tri", k, k + 1))
-        act(a("zz", 3), a("zz", 0), scale=col("jp1"))
-        mset(a("ed", slice(ED["RX"], ED["RW"] + 1), slice(15, 128, 16)), 0.0)
-        for r in range(1, RO):
-            for o in range(NR):
-                lo = NR * S * r + S * o
-                act(c2("xw", lo, lo + CAP), c2("one", 0, CAP), scale=col("tm"))
+    ftw = a("ftab")
+    lk = lambda r, lo, n: cn("lk", 80 * r + lo, n)
+    YB, WB = ("pH", "pB"), ("pF", "pE")
+    yblk = lambda r, i, lo=0, n=CAP: (cn("yr", NR * S * r + S * rank + lo, n) if turn[i] == rank
+                                      else cn("yb", 256 * r + CAP * i + lo, n))
+    turns = [1]
 
-    for lo in range(NR * S, RO * NR * S, 2 * S):
-        mset(c2("yr", lo, lo + 2 * S), 0.0)
-    late()
+    def pack():
+        for j in range(8):
+            mm(cn("pF", 64 * j, 64), [(ed("I"), c2("ftab", 2 * j, FC, 16)), (ed("I4"), c2("ftab", 2 * j + 1, FC, 16))])
+        act(a("f2"), a("pF"), bias=-127.5 - 128.0 * 4096)
 
-    half = lambda nm, h: a(nm, slice(8 * h, 8 * h + 8))
-    ftw = c2("ftab", 0, FC + 32)
-    kw = lambda r, lo, hi, st=1: c2("kw", 32 * r + lo, 32 * r + hi, st)
-    lk = lambda r, lo, hi: c2("lk", 48 * r + lo, 48 * r + hi)
-    tmp = lambda i: c2("tmp", 16 * i, 16 * i + 16)
+    def index(r, lo, n):
+        tag[0] = "i%d%d" % (r, lo // 64)
+        x0, u, m, v0 = 256 * r + lo, lo // 128, n // 4, 3 * lo // 2
+        X, Y, y0, t0 = cn("xl", x0, n), YB[u], 192 * (lo + n == 192), lo // 2
+        form = lambda out, k: mm(out, [(zk(k, l), c2("xl", x0 + l, x0 + n, 4)) for l in range(4)])
+        form(cn("pA", v0, m), "Vc")
+        form(cn("pA", v0 + m, m), "Vb")
+        mm(cn("pA", v0 + 2 * m, n), [(eg("VW"), X)])
+        for i, k in enumerate(("Uc", "Ub", "Lc", "Lb")):
+            form(cn(Y, y0 + m * i, m), k)
+        mm(cn(Y, y0 + n, n), [(eg("UW"), X)])
+        act(cn("va", v0, 2 * m), cn("pA", v0, 2 * m), scale=2.0, bias=col("bva"))
+        act(cn("va", v0 + 2 * m, n), cn("pA", v0 + 2 * m, n), scale=col("sw"), bias=col("bw"))
+        tt(cn("ra", t0, 2 * m), cn(Y, y0, 2 * m), cn("va", v0, 2 * m), Op.mult)
+        tt(cn("tsw", t0, 2 * m), cn(Y, y0 + 2 * m, 2 * m), cn("ra", t0, 2 * m), Op.add)
+        ts(cn("ti", t0, m), cn("tsw", t0, m), 2, Op.logical_shift_right, WC - 1, Op.bitwise_and)
+        cp(cn("of1", lo // 4, m), cn("ti", t0, m))
+        tt(cn("wq", lo, n), cn(Y, y0 + n, n), cn("va", v0 + 2 * m, n), Op.mult)
+        ts(cn("ti", t0 + m, m), cn("tsw", t0 + m, m), 2, Op.logical_shift_right, 63, Op.bitwise_and)
+        cp(cn("b0", lo // 4, m), cn("ti", t0 + m, m))
+        tag[0] = "j%d%d" % (r, lo // 64)
+        w0 = 4 * (lo % 128)
+        for s in range(4):
+            mm(c2("pG", s, 4 * n, 4), [(a("rp", 4 + s), cn("wq", lo, n))])
+        for s in range(4):
+            mm(c2(WB[u], w0 + s, w0 + 4 * n, 4), [(a("rp", s), cn("wq", lo, n))])
+        act(cn("wcd", 4 * lo, 4 * n), cn("pG", 0, 4 * n))
+        for o in range(4 * lo, 4 * (lo + n), 256):
+            (cp if VM[o // 256] else act)(cn("mg", o, 256), ind(mwin, cn("of1", o // 16, 16)))
+        po = cn(Y, y0 + 2 * n, n)
+        mms([(po, eg("CB"), X)]
+            + [(c2(Y, y0 + 2 * n + l, y0 + 3 * n, 4), eg("EB%d" % l), cn("b0", lo // 4, m)) for l in range(4)]
+            + [(po, eg("S%d" % kk), c2("mg", 4 * lo + kk, 4 * (lo + n), 4)) for kk in range(4)])
+        cp(cn("of2", lo, n), po)
 
-    def index(r):
-        al = slice(None)
+    rows = {}
 
-        def front(u):
-            tag[0] = "i%d%d" % (r, u)
-            X = a("xl", slice(8 * r + 4 * u, 8 * r + 4 * u + 4))
-            p3 = lambda nm, h0: a(nm, slice(8 * h0 + 4 * u, 8 * h0 + 4 * u + 4))
-            h2 = lambda nm, k=0: c2(nm, 256 * k + 128 * u, 256 * k + 128 * u + 128)
+    def row(k):
+        if k in rows:
+            ops[-1]["after"].append(rows[k])
+        rows[k] = len(ops) - 1
 
-            def swapped(nm, h0, m):
-                for g2 in range(2):
-                    out = a(nm, slice(8 * h0 + 4 * u, 8 * h0 + 4 * u + 4), slice(16 * g2, 16 * g2 + 16))
-                    mm(out, [(a("ea", 2 * m + g2, slice(16 - 16 * (h - g2), 144 - 16 * (h - g2))),
-                              a("xl", slice(8 * r + 4 * u, 8 * r + 4 * u + 4), slice(16 * h, 16 * h + 16))) for h in range(2)])
-            swapped("pB", 0, 1)
-            swapped("pA", 0, 0)
-            swapped("pA", 1, 2)
-            act(h2("va"), p3("pB", 0), scale=2.0, bias=col("bva"))
-            mm(h2("pD", 1), [(eg("VW"), X)])
-            mm(h2("pD"), [(eg("UW"), X)])
-            mm(h2("pC"), [(eg("UB"), X)])
-            mm(h2("pC", 1), [(eg("LB"), X)])
-            mm(p3("pB", 1), [(ed("VB"), X)])
-            act(h2("va", 2), h2("pD", 1), scale=col("sw"), bias=col("bw"))
-            act(h2("va", 1), p3("pB", 1), scale=2.0, bias=col("bvb"))
-            tt(h2("ra"), p3("pA", 0), h2("va"), Op.mult)
-            tt(h2("tsw"), p3("pA", 1), h2("ra"), Op.add)
-            lb = slice(8 * u, 8 * u + 8)
-            o, i = a("tw", lb), h2("tsw")
-            add("V", lambda: V.transpose(o["ap"], i["ap"]), [o], [i], 128 * CY)
-            ts(a("ti", lb), a("tw", lb, slice(0, 5)), 2, Op.logical_shift_right, WC - 1, Op.bitwise_and)
-            for kk in range(4):
-                cp(c2("of1", 32 * u + 8 * kk, 32 * u + 8 * kk + 8), a("ti", lb, kk))
-            tt(h2("wq"), h2("pD"), h2("va", 2), Op.mult)
-            tt(h2("rbb"), h2("pC"), h2("va", 1), Op.mult)
-            tt(h2("tb"), h2("pC", 1), h2("rbb"), Op.add)
-            ts(h2("tb2"), h2("tb"), 1008, Op.bitwise_and)
-            cp(h2("b16"), h2("tb2"))
-
-        def rest(u):
-            tag[0] = "j%d%d" % (r, u)
-            h2 = lambda nm: c2(nm, 128 * u, 128 * u + 128)
+    def value(r, i):
+        lo, u = 64 * i, i // 2
+        for z, (w, n) in enumerate(VL[min(r, 1)][i]):
+            tag[0] = "v%d%d%d" % (r, i, z)
+            hi, bank = lo + w, ("pC", "pD")[turns[0] % 2]
+            turns[0] += 1
+            if n:
+                ts(cn("vv", 16 * lo, 16 * n), ind(ftw, cn("of2", lo, n)), -128.0, Op.add)
+            for l in range(lo + n, hi, 32):
+                h = min(l + 32, hi)
+                act(c2("vv", 16 * l, 16 * h), ind(ftw, c2("of2", l, h)), bias=-128.0)
+                row("S")
             for s in range(4):
-                mm(c2(("pG", "pH")[u], 128 * s, 128 * s + 128), [(ed("REP%d" % (4 + s)), h2("wq"))])
-                mm(c2(("pE", "pF")[u], 128 * s, 128 * s + 128), [(ed("REP%d" % s), h2("wq"))])
-            act(a("wcd", u), a(("pG", "pH")[u]))
-            for h in range(2):
-                o = 512 * u + 256 * h
-                (act, cp if VM > u else act)[h](c2("mg", o, o + 256), ind(mwin, c2("of1", o // 16, o // 16 + 16)))
-            po = a("pB", slice(8 + 4 * u, 12 + 4 * u))
-            mm(po, [(ed("I"), h2("b16"))]
-               + [(eg("S%d" % kk), c2("mg", 512 * u + 128 * kk, 512 * u + 128 * kk + 128)) for kk in range(4)])
-            cp(h2("of2"), po)
+                tt(a("pp", slice(lo, hi), slice(s, 16, 4), tag=s), c2("vv", 16 * lo + s, 16 * hi, 4),
+                   cn(WB[u], 4 * (lo % 128), 4 * w), Op.mult)
+                row("V")
+            mm(cn(bank, 0, 4 * w), [(ed("I"), a("pp", slice(lo, hi), slice(4 * kk, 4 * kk + 4))) for kk in range(4)])
+            tt(cn("qq", 4 * lo, 4 * w), cn(bank, 0, 4 * w), cn("wcd", 4 * lo, 4 * w), Op.mult)
+            py = cn(bank, 256, w)
+            mm(py, [(ed("CY"), cn("xl", 256 * r + lo, w))] + [(a("i32"), c2("qq", 4 * lo + s, 4 * hi, 4)) for s in range(4)])
+            ts(yblk(r, i, lo % 64, w), py, MAGIC + 128.0, Op.add, MAGIC, Op.subtract)
+            lo = hi
+        if turn[i] != rank:
+            send_one("y%d" % r, turn[i], yblk(r, i), cn("yr", NR * S * r + S * turn[i], CAP))
 
-        front(1)
-        front(0)
-        rest(0)
-        rest(1)
-        tag[0] = "k%d" % r
-        tt(tmp(0), a("ti", al, 4), a("tw", al, 7), Op.add)
-        tt(kw(r, 0, 16), tmp(0), c2("dmp", 0, 16), Op.min)
-        cp(lk(r, 0, 16), kw(r, 0, 16))
-        cp(lk(r, 16, 24), kw(r, 1, 16, 2))
-        ts(a("bw"), a("tw", al, 5), 1008, Op.bitwise_and)
-        cp(a("sid"), a("tw", al, 6))
+    def star(r, u):
+        tag[0] = "k%d%d" % (r, u)
+        x0, s0, p0 = 256 * r + 128 * u, 128 + 32 * u, 384 + 32 * u
+        form = lambda out, k: mm(out, [(zk(k, l), c2("xl", x0 + l, x0 + 128, 4)) for l in range(4)])
+        form(cn("pA", p0, 32), "Vs")
+        form(cn("pH", p0, 32), "Us")
+        form(cn("pH", p0 + 64, 32), "Ls")
+        act(cn("va", p0, 32), cn("pA", p0, 32), scale=2.0, bias=col("bva"))
+        tt(cn("ra", s0, 32), cn("pH", p0, 32), cn("va", p0, 32), Op.mult)
+        tt(cn("tsw", s0, 32), cn("pH", p0 + 64, 32), cn("ra", s0, 32), Op.add)
+        ts(cn("ti", 128 + 64 * u, 32), cn("tsw", s0, 32), 2, Op.logical_shift_right, WC - 1, Op.bitwise_and)
+        ts(cn("ti", 160 + 64 * u, 32), cn("tsw", s0, 32), 2, Op.logical_shift_right, 63, Op.bitwise_and)
+        ts(cn("st", 64 * u, 64), cn("ti", 128 + 64 * u, 64), col("cen"), Op.subtract)
+        mms([(cn("pB", p0, 32), ed("I"), cn("cst", 32 * u, 32))]
+            + wrap(p0, "i", u, 0) + wrap(p0 + 8, "d", u, 0) + wrap(p0 + 16, "s", u, 0) + wrap(p0 + 24, "b", u, 1))
+        cp(lk(r, 32 * u, 32), cn("pB", p0, 32))
+        ts(a("kh", slice(0, 2), slice(8 * u, 8 * u + 8)), cn("pB", p0, 16), -2048.0, Op.add)
+        tag[0] = "g%d%d" % (r, u)
+        h = lambda nm: cn(nm, 128 * u, 128)
+        act(h("tgl"), ind(a("ta"), lk(r, 32 * u + 16, 8)))
+        for j in range(VJ[u], 8):
+            act(cn("v3", 256 * j + 128 * u, 128), ind(cn("f2", 64 * j, 64), lk(r, 32 * u + 24, 8)))
+        if r < RO - 1:
+            act(h("cg"), ind(a("ctab"), lk(r, 32 * u, 8)))
+        else:
+            act(h("yg"), ind(a("ycw"), lk(r, 32 * u, 8)))
+        tag[0] = "h%d%d" % (r, u)
+        act(h("ms"), ind(mwin, lk(r, 32 * u, 8)))
 
-    def value(r):
-        al = slice(None)
-        yb = lambda lo, hi: c2("yb", 256 * r + lo, 256 * r + hi)
-        base = NR * S * r
-        land = lambda q: c2("yr", base + S * q, base + S * q + CAP)
-        for i in range(NR):
-            lo, hi = 64 * i, 64 * i + 64
-            if i == 0 and VL:
-                ts(c2("vv", 16 * lo, 16 * (lo + VL)), ind(ftw, c2("of2", lo, lo + VL)), -128.0, Op.add)
-                lo += VL
-            if hi > lo:
-                act(c2("vv", 16 * lo, 16 * hi), ind(ftw, c2("of2", lo, hi)), bias=-128.0)
-        for i, (lo, n) in enumerate(PC):
-            u, sums, py = lo // 128, ("pC", "pD")[i % 2], c2(("pG", "pH")[i % 2], 0, n)
-            pp = lambda k: c2("pp", 16 * lo + n * k, 16 * lo + n * k + n)
-            for s in range(4):
-                for kk in range(4):
-                    o = 128 * kk + lo % 128
-                    tt(pp(4 * s + kk), c2("vv", 16 * lo + 4 * s + kk, 16 * (lo + n), 16), c2(("pE", "pF")[u], o, o + n), Op.mult)
-                mm(c2(sums, n * s, n * s + n), [(a("i16"), pp(4 * s + kk)) for kk in range(4)])
-            tt(c2("qq", 4 * lo, 4 * lo + 4 * n), c2(sums, 0, 4 * n), a("wcd", u, al, slice(lo % 128, lo % 128 + n)), Op.mult)
-            mm(py, [(ed("CY"), a("xl", slice(8 * r + lo // 32, 8 * r + (lo + n) // 32)))]
-               + [(a("i32"), c2("qq", 4 * lo + n * s, 4 * lo + n * s + n)) for s in range(4)])
-            ts(yb(lo, lo + n), py, MAGIC + 128.0, Op.add, MAGIC, Op.subtract)
-            for c in range(lo // 64, (lo + n) // 64):
-                if turn[c] == rank:
-                    cp(land(rank), yb(64 * c, 64 * c + 64))
-                else:
-                    send_one("y%d" % r, turn[c], yb(64 * c, 64 * c + 64), land(turn[c]))
+    wrap = lambda lo, k, u, h: [(cn("pB", lo, 8), zw(k, n), c2("st", 64 * u + 32 * h + n, 64 * u + 32 * h + 32, 4)) for n in range(4)]
 
-    def dedupe(r, t):
-        key = kw(r, 16 * t, 16 * t + 16)
-        act(c2("kr", 384 * t, 384 * t + 384), ind(a("iot"), lk(r, 24 * t, 24 * t + 24)))
-        tt(a("eq", t), ind(key, a("ld")), c2("kr", 384 * t, 384 * t + 384), Op.is_equal)
-        if t == 0:
-            return
-        al = slice(None)
-        for k in range(16):
-            mm1(c2("pG", 0, 32), a("et", k), a("eq", al, slice(k, 256, 16)), k == 0, False)
-        for k in range(16):
-            mm1(c2("pG", 1, 32, 2), zv(1, k), a("eq", al, slice(256 + k, 384, 16)), False, k == 15)
-        t1, t2 = c2("tmp", 48, 80), c2("tmp", 80, 112)
-        tt(t1, c2("pG", 0, 32), kw(r, 0, 32), Op.add)
-        tt(t2, t1, a("dmp"), Op.min)
-        cp(c2("lo", 32 * r, 32 * r + 32), t2)
-
-    def early(r):
-        al = slice(None)
-        act(a("ms"), ind(mwin, lk(r, 0, 16)))
-        tt(tmp(1), a("bw"), a("tw", al, 7), Op.add)
-        for i, q in enumerate(turn):
-            act(c2("tgl", CAP * i, CAP * i + CAP), ind(c2("ta", S * q, S * q + S), c2("sid", 4 * i, 4 * i + 4)))
-        act(c2("cg", 256 * r, 256 * r + 256), ind(a("ctab"), lk(r, 0, 16)))
-        if PACK:
-            mm(a("pA"), [(ed("I"), c2("ftab", 0, FC, 2)), (ed("I4"), c2("ftab", 1, FC, 2))])
-            act(a("f2"), a("pA"), bias=-127.5 - 128.0 * 4096)
-            ts(a("bw8"), a("tw", al, 5), 1, Op.logical_shift_right, 504, Op.bitwise_and)
-            tt(c2("ofu", 0, 128), ind(a("bw8"), c2("lx", 0, 8)), c2("jj", 0, 128), Op.add)
-            cp(c2("ou", 0, 128), c2("ofu", 0, 128))
-            for i in range(NR):
-                act(c2("v3", 512 * i, 512 * i + 512), ind(a("f2"), c2("ou", 32 * i, 32 * i + 32)))
-
-    def train(r):
-        last = r == RO - 1
-        pg, pu = c2("pE", 256, 512), half("pB", 0)
-        cg, uu = c2("cg", 256 * r, 256 * r + 256), c2("uu", 256 * r, 256 * r + 256)
-        n, w = 16 * LB, LB // 2
-        for c in range(16 // LB):
-            lo, d, sg = n * c, a("pA", slice(w * c, w * c + w)), a("pA", slice(8 + w * c, 8 + w * c + w))
-            mm(d, [(ed("I"), c2("tgl", lo, lo + n)), (ed("NI"), c2("yb", 256 * r + lo, 256 * r + lo + n))])
-            act(sg, d, AF.Sign)
-            for j in range(8):
-                o = 8 * lo + n * j
-                tt(c2("gw", o, o + n), c2("v3", o, o + n), sg, Op.mult)
-                mm1(a("pB", slice(w * c, w * c + w)), c2("z2", 14 - 2 * j, 142 - 2 * j), c2("gw", o, o + n), j == 0, j == 7)
-        act(a("gs"), half("pA", 0), AF.Sign)
-        al = slice(None)
+    def dedupe(r):
         tag[0] = "d%d" % r
-        mm(c2("pE", 0, 16), [(zv(2, k), c2("ms", k, 256, 16)) for k in range(16)])
-        tt(tmp(2), c2("pE", 0, 16), tmp(1), Op.add)
-        tt(kw(r, 16, 32), tmp(2), c2("dmp", 16, 32), Op.min)
-        cp(lk(r, 24, 40), kw(r, 16, 32))
-        cp(lk(r, 40, 48), kw(r, 17, 32, 2))
-        act(a("fg"), ind(ftw, lk(r, 24, 40)))
-        dedupe(r, 0)
-        dedupe(r, 1)
-        mm(c2("pG", 256, 512), [(ed("I"), a("fg")), (ed("I"), a("gs"))])
-        ts(a("fn"), c2("pG", 256, 512), 0.0, Op.max, 255.0, Op.min)
-        tag[0] = "u%d" % r
-        act(a("zc"), pu, scale=col("ev"))
-        ts(a("hi"), pu, MAGIC, Op.add, MAGIC, Op.subtract)
-        pu = c2("pF", 0, 256)
-        mm(pu, [(ed("GW"), a("gs")), (a("i32"), a("zc")), (a("d16"), a("hi"))])
-        act(uu, pu, AF.Sign)
+        mms([(cn("pB", 480, 16), zv(2, k), c2("ms", k, 256, 16)) for k in range(16)] + wrap(480, "b16", 0, 1) + wrap(488, "b16", 1, 1))
+        cp(a("kh", 2), cn("pB", 480, 16))
+        cp(lk(r, 64, 16), cn("pB", 480, 16))
+        act(a("fg"), ind(ftw, lk(r, 64, 16)))
+        tag[0] = "e%d" % r
+        keys = lambda z=al: a("kh", slice(0, 3, 2), z)
+        mmg([[(c2("pA", k, 512, 16), a("rk", k), keys())] for k in range(16)])
+        ts(c2("eq", 0, 512), a("pA"), 0.0, Op.is_equal)
+        out = cn("pB", 448, 32)
+        parts = ([(out, ed("I"), keys()), (out, ed("I"), c2("cst", 64, 96))]
+                 + [(cn("pB", 448 + 16 * t, 16), ed("I"), a("kh", 1)) for t in range(2)]
+                 + [(out, a("et", k), c2("eq", k, 512, 16)) for k in range(16)])
+        if CH == 16:
+            mms(parts)
+            for t in range(2):
+                ts(c2("lo", 64 * r + 32 * t, 64 * r + 32 * t + 32, 2), cn("pB", 448 + 16 * t, 16), col("dm%d" % t), Op.min)
+            return
+        for h in range(0, 16, 4):
+            odd, even = keys(slice(1, 16, 2)), keys(slice(0, 16, 2))
+            mmg([[(c2("pG", 256 + k, 512, 16), l, x) for l, x in ((a("rp", k), odd), (ed("NI"), even))]
+                 for k in range(h, h + 4)])
+        ts(c2("eq", 512, 768), c2("pG", 256, 512), 0.0, Op.is_equal)
+        mms(parts + [(c2("pB", 449, 480, 2), zv(1, k), c2("eq", 512 + k, 768, 16)) for k in range(16)])
+        tt(a("tmp"), out, a("dmp"), Op.min)
+        cp(cn("lo", 64 * r, 32), a("tmp"))
 
-        def scat(win, t, fn):
-            tag[0] = "w%d%s" % (r, win["reg"][0][0])
-            for k in [2 * turn.index(q) + z for q in range(NR - 1, -1, -1) for z in (1, 0)]:
-                o = 32 * r + 16 * t + 2 * k
-                fn(ind(win, c2("lo", o, o + 2)), 32 * k, 32 * k + 32)
-        scat(ftw, 1, lambda w, lo, hi: cp(w, c2("fn", lo, hi)))
-        scat(a("ctab"), 0, lambda w, lo, hi: tt(w, c2("cg", 256 * r + lo, 256 * r + hi), c2("uu", 256 * r + lo, 256 * r + hi), Op.add))
+    def signs(r, u):
+        tag[0] = "t%d%d" % (r, u)
+        d, sg = cn("pE", 256 * u, 128), cn("pE", 256 * u + 128, 128)
+        mms([(d, ed("I"), cn("tgl", 128 * u, 128))]
+            + [(cn("pE", 256 * u + 64 * z, 64), ed("NI"), yblk(r, 2 * u + z)) for z in range(2)])
+        act(cn("gs", 128 * u, 128), d, AF.Sign)
+        act(sg, d, AF.Sign)
+        for j in range(8):
+            o = 256 * j + 128 * u
+            if j < VJ[u]:
+                tt(cn("gw", o, 128), ind(cn("f2", 64 * j, 64), lk(r, 32 * u + 24, 8)), cn("gs", 128 * u, 128), Op.mult)
+            else:
+                tt(cn("gw", o, 128), cn("v3", o, 128), sg, Op.mult)
+            mm(c2(YB[u], j, 64, 8), [(cn("gw", o, 128), a("gq"))])
+
+    def train(r, u):
+        tag[0] = "u%d%d" % (r, u)
+        Y, h = YB[u], lambda nm: cn(nm, 128 * u, 128)
+        hi, lo = c2("zc", 128 * u + 1, 128 * u + 128, 2), c2("zc", 128 * u, 128 * u + 128, 2)
+        ts(hi, cn(Y, 0, 64), MAGIC, Op.add, MAGIC, Op.subtract)
+        tt(lo, cn(Y, 0, 64), hi, Op.subtract)
+        mm(cn(Y, 128, 128), [(ed("GW"), h("gs")), (h("zc"), a("i32"))])
+        act(h("uu"), cn(Y, 128, 128), AF.Sign)
+        if r == RO - 1:
+            mm(cn(Y, 256, 128), [(zv(3, 0), h("uu"))])
+            act(cn("yg", 256 + 128 * u, 128), cn(Y, 256, 128))
+            return
+        old = [(ed("NS4"), h("ms"))] if r == 0 else [(eg("NSU"), h("ms")), (eg("US"), h("su"))]
+        mm(cn(Y, 256, 128), [(ed("I"), h("cg"))] + old + [(ed("I"), h("uu"))])
+        act(h("ee"), cn(Y, 256, 128), AF.Exp, scale=16 * LN4, bias=col("eb"))
+        mm(cn(Y, 128, 128), [(ed("BDH"), h("ee"))])
+        act(h("ohm"), cn(Y, 128, 128), AF.Sign)
+        keep = [(eg("S4"), h("ms")), (eg("PKU"), h("uu"))] if r == 0 else [(eg("S4D"), h("ms"))]
+        mm(cn(Y, 256, 128), keep + [(zv(3, 13 + r), h("uu")), (eg("JW"), h("ohm"))])
+        act(h("mn"), cn(Y, 256, 128), bias=col("e60"))
+
+    def scat(r, win, t, fn):
+        tag[0] = "w%d%s" % (r, win["reg"][0][0])
+        n = 64 // CH
+        for k in [n * turn.index(q) + z for q in range(NR - 1, -1, -1) for z in range(n - 1, -1, -1)]:
+            o = 64 * r + 8 * n * t + 2 * k
+            fn(ind(win, cn("lo", o, CH // 16)), CH * k, CH * k + CH)
+
+    pack()
+    for r in range(RO):
+        last = r == RO - 1
+        if r == 0 or MS == 0:
+            index(r, 128, 128)
+        else:
+            index(r, 192, 64)
+            index(r, 128, 64)
+        tag[0] = "y%d" % r
+        if last:
+            mm(cn("pF", 0, 256), [(ed("I"), cn("mq", 256 * q, 256)) for q in range(2)])
+            tt(c2("yo", 256, 512), cn("pF", 0, 256), c2("yo", 0, 256), Op.add)
+            dma("Y", a("ycw", slice(0, WC), part=slice(0, 128, 16)), c2("yo", 256, 512), mb=0.13)
+        star(r, 1)
+        index(r, 0, 128)
+        star(r, 0)
+        for i in ((3, 2, 0, 1) if r else (0, 1, 2, 3)):
+            value(r, i)
+        dedupe(r)
+        signs(r, 1)
+        signs(r, 0)
+        tag[0] = "f%d" % r
+        if r == 1:
+            mm(cn("pF", 256, 256), [(eg("PV"), a("ms"))])
+            act(a("su"), cn("pF", 256, 256), AF.Sign, bias=col("sb"))
+        mm(cn("pF", 256, 256), [(ed("I"), a("fg")), (ed("I"), a("gs"))])
+        row("F")
+        ts(a("fn"), cn("pF", 256, 256), 0.0, Op.max, 255.0, Op.min)
+        if r == 0:
+            tag[0] = "y0"
+            for q in range(16):
+                mmg([[(cn("pF", 0, 256), zv(3, q), cn("ctab", 256 * q, 256))]], q == 0, q == 15)
+                row("F")
+            act(c2("yo", 0, 256), cn("pF", 0, 256))
+        train(r, 1)
+        train(r, 0)
+        scat(r, ftw, 1, lambda w, lo, hi: cp(w, c2("fn", lo, hi)))
         source(r + 1)
         tag[0] = "m%d" % r
         if last:
             dma("S", T.yf[:], c2("ftab", 0, FC), mb=0.26)
-            mm(c2("pC", 0, 256), [(zv(3, q), c2("ctab", 256 * q, 256 * q + 256)) for q in range(16)])
-            act(a("yo"), c2("pC", 0, 256))
-            dma("Y", T.yc[:], a("yo"), mb=0.13)
-            return
-        mm(c2("pF", 256, 512), [(ed("I"), cg), (ed("NS4"), a("ms")), (ed("I"), uu)])
-        act(a("ee"), c2("pF", 256, 512), AF.Exp, scale=16 * LN4, bias=col("eb"))
-        mm(pg, [(ed("BDH"), a("ee"))])
-        act(a("ohm"), pg, AF.Sign)
-        mm(c2("pF", 0, 256), [(eg("S4"), a("ms")), (eg("JW"), a("ohm"))])
-        act(a("mn"), c2("pF", 0, 256), bias=eye(E60, 0))
-        scat(mwin, 0, lambda w, lo, hi: cp(w, c2("mn", lo, hi)))
+            scat(r, a("ycw"), 0, lambda w, lo, hi: tt(w, c2("yg", lo, hi), c2("yg", 256 + lo, 256 + hi), Op.add))
+            dma("Y", T.yc[:], a("ycw", slice(0, WC), part=slice(0, 128, 16)), mb=0.13)
+            break
+        dma("Y", c2("ftab", FC, DF), c2("ftab", 0, FX), mb=0.2)
+        pack()
+        scat(r, mwin, 0, lambda w, lo, hi: cp(w, c2("mn", lo, hi)))
         for s in range(1, 4):
             sh = SHIFTS[s]
             dma("YSY"[s - 1], mrow(s, PAD, PAD + WC - sh), mrow(0, PAD + sh, PAD + WC), new=s == 1, mb=0.065)
             dma("SYS"[s - 1], mrow(s, PAD + WC - sh, PAD + WC), mrow(0, PAD, PAD + sh), new=False, mb=0.0)
-
-    for r in range(RO):
-        for k, f in enumerate((index, early, value, train)):
-            tag[0] = "p%d%d" % (k, r)
-            f(r)
+        tag[0] = "y%d" % r
+        if r == 1:
+            for q in range(2):
+                dma("Y", cn("mq", 256 * q, 256), mrow(13 + q, PAD, PAD + WC), new=q == 0, mb=0.065)

import math
from concourse.bass import DstId, RemoteDMATransfer
from concourse.mybir import AluOpType as Op, ActivationFunctionType as AF

S, CAP, WC, FC, RO, NR = 160, 64, 4096, 1024, 3, 4
SHIFTS = (0, 47, 229, 276)
PAD = 288
FX = 768
DC, DF = WC, FC + FX
WT = DC + 32
MAGIC = 12582912.0
LN4 = math.log(4.0)
VL = ((((64, 0),), ((64, 16),), ((64, 16),), ((64, 0),)),) * 2
VM = (0, 1, 0, 0)
TQ = "S"
VJ = (0, 0)
CY, WAKE, GAT, SCA, HOP = 0.85e-3, 0.25, 1.45, 3.6, 4.8
MARK, EF = (), {}
SEED, HEAT, MU, LOG, FB, STEP, BACK = 1, 0.15, 1.0, [], 2, 6.0, 50
ADD, ADDP, PEF = 0.0, 0.0, 0.75
BLEND, SPAN, PRIO, WAW, CH, MS, MZ = 4000, [0.0], {}, True, 32, 2, 4

sb = lambda shape, d: ("sbuf", shape, d)
ps = lambda shape: ("psum", shape, "float32")
B, F, I, U, H = "bfloat16", "float32", "int32", "uint16", "float16"
SCRATCH = {
    "mt": sb([128, PAD + WT], B), "ct": sb([128, WC], B), "ctab": sb([128, WC], B), "ftab": sb([128, DF + 32], B),
    "ycw": sb([128, WT], F),
    "ta": sb([128, NR * S], B), "xw": sb([128, RO * NR * S], B), "xl": sb([128, RO * 256], B),
    "yr": sb([128, RO * NR * S], B), "yb": sb([128, RO * 256], B), "rb": sb([128, S + 2 * RO * CAP], B),
    "io_": sb([128, S], F), "pint": sb([128, 16], I), "g16": sb([128, 128], B),
    "r4": sb([128, 128], B), "cc": sb([128, 64], F), "pa": sb([128, 16], F), "eye": sb([128, 4, 16], F),
    "gm": sb([128, 8], F), "one": sb([128, 256], B), "tri": sb([128, 16], F), "kc": sb([128, 2, 256], B),
    "kz": sb([128, 9, 4], B), "zk": sb([128, 9, 140], B), "kw": sb([128, 5, 4], B), "zw": sb([128, 5, 140], B),
    "kg": sb([128, 18, 16], B), "eg": sb([128, 18, 128], B), "pk": sb([128, 16, 16], B), "rk": sb([128, 16, 128], B), "rp": sb([128, 16, 128], B),
    "ed": sb([128, 21, 128], B), "et": sb([128, 16, 128], B), "zz": sb([128, 5, 144], B), "z16": sb([128, 144], B),
    "i32": sb([128, 128], F), "q4": sb([128, 64], I),
    "dmp": sb([128, 32], F), "cst": sb([128, 96], B),
    "x0i": sb([128, S], I), "xp": sb([128, (RO + 1) * S], B), "xq": sb([128, S], B), "clp": sb([128, S], B),
    "th": sb([128, S], B), "cum": sb([128, S], H),
    "prd": sb([128, S], H), "wt": sb([128, S], B), "sl": sb([128, RO * 16], U), "acc": sb([128, RO * S], F),
    "xf": sb([128, S], F),
    "mx": sb([128, 512], F), "ki": sb([128, 256], I), "k2": sb([128, 512], I), "mq": sb([128, 512], B),
    "va": sb([128, 448], F), "ra": sb([128, 192], F), "tsw": sb([128, 192], I), "ti": sb([128, 256], I),
    "of1": sb([128, 64], U), "b0": sb([128, 64], B), "st": sb([128, 128], H),
    "wq": sb([128, 256], B), "wcd": sb([128, 1024], B),
    "mg": sb([128, 1024], B), "ms": sb([128, 256], B), "of2": sb([128, 256], U),
    "vv": sb([128, 4096], B), "pp": sb([128, 256, 16], H), "qq": sb([128, 1024], F),
    "tmp": sb([128, 32], F), "lk": sb([128, RO * 80], U), "kh": sb([128, 3, 16], H),
    "tgl": sb([128, 256], B), "eq": sb([128, 768], B), "lo": sb([128, RO * 64], U),
    "gs": sb([128, 256], B), "uu": sb([128, 256], B), "su": sb([128, 256], B),
    "f2": sb([128, 512], F), "v3": sb([128, 2048], F), "gw": sb([128, 2048], F),
    "zc": sb([128, 256], F), "gq": sb([128, 8], F),
    "cg": sb([128, 256], B), "fg": sb([128, 256], B), "fn": sb([128, 256], B), "ee": sb([128, 256], B),
    "ohm": sb([128, 256], B), "mn": sb([128, 256], B), "yo": sb([128, 512], F), "yg": sb([128, 512], F),
    "pA": ps([128, 512]), "pB": ps([128, 512]), "pC": ps([128, 512]), "pD": ps([128, 512]),
    "pE": ps([128, 512]), "pF": ps([128, 512]), "pG": ps([128, 512]), "pH": ps([128, 512]),
}
MSGS = ["tg"] + [k + str(r) for r in range(RO) for k in "xy"]
SEMAPHORES = (["cV", "cS", "cP", "cG", "sent"] + ["a" + m for m in MSGS] + ["h" + m for m in MSGS]
              + ["b" + m for m in MSGS if m[0] != "y"] + ["d%d" % i for i in range(44)])


def relays(T, topo):
    out = {}
    for q, src in enumerate(T.cores):
        used = []
        for o, dst in enumerate(T.cores):
            if o != q and not topo.may_write(src, dst):
                c = [k for k in topo.cores_of(src) if k not in T.cores and k not in used and topo.may_write(k, dst)]
                c.sort(key=lambda k: topo.die(k) != topo.die(src))
                out[(q, o)] = c[0]
                used.append(c[0])
    return out


def bits(es):
    return sum(1 << e for e in es)


def places(o, rel):
    return sorted(range(NR), key=lambda q: (q == o, (o, q) not in rel))


def landing(T, m, q, o, rel):
    if m == "tg":
        return T.ta[:, S * q:S * q + S]
    r = int(m[1])
    if m[0] == "x":
        i = 256 * r + CAP * places(o, rel).index(q)
        return T.xl[:, i:i + CAP]
    return T.yr[:, NR * S * r + S * q:NR * S * r + S * q + CAP]


def slot(T, m):
    i = MSGS.index(m)
    return T.rb[:, 0:S] if i == 0 else T.rb[:, S + CAP * (i - 1):S + CAP * i]


def relay_program(g, core, T, topo, q, o):
    src, dst = T.cores[q], T.cores[o]
    n = len(topo.engines(core, dst))
    rid, pid = topo.addr(dst, core)
    for m in MSGS:
        g.wait_ge(T.sem["h" + m], n)
        g.remote_dma(landing(T, m, q, o, relays(T, topo)), slot(T, m), T.sem["a" + m], T.sem.sent, pid, rid, topo.mask(core, dst))
    g.wait_ge(T.sem.sent, n * len(MSGS))


def rank_program(g, core, T, topo):
    rel = relays(T, topo)
    rank = T.rank_of(core)
    if rank is None:
        for (q, o), c in rel.items():
            if c == core:
                relay_program(g, core, T, topo, q, o)
        return
    ops = []
    build(g, core, rank, T, topo, rel, ops)
    emit(g, T, ops, rank)


def emit(g, T, ops, rank):
    Q = {"V": g.vector, "S": g.scalar, "P": g.tensor, "G": g, "Y": g.sync}
    hist, group, index = {}, {}, {}
    for n, o in enumerate(ops):
        index[o["key"]] = n
        if o["sem"] is not None:
            group.setdefault(o["sem"], []).append(n)
    for n, o in enumerate(ops):
        e, dep, order = o["e"], set(), set(index[k] for k in o["after"])
        for regs, wr in ((o["r"], False), (o["w"], True)):
            for (nm, lo, hi, tag) in regs:
                for (l2, h2, t2, k, w2) in hist.get(nm, []):
                    p = ops[k]
                    if not (l2 < hi and lo < h2 and (tag is None or t2 is None or tag == t2) and (wr or w2)):
                        continue
                    if p["e"] == e and p["sem"] is None and o["sem"] is None:
                        (order if e == "P" or (wr and not WAW) else dep).add(k)
                    elif p["sem"] is None or p["sem"] != o["sem"]:
                        dep.update([k] if p["sem"] is None else group[p["sem"]])
        o["dep"], o["ord"] = (set() if e == "X" else dep), order - dep
        o["banks"] = set(z[0] for z in o["r"] + o["w"] if SCRATCH[z[0]][0] == "psum")
        if o["sem"] == "sent":
            continue
        for regs, wr in ((o["r"], False), (o["w"], True)):
            for (nm, lo, hi, tag) in regs:
                seen = o["dep"] | o["ord"]
                keep = [z for z in hist.get(nm, []) if not (z[3] in seen and ops[z[3]]["sem"] is None and o["sem"] is None
                                                            and wr and tag is None and lo <= z[0] and z[1] <= hi)]
                hist[nm] = keep + [(lo, hi, tag, n, wr)]
    succ = [[] for o in ops]
    for n, o in enumerate(ops):
        for k in o["dep"] | o["ord"]:
            succ[k].append(n)
    left = [len(o["dep"] | o["ord"]) for o in ops]
    topo_order, stack, cnt0 = [], [n for n in range(len(ops)) if left[n] == 0], list(left)
    while stack:
        n = stack.pop()
        topo_order.append(n)
        for k in succ[n]:
            cnt0[k] -= 1
            if cnt0[k] == 0:
                stack.append(k)
    tail = [0.0] * len(ops)
    for n in reversed(topo_order):
        far = ops[n]["lat"] + ops[n]["mb"] * 5.0
        tail[n] = ops[n]["t"] + max([tail[k] + (far + WAKE if n in ops[k]["dep"] else 0.0) for k in succ[n]] + [far])
    pred = [list(o["dep"] | o["ord"]) for o in ops]

    def plan(prio, back):
        if not back:
            prio = list(prio)
            for n in rev:
                p, d = prio[n], dur[n]
                for k in succ[n]:
                    if p < prio[k] + d:
                        p = prio[k] + d
                prio[n] = p
        at = list(far) if back else [0.0] * len(ops)
        line = {k: ([], []) for k in keys}
        ends, span = [0.0] * len(ops), 0.0

        def gap(key, t, d, pad):
            st, en = line[key]
            hi = n = len(en)
            if not n or en[-1] + pad <= t + 1e-9:
                return t, n
            lo = 0
            while lo < hi:
                mid = (lo + hi) // 2
                if en[mid] + pad <= t + 1e-9:
                    lo = mid + 1
                else:
                    hi = mid
            while lo < n and st[lo] - pad < t + d - 1e-9:
                t = en[lo] + pad
                lo += 1
            return t, lo

        def put(key, t, d):
            i = gap(key, t, d, 0.0)[1]
            line[key][0].insert(i, t)
            line[key][1].insert(i, t + d)

        for n in sorted(range(len(ops)), key=lambda k: -prio[k]):
            t, d = at[n], dur[n]
            look = looks[n]
            i = ok = 0
            while ok < len(look):
                t1 = gap(look[i][0], t, d, look[i][1])[0]
                if t1 > t + 1e-9:
                    t, ok = t1, 0
                ok += 1
                i = (i + 1) % len(look)
            for key in puts[n]:
                put(key, t, d)
            end = ends[n] = t + d
            if back:
                if end > span:
                    span = end
                for k, lag in lags[n]:
                    if at[k] < end + lag:
                        at[k] = end + lag
                continue
            fin = end + ops[n]["lat"]
            if bulk[n]:
                fin = gap("pipe", fin, bulk[n], 0.0)[0]
                put("pipe", fin, bulk[n])
                fin += bulk[n]
            if fin > span:
                span = fin
            for k in hard[n]:
                if at[k] < fin + WAKE:
                    at[k] = fin + WAKE
            for k in soft[n]:
                if at[k] < end:
                    at[k] = end
        return span + MU * sum(ends[n] for n in marks) / len(marks), ends, prio

    rev, dur, bulk = topo_order[::-1], [o["t"] for o in ops], [o["mb"] * 5.0 for o in ops]
    far = [o["lat"] + o["mb"] * 5.0 for o in ops]
    hard = [[k for k in succ[n] if n in ops[k]["dep"]] for n in range(len(ops))]
    soft = [[k for k in succ[n] if n not in ops[k]["dep"]] for n in range(len(ops))]
    lags = [[(k, far[k] + WAKE if k in o["dep"] else 0.0) for k in pred[n]] for n, o in enumerate(ops)]
    looks = [[] if o["e"] == "X" else [(o["e"], 0.0)] + [(b + q, WAKE) for b in o["banks"] for q in "VSP" if q != o["e"]] for o in ops]
    puts = [[] if o["e"] == "X" else [o["e"]] + [b + o["e"] for b in o["banks"]] for o in ops]
    keys = set(k for l in looks for k, pad in l) | {"pipe"}

    marks = [n for n, o in enumerate(ops) if o["e"] != "X" and o["tag"][0] not in "abcly"
             and (o["sem"] is not None or o["w"][0][0] in MARK)]
    if True:
        start = PRIO.get(len(ops), tail)
        turns = BLEND // 4 if len(ops) in PRIO else BLEND
        best = (plan(start, False)[0], start)
        for it in range(FB):
            back = plan(plan(best[1], False)[1], True)[1]
            best = min(best, (plan(back, False)[0], back))
        wide, fine = [o["tag"][:-1] for o in ops], [o["tag"] + (o["w"] or o["r"])[0][0] for o in ops]
        levels = []
        for names in (wide, fine, [x[0] + x[2:] for x in wide], [x[0] + x[2:] for x in fine]):
            kinds = {}
            for n, x in enumerate(names):
                kinds.setdefault(x, []).append(n)
            levels.append([kinds[x] for x in sorted(kinds)])
        state, now = [SEED], best

        def rnd(n):
            state[0] = (state[0] * 1103515245 + 12345) % 2147483648
            return (state[0] >> 8) % n

        for it in range(turns):
            prio = list(now[1])
            for z in range(1 + rnd(2)):
                kinds = levels[rnd(4)]
                d = (rnd(2001) - 1000) / 1000.0
                for n in kinds[rnd(len(kinds))]:
                    prio[n] += STEP * d * abs(d)
            s, en, prio = plan(prio, False)
            if it % BACK == BACK - 1:
                back = [0.7 * x + 0.3 * y for x, y in zip(prio, plan(en, True)[1])]
                s, prio = min((s, prio), (plan(back, False)[0], back))
            if s < now[0] + HEAT * (turns - it) / BLEND:
                now = (s, prio)
            best = min(best, now)
            if it % 200 == 0:
                LOG.append(round(now[0], 1))
        PRIO[len(ops)] = best[1]
    SPAN[0], ends = plan(PRIO[len(ops)], False)[:2]
    seq = sorted(range(len(ops)), key=lambda n: ends[n] - ops[n]["t"])
    SPAN[1:] = [ops, seq, ends, tail]
    pos = {n: i for i, n in enumerate(seq)}
    known, users = {e: {} for e in Q}, {}
    for n in seq:
        o, need = ops[n], {}
        for b in o["banks"]:
            o["dep"].update(k for q, k in users.setdefault(b, {}).items() if q != o["e"])
            users[b][o["e"]] = n
        for k in o["dep"]:
            key = ops[k]["sem"] or ops[k]["e"]
            need[key] = max(need.get(key, -1), pos[k])
        o["wait"], o["kn"] = [], {}
        if o["e"] != "X":
            kn = known[o["e"]]
            for key, k in sorted(need.items(), key=lambda z: -z[1]):
                if kn.get(key, -1) < k:
                    p = ops[seq[k]]
                    o["wait"].append(k)
                    p["sig"] = True
                    kn[key] = k
                    for a, b in p["kn"].items():
                        kn[a] = max(kn.get(a, -1), b)
            o["kn"] = dict(kn)
    ops = [ops[n] for n in seq]
    cnt = {}
    for o in ops:
        key = o["sem"] or "c" + o["e"]
        if o["sem"] is not None:
            cnt[key] = cnt.get(key, 0) + o["inc"]
        elif o.get("sig"):
            cnt[key] = cnt.get(key, 0) + 1
        o["cnt"] = (key, cnt.get(key, 0))
    done = {}
    for o in ops:
        if o["e"] == "X":
            continue
        for k in o["wait"]:
            key, c = ops[k]["cnt"]
            Q[o["e"]].wait_ge(T.sem[key], c)
            done[key] = max(done.get(key, 0), c)
        ins = o["fn"]()
        if o["sem"] is not None and o["sem"] != "sent":
            ins.then_inc(T.sem[o["sem"]], 16)
        elif o["sem"] is None and o.get("sig"):
            ins.then_inc(T.sem["c" + o["e"]], 1)
    for key, c in cnt.items():
        if done.get(key, 0) < c:
            g.wait_ge(T.sem[key], c)


def build(g, core, rank, T, topo, rel, ops):
    V, SC, PE = g.vector, g.scalar, g.tensor
    tag = ["a"]
    turn = places(rank, rel)
    al = slice(None)

    def a(nm, *ix, part=slice(None), tag=None):
        shape = SCRATCH[nm][1][1:]
        ix = list(ix) + [slice(None)] * (len(shape) - len(ix))
        lo, hi, n = 0, 0, 1
        for d, k in zip(shape, ix):
            rg = range(d)[k] if isinstance(k, slice) else range(k, k + 1)
            lo, hi, n = lo * d + rg[0], hi * d + rg[-1], n * len(rg)
        return {"ap": T[nm][tuple([part] + ix)], "reg": [(nm, lo, hi + 1, tag)], "n": n, "d": SCRATCH[nm][2],
                "ps": SCRATCH[nm][0] == "psum", "ind": False}

    def c2(nm, lo, hi, st=1):
        return a(nm, slice(lo, hi, st))

    def cn(nm, lo, n):
        return a(nm, slice(lo, lo + n))

    def ind(win, off):
        return dict(win, ap=win["ap"].indirect(off["ap"]), off=off["reg"], n=16 * off["n"], ind=True)

    def add(e, fn, outs, ins, t, sem=None, inc=16, lat=0.0, mb=0.0, after=()):
        r, w = [], []
        for x in ins:
            if isinstance(x, dict):
                r += x["reg"] + x.get("off", [])
        for x in outs:
            w += x["reg"]
            r += x.get("off", [])
        t = t * PEF + ADDP if e == "P" else t * EF.get(e, 1.0) + (ADD if e in "VS" else 0.0)
        ops.append({"e": e, "fn": fn, "r": r, "w": w, "sem": sem, "inc": inc, "t": t, "lat": lat, "mb": mb,
                    "after": list(after), "key": len(ops), "tag": tag[0] + e})
        return len(ops) - 1

    ap = lambda x: x["ap"] if isinstance(x, dict) else x

    def cost(out, in0, f):
        if out["ind"]:
            return 0.05 + out["n"] * SCA * CY
        if in0["ind"]:
            return 0.06 + in0["n"] * GAT * CY
        if f == 0:
            f = 0.5 if out["d"] in (B, U, H) and in0["d"] in (B, U, H) else 1
        return max(64, in0["n"] * f) * CY

    def ts(out, in0, s1, op0, s2=None, op1=None):
        if op1 is None:
            add("V", lambda: V.tensor_scalar(out["ap"], in0["ap"], ap(s1), None, op0), [out], [in0, s1], cost(out, in0, 0))
        else:
            add("V", lambda: V.tensor_scalar(out["ap"], in0["ap"], ap(s1), ap(s2), op0, op1), [out], [in0, s1, s2],
                cost(out, in0, 0))

    def tt(out, in0, in1, op):
        add("V", lambda: V.tensor_tensor(out["ap"], in0["ap"], in1["ap"], op), [out], [in0, in1],
            cost(out, in0, 1 if in0["ps"] or in1["ps"] else 2))

    def cp(out, in_):
        add("V", lambda: V.tensor_copy(out["ap"], in_["ap"]), [out], [in_], cost(out, in_, 0))

    def mset(out, v):
        add("V", lambda: V.memset(out["ap"], v), [out], [], cost(out, out, 0))

    def act(out, in_, func=AF.Identity, scale=1.0, bias=0.0):
        add("S", lambda: SC.activation(out["ap"], in_["ap"], func, bias=ap(bias), scale=ap(scale)), [out],
            [in_, scale, bias], cost(out, in_, 1))

    def lin(e, out, in_, scale, bias):
        if e == "S":
            act(out, in_, scale=scale, bias=bias)
        else:
            ts(out, in_, scale, Op.mult, bias, Op.add)

    def mm(out, terms):
        mmg([[(out, l, r) for l, r in terms]])

    def mms(parts):
        mmg([parts])

    def mmg(groups, start=True, stop=True):
        def fn():
            for parts in groups:
                for i, (o, l, r) in enumerate(parts):
                    ins = PE.matmul(o["ap"], l["ap"], r["ap"], start and i == 0, stop and i == len(parts) - 1)
            return ins
        flat = [p for parts in groups for p in parts]
        add("P", fn, [p[0] for p in flat], [x for p in flat for x in p[1:]],
            sum(max(min(64, l["n"]), r["n"]) * CY * (2 if r["d"] == F else 0.5) for o, l, r in flat))

    def iota(out, pat, base, cm, after=()):
        t = 0.13 + 2 * out["n"] * CY
        if out["d"] == I:
            add("G", lambda: g.iota(out["ap"], pat, base, cm), [out], [], t, after=after)
        else:
            add("G", lambda: g.iota(out["ap"], pat, base, cm, allow_small_or_imprecise_dtypes=True), [out], [], t, after=after)

    def select(out, in_, pat, op, v, cm):
        add("G", lambda: g.affine_select(out["ap"], in_["ap"], pat, op, v, 0, cm), [out], [in_], 0.17 + 2 * out["n"] * CY,
            after=sent0)

    def fill(out, v, src=None):
        act(out, src or c2("one", 0, out["n"]), scale=0.0, bias=v)

    nd = [0]

    def dma(e, out, in_, new=True, mb=0.02, after=(), behind=None):
        if new:
            nd[0] += 1
        q = {"Y": g.sync, "S": g.scalar}[e]
        return add(e, lambda: q.dma_start(ap(out), ap(in_)), [out] if isinstance(out, dict) else [], [in_, behind], 0.06,
                   sem="d%d" % (nd[0] - 1), lat=2.3, mb=mb, after=after)

    def send(m, piece, land, ready=()):
        via = [o for o in range(NR) if (rank, o) in rel]
        tr, n = [], 0
        es = topo.engines(core, rel[(rank, via[0])])[::-1]
        for i, o in enumerate(via):
            k = rel[(rank, o)]
            w = len(topo.engines(k, T.cores[o]))
            rid, pid = topo.addr(k, core)
            tr.append(RemoteDMATransfer(dst_ids=[DstId(rid=rid, pnc=pid)], dma_engine_mask=bits(es[n:n + w]),
                                        remote_sem=T.sem["h" + m], src=piece(o)["ap"], dst=slot(T, m)))
            n += w
        calls = [add("G", lambda: g.remote_dma_fused(tr, local_sem=T.sem.sent), [], [piece(o) for o in via] + list(ready),
                     2.5 if m == "tg" else 0.5, sem="sent", inc=n)]
        for o in range(NR):
            if o != rank and o not in via:
                d = T.cores[o]
                rid, pid = topo.addr(d, core)
                calls.append(add("G", lambda o=o, d=d, rid=rid, pid=pid: g.remote_dma(
                    landing(T, m, rank, o, rel), piece(o)["ap"], T.sem["b" + m], T.sem.sent, pid, rid, topo.mask(core, d)),
                    [], [piece(o)], 0.5, sem="sent", inc=len(topo.engines(core, d)), after=calls[:1]))
                add("X", None, [land(o)], [], HOP / 2, sem="b" + m, inc=len(topo.engines(d, core)), after=calls)
        tot = sum(len(topo.engines(rel[(q, rank)], core)) for q in via)
        add("X", None, [land(q) for q in via], [], HOP + 0.5, sem="a" + m, inc=tot, after=calls[:1])
        return calls

    def send_one(m, o, piece, land):
        via = [k for k in range(NR) if (rank, k) in rel]
        d = rel.get((rank, o), T.cores[o])
        rid, pid = topo.addr(d, core)
        if o in via:
            w = len(topo.engines(d, T.cores[o]))
            es = topo.engines(core, d)[::-1][w * via.index(o):w * via.index(o) + w]
            dst, sem = slot(T, m), T.sem["h" + m]
        else:
            es, dst, sem = topo.engines(core, d), landing(T, m, rank, o, rel), T.sem["a" + m]
        k = add("G", lambda: g.remote_dma(dst, piece["ap"], sem, T.sem.sent, pid, rid, bits(es)), [], [piece], 0.5,
                sem="sent", inc=len(es))
        add("X", None, [land], [], HOP + 0.5 if o in via else HOP / 2, sem="a" + m,
            inc=len(topo.engines(rel.get((o, rank), T.cores[o]), core)), after=[k])

    cols = {}

    def col(nm):
        if nm not in cols:
            cols[nm] = len(cols)
        return c2("cc", cols[nm], cols[nm] + 1)

    eye = lambda k, i: a("eye", k, slice(i, i + 1))
    ED = {k: i for i, k in enumerate(["RXO", "MH", "RX", "RW", "MZ", "I", "NI", "BDH", "NS4", "CY", "GW", "I4", "BD"]
                                     + ["REP%d" % q for q in range(8)])}
    KG = {k: i for i, k in enumerate(["UW", "VW", "S0", "S1", "S2", "S3", "EB0", "EB1", "EB2", "EB3", "CB",
                                      "JW", "S4", "S4D", "NSU", "US", "PV", "PKU"])}
    ZK = {k: i for i, k in enumerate(["Vc", "Vb", "Uc", "Ub", "Lc", "Lb", "Vs", "Us", "Ls"])}
    ZW = {k: i for i, k in enumerate(["i", "s", "b", "b16", "d"])}
    ed = lambda k: a("ed", ED[k])
    eg = lambda k: a("eg", KG[k])
    zv = lambda k, r: a("zz", k, slice(15 - r, 143 - r))
    zk = lambda k, l: a("zk", ZK[k], slice(12 - 4 * l, 140 - 4 * l))
    zw = lambda k, l: a("zw", ZW[k], slice(12 - 4 * l, 140 - 4 * l))
    mwin = c2("mt", PAD, PAD + WT)
    mrow = lambda s, lo, hi: a("mt", slice(lo, hi), part=slice(s, 128, 16), tag=s)
    one = lambda n: c2("one", 0, n)
    pi = lambda i: c2("pint", i, i + 1)
    E1, E4, EN, EN4 = range(4)
    HI, HS, XR, ONE, DEAD, SID = 0, 4, 8, 12, 13, 15
    e1 = lambda i: eye(E1, i)

    mset(a("x0i"), 0)
    first = [dma("S", c2("ta", S * rank, S * rank + S), T.tg[:])]
    for e in range(4):
        first.append(dma("YS"[e % 2], a("x0i", part=slice(8 + e, 128, 16), tag=e), T.x0[e::4, :], new=e == 0))
    for m in range(16):
        first.append(dma("YS"[m % 2], cn("ct", 256 * m, 256), T.cf[m::16, :], mb=0.065, after=first[:5]))
    iota(c2("pint", 0, 1), [[1, 1]], 0, 1)
    iota(a("r4"), [[16, 8], [0, 4], [1, 4]], 8, 0)
    iota(a("io_"), [[1, S]], 0, 0)
    iota(a("g16"), [[16, 8], [0, 16]], 0, 0)
    send("tg", lambda o: c2("ta", S * rank, S * rank + S), lambda q: c2("ta", S * q, S * q + S))

    mset(a("one"), 1.0)
    mset(c2("yr", 0, NR * S), 0.0)
    mset(ed("MH"), 0.0)
    cp(col("p"), pi(0))
    ts(pi(1), pi(0), 15, Op.bitwise_and)
    ts(pi(2), pi(0), 2, Op.logical_shift_right, 3, Op.bitwise_and)
    ts(ed("RXO"), a("r4"), col("p"), Op.is_equal)
    cp(col("p16"), pi(1))
    ts(col("ini"), pi(2), float(S), Op.mult, -1.0, Op.add)
    ts(col("thr"), pi(2), float(S), Op.mult, float(CAP), Op.add)
    ts(a("ed", ED["RXO"], slice(15, 128, 16)), c2("io_", 15, 128, 16), col("p"), Op.is_equal)
    ts(a("eye", 0), c2("io_", 0, 16), col("p16"), Op.is_equal)
    ts(col("g16"), col("p"), col("p16"), Op.subtract)
    ts(col("off"), col("p16"), 8.0, Op.is_lt, -192.0, Op.mult)
    ts(col("t1"), col("p16"), 8.0, Op.is_ge, 0.75, Op.mult)
    ts(col("t2"), pi(2), 1.0, Op.is_equal, 0.25, Op.mult)
    ts(col("tm"), e1(12), e1(13), Op.add)
    ts(a("z16"), c2("io_", 0, 144), -15.0, Op.add, col("g16"), Op.is_equal)
    ts(a("gm"), c2("g16", 0, 128, 16), col("g16"), Op.is_equal)
    ts(col("t3"), col("off"), 0.375 / 192, Op.mult, col("t2"), Op.add)
    ts(col("sc"), col("t1"), 0.25, Op.add, col("tm"), Op.subtract)
    ts(col("bi0"), col("t3"), e1(12), Op.add, col("off"), Op.subtract)
    act(col("tsc"), e1(12), scale=-1.0 / 256, bias=1.0 / 256)
    ts(col("t4"), pi(2), -0.25, Op.mult, 192.0 - 127.5 / 256, Op.add)
    ts(col("tb0"), col("t4"), col("tsc"), Op.mult, 256.0, Op.mult)
    act(col("tb0"), col("tb0"), bias=e1(12))
    for o in range(NR):
        if o < 3:
            act(col("h%d" % o), e1(4 * o + 6), scale=-1.0, bias=e1(4 * o + 2))
        else:
            ts(col("h3"), e1(14), e1(2), Op.subtract, e1(12), Op.add)
        act(a("ed", ED["MH"], slice(4 * o, 128, 16)), a("gm"), scale=col("h%d" % o))
        act(c2("xw", S * o, S * o + CAP), one(CAP), scale=col("tm"))
    cp(c2("xp", 0, S), a("x0i"))

    def source(r):
        tag[0] = "s%d" % r
        px, pm, ph, pslot = c2("pC", 0, S), cn("pC", 256, S), c2("pD", 0, S), c2("pD", 256, 266)
        old = c2("xp", S * r, S * r + S)
        if r == 0:
            ts(a("clp"), a("io_"), e1(15), Op.mult)
            mm(px, [(ed("RXO"), a("clp")), (ed("RXO"), old)])
            pm = px
        else:
            back = ind(c2("yr", NR * S * (r - 1), NR * S * r), c2("sl", 16 * (r - 1), 16 * (r - 1) + 10))
            ts(a("clp"), back, 120.0, Op.max, 136.0, Op.min)
            terms = [(ed("RXO"), old), (ed("RW"), a("wt")), (ed("RX"), a("clp"))]
            mm(px, terms)
        lin(TQ, a("th"), px, col("tsc"), col("tb%d" % min(r, 1)))
        if r < RO:
            mm(ph, [(ed("MH"), a("th"))])
        if r > 0:
            mm(pm, terms + [(ed("MZ"), a("th"))])
            sums = c2("acc", S * (r - 1), S * r)
            if r == 1:
                act(sums, back)
            else:
                tt(sums, back, c2("acc", S * (r - 2), S * (r - 1)), Op.add)
        if r == RO:
            dma("Y", T.ys[:], sums)
            act(a("xf"), pm, bias=256.0 * 192 - 128)
            for e in range(4):
                dma("YS"[e % 2], T.yx[e::4, :], a("xf", part=slice(e, 128, 16)), new=e == 0)
            return
        add("V", lambda: V.tensor_tensor_scan(T.cum[:], T.one[:, 0:S], ph["ap"], col("ini")["ap"], Op.mult, Op.add),
            [a("cum")], [one(S), ph, col("ini")], S * CY)
        new = c2("xp", S * (r + 1), S * (r + 2))
        tt(a("prd"), ph, a("cum"), Op.mult)
        mm(pslot, [(c2("z16", 15 - k, 143 - k), c2("prd", k, S, 16)) for k in range(16)])
        act(a("xq"), pm, scale=col("sc"), bias=col("bi%d" % min(r, 1)))
        act(new, a("xq"), bias=col("off"))
        sl = c2("sl", 16 * r, 16 * r + 10)
        cp(sl, pslot)
        base = NR * S * r
        cp(ind(c2("xw", base, base + NR * S), sl), new)
        ts(a("wt"), a("prd"), col("thr"), Op.is_ge)
        piece = lambda o: c2("xw", base + S * o, base + S * o + CAP)
        land = lambda q: cn("xl", 256 * r + CAP * turn.index(q), CAP)
        act(land(rank), piece(rank))
        return send("x%d" % r, piece, land, [c2("yr", base, base + NR * S)])

    sent0 = source(0)
    tag[0] = "b"
    dma("Y", c2("ftab", 0, FC), T.ft[:], mb=0.26, behind=c2("xl", 192, 256))
    dma("Y", c2("ftab", FC, DF), T.ft[:, 0:FX], mb=0.2, new=False, behind=c2("xl", 192, 256))
    iota(a("q4"), [[4, 4], [0, 4], [1, 4]], 0, 0)
    for lo in range(0, WT, WT // 16):
        iota(c2("ycw", lo, lo + WT // 16), [[1, WT // 16]], lo, 0, after=sent0)

    ts(ed("BD"), a("g16"), col("g16"), Op.is_equal)
    ts(ed("I"), c2("io_", 0, 128), col("p"), Op.is_equal)
    act(ed("I4"), ed("I"), scale=16.0)
    for q in range(8):
        act(a("rp", q), ed("BD"), scale=e1(q))
    act(col("k0"), col("p16"), scale=-1.0, bias=15.0)
    act(a("kc", 0), one(256), scale=col("k0"))
    act(a("kc", 1), one(256), scale=col("k0"), bias=-8.0)
    for i, lo in enumerate(range(PAD, PAD + WT, WT // 8)):
        if i < MZ:
            mset(cn("mt", lo, WT // 8), 0.0)
        else:
            fill(cn("mt", lo, WT // 8), 0.0, cn("ct", 0, WT // 8))
    tag[0] = "c"
    for m in range(16):
        bank = cn(("pE", "pF", "pG", "pH")[m % 4], 0, 256)
        mm(bank, [(a("rp", m % 8), a("kc", m // 8)), (ed("I4"), cn("ct", 256 * m, 256))])
        acc = cn("mx", 256 * (m % 2), 256)
        if m < 2:
            act(acc, bank)
        else:
            tt(cn("pE", 256, 256) if m == 14 else acc, bank, acc, Op.max)
    tt(a("ki"), cn("pE", 256, 256), acc, Op.max)
    ts(c2("k2", 0, 256), a("ki"), 15, Op.bitwise_and)
    ts(c2("mq", 0, 256), c2("k2", 0, 256), -1.0, Op.mult, 15.0, Op.add)
    for s, sh in enumerate(SHIFTS):
        dma("YS"[s % 2], mrow(s, PAD - sh, PAD - sh + WC), c2("mq", 0, 256), new=s == 0, mb=0.065)
        for q in range(2):
            n = min(sh - 256 * q, 256)
            if n > 0:
                lo = PAD - sh + WC + 256 * q
                dma("SY"[s % 2], mrow(s, lo, lo + n), a("mq", slice(0, n), part=slice(q, 128, 16)), new=False)
    ts(c2("k2", 256, 512), a("ki"), 4, Op.logical_shift_right)
    cp(c2("mq", 256, 512), c2("k2", 256, 512))
    dma("Y", mrow(4, PAD, PAD + WC), c2("mq", 256, 512), mb=0.065)
    dma("Y", a("ctab"), T.cf[:], mb=1.0, behind=mwin)

    tag[0] = "b"
    ts(pi(4), pi(0), 1, Op.logical_shift_right, 1, Op.bitwise_and)
    ts(a("pa"), c2("io_", 0, 16), -1.0, Op.mult, col("p"), Op.add)
    mset(a("kz"), 0.0)
    mset(a("kg"), 0.0)
    mset(a("zk"), 0.0)
    for k, v in enumerate((4.0, -1.0, -4.0)):
        act(a("eye", k + 1), a("eye", 0), scale=v)

    def kset(nm, m, lo, hi, st, t1, t2=0.0):
        out = a(nm, m, slice(lo, hi, st))
        act(out, one(out["n"]), scale=t1, bias=t2)

    def mix(nm, c1, r1, c2_, r2):
        act(col(nm), e1(r1), scale=c1)
        ts(col(nm), e1(r2), c2_, Op.mult, col(nm), Op.add)
        return col(nm)

    kset("kz", ZK["Vc"], 0, 4, 1, e1(HI + 1)); kset("kz", ZK["Vb"], 0, 4, 1, e1(HI + 3))
    for nm, r0 in (("Uc", HI), ("Ub", HI + 2)):
        kset("kz", ZK[nm], 0, 4, 2, e1(r0)); kset("kz", ZK[nm], 1, 4, 2, e1(r0), e1(ONE))
    kset("kz", ZK["Lc"], 0, 4, 1, mix("lc", 188.0, HI + 2, 916.0, HI + 3))
    kset("kz", ZK["Lb"], 0, 4, 1, mix("lb", 148.0, HI, 44.0, HI + 1))
    cp(a("kz", ZK["Vs"], slice(0, 2)), a("eye", E1, slice(HS + 1, HS + 4, 2)))
    cp(a("kz", ZK["Us"], slice(0, 2)), a("eye", E1, slice(HS, HS + 4, 2)))
    kset("kz", ZK["Ls"], 0, 1, 1, mix("ls", 188.0, HS + 2, 916.0, HS + 3))
    kset("kz", ZK["Ls"], 1, 2, 1, mix("lt", 148.0, HS, 44.0, HS + 1))
    kset("kz", ZK["Ls"], 2, 3, 1, eye(E4, SID)); kset("kz", ZK["Ls"], 3, 4, 1, eye(E4, DEAD))
    for b, e in ((0, 0), (4, 2)):
        kset("kg", KG["UW"], b, b + 4, 2, eye(E4, HI + e), eye(EN, XR + e))
        out = a("kg", KG["UW"], slice(b, b + 4, 2))
        act(out, out, bias=eye(E4, ONE))
        kset("kg", KG["UW"], b + 1, b + 4, 2, eye(EN4, HI + e), e1(XR + e))
        kset("kg", KG["VW"], b, b + 4, 1, eye(EN4, HI + e + 1), e1(XR + e + 1))
    for kk in range(4):
        cp(a("kg", KG["S%d" % kk], slice(4 * kk, 4 * kk + 4)), a("eye", 0, slice(0, 4)))
    ts(a("kg", slice(KG["EB0"], KG["EB0"] + 4)), a("q4"), col("p16"), Op.is_equal, 16.0, Op.mult)
    for kk, v in ((1, 592.0), (2, 176.0), (3, 768.0)):
        ts(a("kg", KG["CB"], slice(4 * kk, 4 * kk + 4)), one(4), e1(ONE), Op.mult, v, Op.mult)
    ts(col("bva"), pi(4), 2.0, Op.mult, 1.0, Op.add)
    ts(col("sw"), pi(4), 2.0, Op.mult, -1.0, Op.add)
    ts(col("bw"), pi(4), -4.0, Op.mult, 4.0, Op.add)
    NE = KG["JW"]
    for gq in range(8):
        gm = c2("gm", gq, gq + 1)
        act(a("zk", al, slice(12 + 16 * gq, 16 + 16 * gq)), a("kz"), scale=gm)
        ts(a("eg", slice(0, NE), slice(16 * gq, 16 * gq + 16)), a("kg", slice(0, NE)), gm, Op.mult)
    ts(ed("CY"), a("g16"), c2("pa", ONE, ONE + 1), Op.is_equal, -255.0 / 512, Op.mult)
    act(a("i32"), ed("I"), scale=1.0 / 256)

    tag[0] = "l"
    act(ed("NI"), ed("I"), scale=-1.0)
    act(a("zz", 1), a("z16"), scale=8192.0)
    act(a("zz", 2), a("z16"), scale=e1(0))
    act(col("dm0"), col("p16"), bias=float(DC))
    act(col("dm1"), col("p16"), bias=float(DF))
    if CH == 32:
        for t in range(2):
            for z in range(2):
                act(c2("dmp", 16 * t + z, 16 * t + 16, 2), one(8), scale=col("dm%d" % t), bias=16.0 * z)
    fill(c2("ftab", DF, DF + 32), 0.0)
    for k in range(5):
        fill(a("zw", k), 0.0)
    for nm, t, v in (("i", 0, 1.0), ("s", 2, 1.0), ("b", 1, 1.0), ("b16", 1, 16.0), ("d", 3, 8192.0)):
        act(a("kw", ZW[nm]), a("eye", E1, slice(t, 16, 4)), scale=v)
    fill(a("cst"), 0.0)
    for lo, n, v in ((0, 8, 2048.0), (32, 8, 2048.0), (64, 16, 4096.0), (80, 16, 2048.0)):
        fill(cn("cst", lo, n), v)
    for i, q in enumerate(turn):
        fill(cn("cst", 32 * (i // 2) + 16 + 4 * (i % 2), 4), float(S * q))
    ts(pi(3), pi(0), 3, Op.bitwise_and)
    ts(col("cen"), pi(3), 0.0, Op.is_equal, 2048.0, Op.mult)
    for k in range(8, 16):
        act(a("rp", k), ed("BD"), scale=e1(k))
    for k in range(0, 16, 2):
        select(a("rk", slice(k, k + 2)), a("rp", slice(k, k + 2)), [[0, 2], [-1, 128]], Op.not_equal, -1.0, 1)
    for k in range(16):
        select(a("et", k), zv(1, k), [[1, 128]], Op.is_gt, 0.0, -1)
    ts(pi(6), pi(0), 1, Op.bitwise_and)
    ts(col("sb"), pi(6), 4.0, Op.mult, -2.0, Op.add)
    ts(col("w4"), pi(6), 3.0, Op.mult, 1.0, Op.add)
    ts(pi(7), pi(1), 1, Op.logical_shift_right)
    cp(col("ph"), pi(7))
    act(a("kg", KG["JW"], slice(0, 1)), col("p16"), scale=0.5)
    act(a("kg", KG["S4"], slice(4, 5)), e1(4))
    act(a("kg", KG["S4D"], slice(4, 5)), e1(4))
    act(a("kg", KG["S4D"], slice(13, 14)), e1(13))
    for z in range(2):
        act(a("kg", KG["PV"], slice(z, 16, 2)), a("eye", E1, slice(5, 13)))
        ts(a("kg", KG["US"], slice(z, 16, 2)), c2("io_", 0, 8), col("ph"), Op.is_equal, (-2.0, 0.5)[z], Op.mult)
    act(a("kg", KG["NSU"], slice(0, 16, 2)), a("eye", E1, slice(5, 13)), bias=eye(EN, 4))
    act(a("kg", KG["NSU"], slice(1, 16, 2)), one(8), scale=eye(EN, 4))
    ts(a("kg", KG["PKU"], slice(5, 13)), c2("io_", 0, 8), col("ph"), Op.is_equal, col("w4"), Op.mult)
    for gq in range(8):
        gm = c2("gm", gq, gq + 1)
        act(a("zw", al, slice(12 + 16 * gq, 16 + 16 * gq)), a("kw"), scale=gm)
        ts(a("eg", slice(NE, 18), slice(16 * gq, 16 * gq + 16)), a("kg", slice(NE, 18)), gm, Op.mult)
    act(col("jp1"), col("p16"), bias=1.0)
    act(col("eb"), col("p16"), scale=-LN4)
    act(col("e60"), e1(0), scale=60.0)
    ts(col("t5"), col("p16"), 12.0, Op.is_lt, col("sc"), Op.mult)
    act(col("bi1"), col("t5"), scale=256.0 * 192 - 128, bias=col("bi0"))
    act(col("tb1"), col("tsc"), scale=-128.0, bias=col("tb0"))
    ts(ed("RX"), a("r4"), -8.0, Op.add, col("p"), Op.is_equal)
    act(ed("RW"), ed("BD"), scale=8.0)
    mset(a("ed", slice(ED["RX"], ED["RW"] + 1), slice(15, 128, 16)), 0.0)
    act(ed("MZ"), ed("RX"), scale=-256.0)
    act(ed("GW"), ed("BD"), scale=-0.5)
    tt(ed("BDH"), ed("GW"), ed("I"), Op.add)
    act(ed("I4"), ed("I"), scale=4096.0)
    ts(a("ed", ED["GW"], slice(0, 128, 2)), c2("g16", 0, 128, 2), col("g16"), Op.is_equal, 127.5 / 4096 / 256, Op.mult)
    ts(a("ed", ED["GW"], slice(1, 128, 2)), c2("g16", 1, 128, 2), col("g16"), Op.is_equal, 0.5, Op.mult)
    act(a("gq"), a("gm"), scale=1.0 / 4096)
    act(ed("NS4"), ed("BD"), scale=eye(EN, 4))
    act(a("zz", 3), a("z16"), scale=col("jp1"))
    for r in range(1, RO):
        for o in range(NR):
            lo = NR * S * r + S * o
            act(c2("xw", lo, lo + CAP), one(CAP), scale=col("tm"))
    for lo in range(NR * S, RO * NR * S, S):
        fill(c2("yr", lo, lo + S), 0.0)

    ftw = a("ftab")
    lk = lambda r, lo, n: cn("lk", 80 * r + lo, n)
    YB, WB = ("pH", "pB"), ("pF", "pE")
    yblk = lambda r, i, lo=0, n=CAP: (cn("yr", NR * S * r + S * rank + lo, n) if turn[i] == rank
                                      else cn("yb", 256 * r + CAP * i + lo, n))
    turns = [1]

    def pack():
        for j in range(8):
            mm(cn("pF", 64 * j, 64), [(ed("I"), c2("ftab", 2 * j, FC, 16)), (ed("I4"), c2("ftab", 2 * j + 1, FC, 16))])
        act(a("f2"), a("pF"), bias=-127.5 - 128.0 * 4096)

    def index(r, lo, n):
        tag[0] = "i%d%d" % (r, lo // 64)
        x0, u, m, v0 = 256 * r + lo, lo // 128, n // 4, 3 * lo // 2
        X, Y, y0, t0 = cn("xl", x0, n), YB[u], 192 * (lo + n == 192), lo // 2
        form = lambda out, k: mm(out, [(zk(k, l), c2("xl", x0 + l, x0 + n, 4)) for l in range(4)])
        form(cn("pA", v0, m), "Vc")
        form(cn("pA", v0 + m, m), "Vb")
        mm(cn("pA", v0 + 2 * m, n), [(eg("VW"), X)])
        for i, k in enumerate(("Uc", "Ub", "Lc", "Lb")):
            form(cn(Y, y0 + m * i, m), k)
        mm(cn(Y, y0 + n, n), [(eg("UW"), X)])
        act(cn("va", v0, 2 * m), cn("pA", v0, 2 * m), scale=2.0, bias=col("bva"))
        act(cn("va", v0 + 2 * m, n), cn("pA", v0 + 2 * m, n), scale=col("sw"), bias=col("bw"))
        tt(cn("ra", t0, 2 * m), cn(Y, y0, 2 * m), cn("va", v0, 2 * m), Op.mult)
        tt(cn("tsw", t0, 2 * m), cn(Y, y0 + 2 * m, 2 * m), cn("ra", t0, 2 * m), Op.add)
        ts(cn("ti", t0, m), cn("tsw", t0, m), 2, Op.logical_shift_right, WC - 1, Op.bitwise_and)
        cp(cn("of1", lo // 4, m), cn("ti", t0, m))
        tt(cn("wq", lo, n), cn(Y, y0 + n, n), cn("va", v0 + 2 * m, n), Op.mult)
        ts(cn("ti", t0 + m, m), cn("tsw", t0 + m, m), 2, Op.logical_shift_right, 63, Op.bitwise_and)
        cp(cn("b0", lo // 4, m), cn("ti", t0 + m, m))
        tag[0] = "j%d%d" % (r, lo // 64)
        w0 = 4 * (lo % 128)
        for s in range(4):
            mm(c2("pG", s, 4 * n, 4), [(a("rp", 4 + s), cn("wq", lo, n))])
        for s in range(4):
            mm(c2(WB[u], w0 + s, w0 + 4 * n, 4), [(a("rp", s), cn("wq", lo, n))])
        act(cn("wcd", 4 * lo, 4 * n), cn("pG", 0, 4 * n))
        for o in range(4 * lo, 4 * (lo + n), 256):
            (cp if VM[o // 256] else act)(cn("mg", o, 256), ind(mwin, cn("of1", o // 16, 16)))
        po = cn(Y, y0 + 2 * n, n)
        mms([(po, eg("CB"), X)]
            + [(c2(Y, y0 + 2 * n + l, y0 + 3 * n, 4), eg("EB%d" % l), cn("b0", lo // 4, m)) for l in range(4)]
            + [(po, eg("S%d" % kk), c2("mg", 4 * lo + kk, 4 * (lo + n), 4)) for kk in range(4)])
        cp(cn("of2", lo, n), po)

    rows = {}

    def row(k):
        if k in rows:
            ops[-1]["after"].append(rows[k])
        rows[k] = len(ops) - 1

    def value(r, i):
        lo, u = 64 * i, i // 2
        for z, (w, n) in enumerate(VL[min(r, 1)][i]):
            tag[0] = "v%d%d%d" % (r, i, z)
            hi, bank = lo + w, ("pC", "pD")[turns[0] % 2]
            turns[0] += 1
            if n:
                ts(cn("vv", 16 * lo, 16 * n), ind(ftw, cn("of2", lo, n)), -128.0, Op.add)
            for l in range(lo + n, hi, 32):
                h = min(l + 32, hi)
                act(c2("vv", 16 * l, 16 * h), ind(ftw, c2("of2", l, h)), bias=-128.0)
                row("S")
            for s in range(4):
                tt(a("pp", slice(lo, hi), slice(s, 16, 4), tag=s), c2("vv", 16 * lo + s, 16 * hi, 4),
                   cn(WB[u], 4 * (lo % 128), 4 * w), Op.mult)
                row("V")
            mm(cn(bank, 0, 4 * w), [(ed("I"), a("pp", slice(lo, hi), slice(4 * kk, 4 * kk + 4))) for kk in range(4)])
            tt(cn("qq", 4 * lo, 4 * w), cn(bank, 0, 4 * w), cn("wcd", 4 * lo, 4 * w), Op.mult)
            py = cn(bank, 256, w)
            mm(py, [(ed("CY"), cn("xl", 256 * r + lo, w))] + [(a("i32"), c2("qq", 4 * lo + s, 4 * hi, 4)) for s in range(4)])
            ts(yblk(r, i, lo % 64, w), py, MAGIC + 128.0, Op.add, MAGIC, Op.subtract)
            lo = hi
        if turn[i] != rank:
            send_one("y%d" % r, turn[i], yblk(r, i), cn("yr", NR * S * r + S * turn[i], CAP))

    def star(r, u):
        tag[0] = "k%d%d" % (r, u)
        x0, s0, p0 = 256 * r + 128 * u, 128 + 32 * u, 384 + 32 * u
        form = lambda out, k: mm(out, [(zk(k, l), c2("xl", x0 + l, x0 + 128, 4)) for l in range(4)])
        form(cn("pA", p0, 32), "Vs")
        form(cn("pH", p0, 32), "Us")
        form(cn("pH", p0 + 64, 32), "Ls")
        act(cn("va", p0, 32), cn("pA", p0, 32), scale=2.0, bias=col("bva"))
        tt(cn("ra", s0, 32), cn("pH", p0, 32), cn("va", p0, 32), Op.mult)
        tt(cn("tsw", s0, 32), cn("pH", p0 + 64, 32), cn("ra", s0, 32), Op.add)
        ts(cn("ti", 128 + 64 * u, 32), cn("tsw", s0, 32), 2, Op.logical_shift_right, WC - 1, Op.bitwise_and)
        ts(cn("ti", 160 + 64 * u, 32), cn("tsw", s0, 32), 2, Op.logical_shift_right, 63, Op.bitwise_and)
        ts(cn("st", 64 * u, 64), cn("ti", 128 + 64 * u, 64), col("cen"), Op.subtract)
        mms([(cn("pB", p0, 32), ed("I"), cn("cst", 32 * u, 32))]
            + wrap(p0, "i", u, 0) + wrap(p0 + 8, "d", u, 0) + wrap(p0 + 16, "s", u, 0) + wrap(p0 + 24, "b", u, 1))
        cp(lk(r, 32 * u, 32), cn("pB", p0, 32))
        ts(a("kh", slice(0, 2), slice(8 * u, 8 * u + 8)), cn("pB", p0, 16), -2048.0, Op.add)
        tag[0] = "g%d%d" % (r, u)
        h = lambda nm: cn(nm, 128 * u, 128)
        act(h("tgl"), ind(a("ta"), lk(r, 32 * u + 16, 8)))
        for j in range(VJ[u], 8):
            act(cn("v3", 256 * j + 128 * u, 128), ind(cn("f2", 64 * j, 64), lk(r, 32 * u + 24, 8)))
        if r < RO - 1:
            act(h("cg"), ind(a("ctab"), lk(r, 32 * u, 8)))
        else:
            act(h("yg"), ind(a("ycw"), lk(r, 32 * u, 8)))
        tag[0] = "h%d%d" % (r, u)
        act(h("ms"), ind(mwin, lk(r, 32 * u, 8)))

    wrap = lambda lo, k, u, h: [(cn("pB", lo, 8), zw(k, n), c2("st", 64 * u + 32 * h + n, 64 * u + 32 * h + 32, 4)) for n in range(4)]

    def dedupe(r):
        tag[0] = "d%d" % r
        mms([(cn("pB", 480, 16), zv(2, k), c2("ms", k, 256, 16)) for k in range(16)] + wrap(480, "b16", 0, 1) + wrap(488, "b16", 1, 1))
        cp(a("kh", 2), cn("pB", 480, 16))
        cp(lk(r, 64, 16), cn("pB", 480, 16))
        act(a("fg"), ind(ftw, lk(r, 64, 16)))
        tag[0] = "e%d" % r
        keys = lambda z=al: a("kh", slice(0, 3, 2), z)
        mmg([[(c2("pA", k, 512, 16), a("rk", k), keys())] for k in range(16)])
        ts(c2("eq", 0, 512), a("pA"), 0.0, Op.is_equal)
        out = cn("pB", 448, 32)
        parts = ([(out, ed("I"), keys()), (out, ed("I"), c2("cst", 64, 96))]
                 + [(cn("pB", 448 + 16 * t, 16), ed("I"), a("kh", 1)) for t in range(2)]
                 + [(out, a("et", k), c2("eq", k, 512, 16)) for k in range(16)])
        if CH == 16:
            mms(parts)
            for t in range(2):
                ts(c2("lo", 64 * r + 32 * t, 64 * r + 32 * t + 32, 2), cn("pB", 448 + 16 * t, 16), col("dm%d" % t), Op.min)
            return
        for h in range(0, 16, 4):
            odd, even = keys(slice(1, 16, 2)), keys(slice(0, 16, 2))
            mmg([[(c2("pG", 256 + k, 512, 16), l, x) for l, x in ((a("rp", k), odd), (ed("NI"), even))]
                 for k in range(h, h + 4)])
        ts(c2("eq", 512, 768), c2("pG", 256, 512), 0.0, Op.is_equal)
        mms(parts + [(c2("pB", 449, 480, 2), zv(1, k), c2("eq", 512 + k, 768, 16)) for k in range(16)])
        tt(a("tmp"), out, a("dmp"), Op.min)
        cp(cn("lo", 64 * r, 32), a("tmp"))

    def signs(r, u):
        tag[0] = "t%d%d" % (r, u)
        d, sg = cn("pE", 256 * u, 128), cn("pE", 256 * u + 128, 128)
        mms([(d, ed("I"), cn("tgl", 128 * u, 128))]
            + [(cn("pE", 256 * u + 64 * z, 64), ed("NI"), yblk(r, 2 * u + z)) for z in range(2)])
        act(cn("gs", 128 * u, 128), d, AF.Sign)
        act(sg, d, AF.Sign)
        for j in range(8):
            o = 256 * j + 128 * u
            if j < VJ[u]:
                tt(cn("gw", o, 128), ind(cn("f2", 64 * j, 64), lk(r, 32 * u + 24, 8)), cn("gs", 128 * u, 128), Op.mult)
            else:
                tt(cn("gw", o, 128), cn("v3", o, 128), sg, Op.mult)
            mm(c2(YB[u], j, 64, 8), [(cn("gw", o, 128), a("gq"))])

    def train(r, u):
        tag[0] = "u%d%d" % (r, u)
        Y, h = YB[u], lambda nm: cn(nm, 128 * u, 128)
        hi, lo = c2("zc", 128 * u + 1, 128 * u + 128, 2), c2("zc", 128 * u, 128 * u + 128, 2)
        ts(hi, cn(Y, 0, 64), MAGIC, Op.add, MAGIC, Op.subtract)
        tt(lo, cn(Y, 0, 64), hi, Op.subtract)
        mm(cn(Y, 128, 128), [(ed("GW"), h("gs")), (h("zc"), a("i32"))])
        act(h("uu"), cn(Y, 128, 128), AF.Sign)
        if r == RO - 1:
            mm(cn(Y, 256, 128), [(zv(3, 0), h("uu"))])
            act(cn("yg", 256 + 128 * u, 128), cn(Y, 256, 128))
            return
        old = [(ed("NS4"), h("ms"))] if r == 0 else [(eg("NSU"), h("ms")), (eg("US"), h("su"))]
        mm(cn(Y, 256, 128), [(ed("I"), h("cg"))] + old + [(ed("I"), h("uu"))])
        act(h("ee"), cn(Y, 256, 128), AF.Exp, scale=16 * LN4, bias=col("eb"))
        mm(cn(Y, 128, 128), [(ed("BDH"), h("ee"))])
        act(h("ohm"), cn(Y, 128, 128), AF.Sign)
        keep = [(eg("S4"), h("ms")), (eg("PKU"), h("uu"))] if r == 0 else [(eg("S4D"), h("ms"))]
        mm(cn(Y, 256, 128), keep + [(zv(3, 13 + r), h("uu")), (eg("JW"), h("ohm"))])
        act(h("mn"), cn(Y, 256, 128), bias=col("e60"))

    def scat(r, win, t, fn):
        tag[0] = "w%d%s" % (r, win["reg"][0][0])
        n = 64 // CH
        for k in [n * turn.index(q) + z for q in range(NR - 1, -1, -1) for z in range(n - 1, -1, -1)]:
            o = 64 * r + 8 * n * t + 2 * k
            fn(ind(win, cn("lo", o, CH // 16)), CH * k, CH * k + CH)

    pack()
    for r in range(RO):
        last = r == RO - 1
        if r == 0 or MS == 0:
            index(r, 128, 128)
        else:
            index(r, 192, 64)
            index(r, 128, 64)
        tag[0] = "y%d" % r
        if last:
            mm(cn("pF", 0, 256), [(ed("I"), cn("mq", 256 * q, 256)) for q in range(2)])
            tt(c2("yo", 256, 512), cn("pF", 0, 256), c2("yo", 0, 256), Op.add)
            dma("Y", a("ycw", slice(0, WC), part=slice(0, 128, 16)), c2("yo", 256, 512), mb=0.13)
        star(r, 1)
        index(r, 0, 128)
        star(r, 0)
        for i in ((3, 2, 0, 1) if r else (0, 1, 2, 3)):
            value(r, i)
        dedupe(r)
        signs(r, 1)
        signs(r, 0)
        tag[0] = "f%d" % r
        if r == 1:
            mm(cn("pF", 256, 256), [(eg("PV"), a("ms"))])
            act(a("su"), cn("pF", 256, 256), AF.Sign, bias=col("sb"))
        mm(cn("pF", 256, 256), [(ed("I"), a("fg")), (ed("I"), a("gs"))])
        row("F")
        ts(a("fn"), cn("pF", 256, 256), 0.0, Op.max, 255.0, Op.min)
        if r == 0:
            tag[0] = "y0"
            for q in range(16):
                mmg([[(cn("pF", 0, 256), zv(3, q), cn("ctab", 256 * q, 256))]], q == 0, q == 15)
                row("F")
            act(c2("yo", 0, 256), cn("pF", 0, 256))
        train(r, 1)
        train(r, 0)
        scat(r, ftw, 1, lambda w, lo, hi: cp(w, c2("fn", lo, hi)))
        source(r + 1)
        tag[0] = "m%d" % r
        if last:
            dma("S", T.yf[:], c2("ftab", 0, FC), mb=0.26)
            scat(r, a("ycw"), 0, lambda w, lo, hi: tt(w, c2("yg", lo, hi), c2("yg", 256 + lo, 256 + hi), Op.add))
            dma("Y", T.yc[:], a("ycw", slice(0, WC), part=slice(0, 128, 16)), mb=0.13)
            break
        dma("Y", c2("ftab", FC, DF), c2("ftab", 0, FX), mb=0.2)
        pack()
        scat(r, mwin, 0, lambda w, lo, hi: cp(w, c2("mn", lo, hi)))
        for s in range(1, 4):
            sh = SHIFTS[s]
            dma("YSY"[s - 1], mrow(s, PAD, PAD + WC - sh), mrow(0, PAD + sh, PAD + WC), new=s == 1, mb=0.065)
            dma("SYS"[s - 1], mrow(s, PAD + WC - sh, PAD + WC), mrow(0, PAD, PAD + sh), new=False, mb=0.0)
        tag[0] = "y%d" % r
        if r == 1:
            for q in range(2):
                dma("Y", cn("mq", 256 * q, 256), mrow(13 + q, PAD, PAD + WC), new=q == 0, mb=0.065)
